import numpy as np, ml_dtypes
CORES = [48,51,52,55]
N = 4
import mx_ref
BF = ml_dtypes.bfloat16
def entries(a):
    return np.ascontiguousarray(a.T).reshape(-1)
def table(e):
    return np.ascontiguousarray(np.reshape(e, (-1, 16)).T).astype(np.int32)
def gcols(t, e):
    v = np.concatenate([t.reshape(8, 16, -1, 4), np.zeros((8, 16, 1, 4), BF)], axis=2)
    return np.ascontiguousarray(np.stack([v[g][:, e[g]] for g in range(8)])).reshape(128, -1)
def gpick(z, e):
    return np.concatenate([z[16 * g:16 * g + 16][:, e[g]] for g in range(8)])
def tile(rs):
    return np.stack(rs, axis=2).reshape(128, -1).astype(BF)
def pick(q, e):
    c = np.concatenate([q[0].reshape(128, -1, 4), np.zeros((128, 1, 4), np.uint8)], axis=1); s = np.concatenate([q[1], np.ones((16, 1), np.uint8)], axis=1)
    return (np.ascontiguousarray(c[:, e].reshape(128, -1)), np.ascontiguousarray(s[:, e]))
def join(*qs):
    return (np.concatenate([q[0] for q in qs], axis=1), np.concatenate([q[1] for q in qs], axis=1))
def put(q, e, v):
    c, s = q[0].reshape(128, -1, 4).copy(), q[1].copy(); c[:, e] = v[0].reshape(128, -1, 4); s[:, e] = v[1]
    return (c.reshape(128, -1), s)
def pk(c, s):
    return (np.ascontiguousarray(c), mx_ref.live(s))
def emit(q):
    return q[0], q[1]
def packed(v, rng):
    q = [mx_ref.quantize(np.ascontiguousarray(v[r])) for r in range(N)]
    return np.stack([a for a, b in q]), np.stack([mx_ref.plane(b, rng) for a, b in q])
def values_of_codes():
    e, c = np.zeros((128, 128, 4), np.float32), np.zeros((128, 2, 4), np.uint8)
    e[np.arange(128), np.arange(128), 0] = 1
    c[:127, :, 0] = np.arange(256).reshape(2, 128).T[:127]
    return mx_ref.matmul(mx_ref.quantize(e.reshape(128, 512).astype(BF)), (c.reshape(128, 8), np.full((16, 2), 127, np.uint8))).T.reshape(-1).astype(np.float64)
CODE_VALUE, SCALE_VALUE = values_of_codes(), 2.0 ** (np.arange(256) - 127.0)
def decode(q):
    return (CODE_VALUE[q[0]].reshape(16, 8, -1, 4) * SCALE_VALUE[q[1]][:, None, :, None] + 0.0).reshape(128, -1).astype(np.float32)
def f(rng, *shape):
    return mx_ref.flush((rng.standard_normal(shape, dtype=np.float32) * np.exp2(rng.integers(-2, 3, shape[:-1] + (1,)))).astype(BF))
def wide(rng, *shape, cols=0):
    v = rng.standard_normal(shape, dtype=np.float32) * np.exp2(rng.integers(-12, 13, shape)).astype(np.float32)
    if cols: v *= np.repeat(np.exp2(rng.integers(-cols, cols + 1, shape[:-2] + (1, shape[-1] // 4))) * (rng.random(shape[:-2] + (1, shape[-1] // 4)) > 0.0625), 4, axis=-1).astype(np.float32)
    return mx_ref.flush(v.astype(BF))
C, H, R = 512, 256, 3
WIDTH = [2, 4, 8, 16, 32, 64, 128, 256]
def big(v):
    v = v.astype(np.float32)
    v[np.abs(v) < np.float32(2.0 ** -16)] = 0
    return v.astype(BF)
def numbers_of(rng):
    return {"x": big(f(rng, N, 128, 4 * C)), "u": np.array(f(rng, N, 128, 512)), "v": np.array(f(rng, N, 128, 512))}
def bases(rng):
    return np.stack([table(rng.permutation(C)) for r in range(N)])
def layers(rng):
    return big(f(rng, N, 128, 2048)).reshape(N, 8, 16, 4, 8, 16, 4)
def weights(rng, w):
    c, s = packed(np.ascontiguousarray(w).reshape(N, 128, 2048), rng)
    return {"wc": c, "ws": s}
def setup_inputs(rng):
    return {**numbers_of(rng), "p": bases(rng), **weights(rng, layers(rng))}
def setup_inputs_ties(rng):
    d = numbers_of(rng)
    p = bases(rng)
    o = rng.permutation(N)
    x = d["x"].astype(np.float32).reshape(N, 8, 16, C, 4)
    n = (N, 8, 8, C, 4)
    x[:, :, 8:] = (1.125 + 0.25 * rng.integers(0, 4, n)) * np.exp2(-1.0 * rng.integers(8, 15, n)) * rng.choice([-1.0, 1.0], n)
    x[:, :, 8, :, 0] = 1.96875
    x[:, :, :8] = 0
    u = d["u"].reshape(N, 128, 128, 4)
    u[:, :, ::16] = 0
    for r in range(N):
        if o[r] % 2 == 1: x[r, :, 0, :, 0] = rng.integers(0, 4, (8, C))
        else: x[r, :, 0, :, 0] = rng.integers(0, 7, (1, C)) + rng.integers(0, 2, (8, C))
        for h in range(0, 128, 16): u[r, h, h, 0] = 0.0 if o[r] == 0 else -1.0 if o[r] == 1 else 1.0
        if o[r] == 0:
            x[r, 7, 0, :, 0] = 0
            x[r, 7, 0, p[r, 0, 0], 0] = 1
            u[r, 112, 112, 0] = 1.0
    w = layers(rng)
    w[:, :, :, :, :, :8] = 0
    return {"x": x.reshape(N, 128, 4 * C).astype(BF), "u": u.reshape(N, 128, 512), "v": d["v"], "p": p, **weights(rng, w)}
def setup_inputs_near(rng):
    d = numbers_of(rng)
    x = d["x"].astype(np.float32).reshape(N, 8, 16, C, 4)
    u = d["u"].reshape(N, 128, 128, 4)
    o = rng.permutation(N) % 4
    x[:, :, 0] = 0
    x[:, :, 8:] = 0
    u[:, :, ::16] = 0
    for r in range(N):
        k = 1.0 if o[r] == 0 else 2.0 ** -30
        if o[r] < 3:
            s = rng.integers(0, 252, (1, C)) + rng.integers(0, 4, (8, C))
            for i in range(2): x[r, :, 8 + i] = ((s[:, :, None] >> (4 * i + np.arange(4))) & 1) * np.exp2(4 * i + np.arange(4) - 23.0)
            if o[r] < 2:
                x[r, :, 0, :, 0] = rng.choice([-1.0, 1.0], C)
                x[r, :, 11, :, 0] = 2.0 ** -10
            for g in rng.permutation(8)[:4]: x[r, g, 0, rng.integers(C), 0] = 2.0 ** 29 * rng.choice([-1.0, 1.0])
        else:
            for i in (10, 12): x[r, :, i, :, 0] = (1.0 + 0.125 * rng.integers(0, 2, (8, C))) * 2.0 ** -30
        for h in range(0, 128, 16):
            if o[r] < 3:
                u[r, h, h, 0] = k
                u[r, h + 8:h + 10, h] = k
                u[r, h + 11, h, 0] = k
            else:
                a = rng.choice([-1.0, 1.0])
                u[r, h + 10, h, 0] = 1.125 * k * a
                u[r, h + 12, h, 0] = -k * a
    w = layers(rng)
    for i in (0, 8, 9, 10, 11, 12, 13, 14, 15):
        w[:, :, i] = 0
        w[:, :, :, :, :, i] = 0
    return {"x": x.reshape(N, 128, 4 * C).astype(BF), "u": u.reshape(N, 128, 512), "v": d["v"], "p": bases(rng), **weights(rng, w)}
def setup_inputs_huge(rng):
    d = numbers_of(rng)
    o = rng.permutation(N)
    x = 0.6 + 0.06 * rng.random((N, 8, 16, C, 4)) + 0.03 * rng.random((N, 1, 1, C, 1))
    a = 1.0 - 0.1 * rng.random((N, 128, 8, 4))
    for r in range(N):
        if o[r] < N // 2: a[r] *= -1.0
        else:
            x[r] *= rng.choice([-1.0, 1.0], (1, 1, C, 1))
            a[r] *= rng.choice([-1.0, 1.0], (1, 8, 1))
    u = d["u"].reshape(N, 128, 128, 4)
    u[:, :, ::16] = (2.0 ** 30 * a).astype(np.float32).astype(BF)
    w = np.zeros((N, 128, 4, 128, 4), np.float32)
    i = np.arange(128)
    for b in range(4): w[:, i, b, i, b] = -4
    return {"x": (2.0 ** 30 * x).astype(np.float32).reshape(N, 128, 4 * C).astype(BF), "u": u.reshape(N, 128, 512), "v": d["v"], "p": bases(rng), **weights(rng, w.astype(BF))}
def setup_inputs_ends(rng):
    v = np.array(f(rng, N, 128, 512))
    o = rng.permutation(N) % 4
    x, u = np.zeros((N, 128, C, 4), np.float32), np.zeros((N, 128, 128, 4), np.float32)
    w, e = np.zeros((N, 128, 4, 128, 4), np.float32), []
    i = np.arange(128)
    for r in range(N):
        c = rng.choice([-1.0, 1.0], (1, C, 1))
        a = rng.choice([-1.0, 1.0], (1, 128, 1))
        if o[r] == 0:
            x[r] = 2.0 ** 30
            x[r, 64:] *= rng.choice([0.5, 1.0], (64, C, 4))
            x[r, 64:, ::4] = 2.0 ** 30
            u[r] = -2.0 ** 30
            u[r, 64:, :64] = 0
        elif o[r] == 1:
            x[r] = 2.0 ** 30 * c
            u[r] = 2.0 ** 30 * a
        elif o[r] == 2:
            x[r] = 2.0 ** -29 * rng.choice([-1.0, 1.0], (128, C, 4))
            u[r] = 2.0 ** -30 * rng.choice([-1.0, 1.0], (128, 128, 4))
        else:
            x[r] = 2.0 ** -29 * c
            u[r] = 2.0 ** -30 * a
        if o[r] > 1:
            for b in range(4): w[r, i, b, i, b] = 2.0 ** -20
        e.append(table(np.arange(C) if o[r] % 2 == 0 else C - 1 - np.arange(C)))
    v = (np.where(v < 0, -1.0, 1.0) * np.where(rng.permutation(N) % 2, 2.0 ** -30, 2.0 ** 30)[:, None, None]).astype(np.float32).astype(BF)
    return {"x": x.reshape(N, 128, 4 * C).astype(BF), "u": u.reshape(N, 128, 512).astype(BF), "v": v, "p": np.stack(e), **weights(rng, w.astype(BF))}
def setup_inputs_spread(rng):
    d = setup_inputs(rng)
    d["x"] = big(wide(rng, N, 128, 4 * C, cols=6))
    return d
def check_inputs(d):
    bad = []
    for k in ("x", "u", "v"):
        a = np.abs(d[k].astype(np.float32))
        if not (np.isfinite(a).all() and ((a == 0) | (a >= 2.0 ** -30) & (a <= 2.0 ** 30)).all()): bad.append("a value of " + k)
    none, least, most = [emit(mx_ref.quantize(np.full((128, 16), k, np.float32).astype(BF)))[1][0, 0] for k in (0.0, 2.0 ** -30, 2.0 ** 30)]
    for r in range(N):
        if not np.array_equal(np.sort(d["p"][r].reshape(-1)), np.arange(C)): bad.append("p: not every column once")
        if ((d["wc"][r] == 0x7F) | (d["wc"][r] == 0xFF)).any(): bad.append("wc: a code that is no number")
        s = mx_ref.live(d["ws"][r])
        if ((s != none) & ((s < least) | (s > most))).any(): bad.append("ws: a scale out of range")
    return bad
def reference(x, u, v, p, wc, ws):
    qu = [mx_ref.quantize(u[r]) for r in range(N)]
    lay = [pk(wc[r], ws[r]) for r in range(N)]
    now = [x[r] for r in range(N)]
    base = [entries(p[r]) for r in range(N)]
    order = np.zeros((N, 8, C), np.int64)
    for t in range(R):
        own, sent = [], []
        for r in range(N):
            q = mx_ref.quantize(now[r])
            own.append(decode(q))
            s = mx_ref.matmul(qu[r], q)[::16] + np.float32(0.0)
            o = base[r]
            for g in range(8):
                key = np.maximum.accumulate(s[g][o].reshape(-1, WIDTH[g]), axis=1).reshape(-1, 2 * WIDTH[g])
                o = np.take_along_axis(o.reshape(-1, 2 * WIDTH[g]), np.argsort(key, axis=1, kind="stable"), axis=1).reshape(-1)
                order[r, g] = o
            base[r] = o
            a = own[r].astype(BF)
            z = (gcols(a, order[r, :, :H]).astype(np.float32) + gcols(a, order[r, :, H:]).astype(np.float32)) * np.float32(0.5)
            sent.append(mx_ref.quantize(z.astype(BF)))
        for r in range(N):
            q = sent[(r - 1) % N]
            place = np.argsort(order[r], axis=1) % H
            now[r] = tile([gpick(mx_ref.matmul(pick(lay[r], np.arange(128 * b, 128 * b + 128)), q), place) * np.float32(0.03125) + own[r][:, b::4] for b in range(4)])
    y, od = np.zeros((N, 128, C), np.float32), np.zeros((N, 8, C), np.float32)
    oc, osc = np.zeros((N, 128, 4 * C), np.uint8), np.zeros((N, 16, C), np.uint8)
    for r in range(N):
        q = mx_ref.quantize(now[r])
        y[r] = mx_ref.matmul(mx_ref.quantize(v[r]), q)
        od[r] = order[r]
        oc[r], osc[r] = emit(q)
    return {"y": y, "od": od, "oc": oc, "osc": osc}

@@ -1,0 +1,644 @@
+from concourse.mybir import dt, AluOpType as OP, ActivationFunctionType as AF
+
+BIG = 2.0 ** 75
+EPS = 2.0 ** -120
+SEP = 64.0
+DIG = 2.0 ** 14
+R = 3
+WID = {0: 2, 1: 4, 2: 8, 3: 16, 4: 32}
+
+SCRATCH = {}
+PLACE = {}
+_used = {"ar": 0, "ar16": 0}
+SEMAPHORES = ["sv", "ss", "sp", "sg", "dx0", "dx1", "du", "dv", "dp", "dw", "doc", "dos", "dod", "dy"]
+
+
+def _buf(name, cols, dtype="float32", where="sbuf"):
+    SCRATCH[name] = (where, [128, cols], dtype)
+    PLACE[name] = (name, 0, cols)
+
+
+def _part(name, cols, arena="ar"):
+    PLACE[name] = (arena, _used[arena], cols)
+    _used[arena] += -(-cols // 16) * 16
+
+
+for _n, _c in (("n16", 512), ("i17", 68), ("iot", 512), ("iotm", 512), ("io4", 4), ("bff", 16), ("sgk", 32), ("rtab", 4),
+               ("mh", 64), ("md", 512), ("mda", 512), ("t2", 64), ("msk3", 68), ("msk4", 132), ("msk5", 260),
+               ("c0", 68), ("c1", 68), ("c2", 68), ("c3", 68), ("c4", 132), ("c5", 260), ("c6", 516), ("c7", 1028),
+               ("kk", 64), ("gm", 64), ("kd", 64), ("sm", 260), ("no", 256), ("np", 256), ("gg", 512), ("hh", 64), ("g5", 64), ("o5", 64), ("o6", 64),
+               ("jk", 1028), ("sum4", 4), ("sh", 32), ("shs", 128), ("a5", 8), ("ap6", 32), ("tr", 32), ("sw", 64), ("tr2", 64),
+               ("qa", 32), ("qb", 32), ("qt", 32), ("qe", 32), ("tl", 32), ("tr7", 32),
+               ("id6", 64), ("id7", 64), ("posw", 512), ("pds", 512), ("lr", 20), ("tbf", 4), ("idw", 64), ("ds", 512)):
+    _part(_n, _c)
+for _g in range(5):
+    for _s in ("g%d", "o%d", "id%dr", "rst%d"):
+        if _s != "o%d" or _g:
+            _part(_s % _g, 64)
+for _g in range(3):
+    for _s, _c in (("mq%d", 64), ("ms%d", 68), ("t1%d", 64), ("t3%d", 68)):
+        _part(_s % _g, _c)
+for _r in range(R):
+    _part("list%d" % _r, 32)
+    for _s, _c in (("w5s%d", 128), ("w5%d", 128), ("w6%d", 256), ("w7%d", 512)):
+        _part(_s % _r, _c)
+    SCRATCH["dg%d" % _r] = ("dram", [5, 128, 4], "float32")
+for _n, _c in (("uo", 64), ("rk", 4), ("tb", 4), ("tab5", 4), ("tab7", 32), ("own6", 4), ("own7", 4), ("off", 32), ("pos", 32),
+               ("tbl0", 4), ("tbl1", 4), ("tbl2", 4), ("tbl3", 4)):
+    _part(_n, _c, "ar16")
+_buf("ar", _used["ar"])
+_buf("ar16", _used["ar16"], "uint16")
+_buf("row", 512)
+_buf("yy", 512)
+for _g in range(8):
+    _buf("sw%d" % _g, 512)
+for _b in range(4):
+    _buf("fh%d" % _b, 512)
+    _buf("pa%d" % _b, 256)
+    _buf("pp%d" % _b, 256)
+for _b in range(2):
+    _buf("f%d" % _b, 512)
+    _buf("gp%d" % (_b + 2), 512)
+for _n, _c in (("pi", 1), ("bi", 16), ("uoi", 64), ("tbi", 4)):
+    _buf(_n, _c, "int32")
+for _n, _c in (("xt", 2048), ("ut", 512), ("vt", 512), ("zt", 1024), ("ee", 2048), ("ones", 512)):
+    _buf(_n, _c, "bfloat16")
+for _n, _c in (("xq", 512), ("uq", 128), ("uc", 1024), ("vq", 128), ("wq", 512), ("zq", 256), ("eq", 512)) + tuple(("zl%d" % r, 256) for r in range(R)):
+    _buf(_n, _c, "float8_e4m3fn_x4")
+    _buf(_n + "s", _c, "uint8")
+for _b in range(8):
+    _buf("b%d" % _b, 512, "float32", "psum")
+for _r in range(R):
+    SEMAPHORES += [s % _r for s in ("ac%d", "as%d", "lc%d", "ls%d", "dl%d", "dm%d", "dn%d", "db%d")]
+    SEMAPHORES += ["dga%d%d" % (_r, g) for g in range(5)]
+
+
+def rank_program(g, core, T, topo):
+    rank = T.rank_of(core)
+    if rank is None:
+        return
+    nxt = T.cores[(rank + 1) % len(T.cores)]
+    queues = {"v": g.vector, "s": g.scalar, "t": g.tensor, "g": g, "y": g.sync}
+    semof = {"v": "sv", "s": "ss", "t": "sp", "g": "sg"}
+    count = {k: 0 for k in semof}
+    known = {k: {} for k in queues}
+    hist = {}
+    total = {}
+
+    def need(q, tok):
+        sem, val = tok
+        if known[q].get(sem, 0) < val:
+            queues[q].wait_ge(T.sem[sem], val)
+            known[q][sem] = val
+
+    def v(name, c0=0, c1=None, st=1, p0=0, p1=128):
+        name, at, cols = PLACE[name]
+        c0, c1 = c0 + at, (cols if c1 is None else c1) + at
+        ap = T[name][p0:p1, c0:c1] if st == 1 else T[name][p0:p1, c0:c1:st]
+        return (name, p0, p1, c0, c1, ap, st)
+
+    def quad(name, c0, c1, a):
+        return v(name, c0, c1, 1, 32 * a, 32 * a + 32)
+
+    def deps(q, ins, outs):
+        toks = {}
+        for w, views in ((0, ins), (1, outs)):
+            for n, p0, p1, c0, c1, ap, st in views:
+                ps = n in SCRATCH and SCRATCH[n][0] == "psum"
+                for (tok, eng, hw, a, b, c, d, s) in hist.get(n, []):
+                    if ps and eng != q or (w or hw) and a < p1 and p0 < b and c < c1 and c0 < d and not (s == st > 1 and (c - c0) % st):
+                        toks[tok[0]] = max(toks.get(tok[0], 0), tok[1])
+        for s in sorted(toks):
+            need(q, (s, toks[s]))
+
+    def note(q, tok, ins, outs):
+        for w, views in ((0, ins), (1, outs)):
+            for n, p0, p1, c0, c1, ap, st in views:
+                h = hist.setdefault(n, [])
+                if w:
+                    h[:] = [e for e in h if not (st in (1, e[7]) and p0 <= e[3] and e[4] <= p1 and c0 <= e[5] and e[6] <= c1 and (e[5] - c0) % st == 0)]
+                else:
+                    h[:] = [e for e in h if not (e[1] == q and not e[2] and e[0][0] == tok[0] and e[3:] == (p0, p1, c0, c1, st))]
+                h.append((tok, q, w, p0, p1, c0, c1, st))
+
+    def op(q, fn, outs, ins):
+        deps(q, ins, outs)
+        i = fn(queues[q])
+        count[q] += 1
+        i.then_inc(T.sem[semof[q]], 1)
+        note(q, (semof[q], count[q]), ins, outs)
+
+    def dma(q, sem, group, out, in_):
+        out, in_ = [a if len(a) > 6 else a + (1,) for a in (out, in_)]
+        deps(q, [in_], [out])
+        queues[q].dma_start(out[5], in_[5]).then_inc(T.sem[sem], 16)
+        total[sem] = 16 * group
+        note(q, (sem, 16 * group), [in_], [out])
+
+    def cd(name):
+        n, p0, p1, a, b, ap, st = v(name)
+        return (n, p0, p1, a, b, ap.bitcast(dt.uint8), 1)
+
+    def ts(out, in0, s1, op0, s2=None, op1=None):
+        ins = [in0] + [s for s in (s1, s2) if isinstance(s, tuple)]
+        a, b = [s[5] if isinstance(s, tuple) else s for s in (s1, s2)]
+        if op1 is None:
+            op("v", lambda e: e.tensor_scalar(out[5], in0[5], a, None, op0), [out], ins)
+        else:
+            op("v", lambda e: e.tensor_scalar(out[5], in0[5], a, b, op0, op1), [out], ins)
+
+    def tt(out, a, b, o):
+        op("v", lambda e: e.tensor_tensor(out[5], a[5], b[5], o), [out], [a, b])
+
+    def ttg(out, win, off, b):
+        op("v", lambda e: e.tensor_tensor(out[5], win[5].indirect(off[5]), b[5], OP.add), [out], [win, off, b])
+
+    def scan(out, d0, d1, init, o0, o1):
+        op("v", lambda e: e.tensor_tensor_scan(out[5], d0[5], d1[5], init, o0, o1), [out], [d0, d1])
+
+    def copy(out, in_):
+        op("v", lambda e: e.tensor_copy(out[5], in_[5]), [out], [in_])
+
+    def trans(out, in_):
+        op("v", lambda e: e.transpose(out[5], in_[5]), [out], [in_])
+
+    def fill(out, c):
+        op("v", lambda e: e.memset(out[5], c), [out], [])
+
+    def vgather(out, win, off):
+        op("v", lambda e: e.tensor_copy(out[5], win[5].indirect(off[5])), [out], [win, off])
+
+    def scatter(win, off, in_):
+        op("v", lambda e: e.tensor_copy(win[5].indirect(off[5]), in_[5]), [win], [off, in_])
+
+    def act(out, in_, scale=1.0):
+        op("s", lambda e: e.activation(out[5], in_[5], AF.Copy, scale=scale), [out], [in_])
+
+    def sgather(out, win, off):
+        op("s", lambda e: e.activation(out[5], win[5].indirect(off[5]), AF.Copy), [out], [win, off])
+
+    def accum(out, in_, acc):
+        op("s", lambda e: e.activation(out[5], in_[5], AF.Copy, accum_out=acc[5]), [out, acc], [in_])
+
+    def quant(c, s, t):
+        op("v", lambda e: e.quantize_mx(c[5], s[5], t[5]), [c, s], [t])
+
+    def mm(out, l, ls, r_, rs):
+        op("t", lambda e: e.matmul_mx(out[5], l[5], ls[5], r_[5], rs[5], True, True), [out], [l, ls, r_, rs])
+
+    def iota(out, pat, base=0, cm=0):
+        if out[0] in ("pi", "uoi"):
+            op("g", lambda e: e.iota(out[5], pat, base, cm), [out], [])
+        else:
+            op("g", lambda e: e.iota(out[5], pat, base, cm, allow_small_or_imprecise_dtypes=True), [out], [])
+
+    def select(out, in_, pat, fill_, base, cm):
+        op("g", lambda e: e.affine_select(out[5], in_[5], pat, OP.is_equal, fill_, base, cm), [out], [in_])
+
+    def group_of(B):
+        return 2 * (B % 4) + B // 4
+
+    dma("y", "du", 1, v("ut"), ("u", 0, 128, 0, 512, T.u[:, :]))
+    dma("s", "dx0", 1, v("xt", 0, 1024), ("x", 0, 128, 0, 1024, T.x[:, 0:1024]))
+    dma("y", "dx1", 1, v("xt", 1024, 2048), ("x", 0, 128, 1024, 2048, T.x[:, 1024:2048]))
+    for B in range(8):
+        h = 16 * group_of(B)
+        dma("y", "dp", 8, v("tbi", 0, 4, 1, h, h + 16), ("p", 0, 16, 4 * B, 4 * B + 4, T.p[:, 4 * B:4 * B + 4]))
+    dma("y", "dv", 1, v("vt"), ("v", 0, 128, 0, 512, T.v[:, :]))
+    dma("y", "dw", 2, cd("wq"), ("wc", 0, 128, 0, 2048, T.wc[:, :]))
+    dma("y", "dw", 2, v("wqs"), ("ws", 0, 128, 0, 512, T.ws[:, :]))
+
+    iota(v("pi"), [[0, 1]], 0, 1)
+    iota(v("n16", 0, 64), [[0, 4], [1, 16]])
+    iota(v("io4"), [[16, 4]])
+    iota(v("i17"), [[0, 4], [1, 17]])
+    iota(v("uoi"), [[16, 8], [0, 8]])
+    iota(v("iot"), [[1, 512]])
+    fill(v("ones"), 1.0)
+    for b in range(4):
+        select(v("ee", 512 * b, 512 * b + 512), v("ones"), [[-1, 512]], 0.0, b, 4)
+    iota(v("n16", 64, 512), [[0, 28], [1, 16]])
+    iota(v("ap6"), [[0, 32]])
+    for r in range(R):
+        select(v("w5s%d" % r), v("iot", 0, 128), [[0, 128]], BIG, -1, 0)
+        for n, c in (("w5%d", 128), ("w6%d", 256), ("w7%d", 512), ("list%d", 32)):
+            iota(v(n % r), [[0, c]])
+    iota(v("iotm"), [[0, 2], [1, 256]])
+
+    def upick(a, b):
+        o, w, f = v("uc", 128 * a, 128 * b), v("uq"), v("uo", 8 * a, 8 * b)
+        op("v", lambda e: e.tensor_copy(o[5].bitcast(dt.uint32), w[5].bitcast(dt.uint32).indirect(f[5])), [o], [w, f])
+        sgather(v("ucs", 128 * a, 128 * b), v("uqs"), f)
+
+    col = [0]
+
+    def newcol():
+        col[0] += 1
+        return v("sgk", col[0] - 1, col[0])
+
+    def dscp(a, b):
+        return v("sgk", 0, 1, 1, a, b)
+
+    q = v("bff", 0, 1)
+    dsc, q1, e6, e7 = newcol(), newcol(), newcol(), newcol()
+    bit, th, rs0, rs, rw = {}, {}, {}, {}, {}
+    for k, c in ((0, 1), (1, 2), (2, 3), (5, 4), (6, 5), (7, 6)):
+        bit[k], th[k] = v("bff", c, c + 1), newcol()
+    lo = {0: v("bff", 7, 8), 1: v("bff", 8, 9), 2: bit[2]}
+    for k in range(3):
+        rs0[k], rs[k], rw[k] = newcol(), newcol(), newcol()
+    spare = []
+
+    def later(f, *a):
+        spare.append((f, a))
+
+    def fit(n):
+        for f, a in spare[:n]:
+            f(*a)
+        del spare[:n]
+
+    def masks(k):
+        m, t, s, u = "mq%d" % k, "t1%d" % k, "ms%d" % k, "t3%d" % k
+        later(ts, rs0[k], bit[k], -2.0, OP.mult, lo[k], OP.add)
+        later(ts, v(t), v("n16", 0, 64), lo[k], OP.is_ge)
+        later(ts, v("c%d" % k, 16, 68, 17), v("rtab"), bit[k], OP.subtract, SEP, OP.mult)
+        later(fill, v("rst%d" % k), -BIG)
+        later(ts, rs[k], rs0[k], float(WID[k]), OP.add)
+        later(ts, rw[k], rs0[k], 2.0 * WID[k], OP.add)
+        later(tt, v(m), v(t), v("t2"), OP.mult)
+        later(fill, v("rst%d" % k, 0, 64, WID[k]), BIG)
+        later(ts, v(s), v("i17"), rs[k], OP.not_equal)
+        later(ts, v(u), v("i17"), rw[k], OP.is_equal, SEP - 1.0, OP.mult)
+        later(ts, v(m), v(m), BIG, OP.add)
+        later(tt, v(s), v(s), v(u), OP.add)
+        later(fill, v(s, 0, 68, 17), 0.0)
+
+    def masks3():
+        later(fill, v("msk3"), 1.0)
+        later(ts, v("mh"), v("n16", 0, 64), q, OP.is_equal, -2 * BIG, OP.mult)
+        later(copy, v("c3", 16, 68, 34), v("rtab", 0, 4, 2))
+        later(ts, v("c3", 33, 68, 34), v("rtab", 1, 4, 2), -16.0, OP.add)
+        later(fill, v("msk3", 0, 68, 17), 0.0)
+        later(ts, v("mh"), v("mh"), BIG, OP.add)
+
+    def masks4():
+        later(fill, v("rst4"), -BIG)
+        later(fill, v("msk4"), 1.0)
+        later(copy, v("c4", 32, 66, 33), v("rtab", 0, 2))
+        later(ts, v("c4", 98, 132, 33), v("rtab", 2, 4), -32.0, OP.add)
+        later(fill, v("rst4", 0, 64, 32), BIG)
+        later(fill, v("msk4", 0, 132, 33), 0.0)
+
+    def places(a, b):
+        for c in range(a, b, 64):
+            later(ts, v("mda", c, c + 64), v("n16", c, c + 64), q1, OP.is_equal, DIG - 1.0, OP.mult)
+            later(ts, v("md", c, c + 64), v("n16", c, c + 64), q, OP.is_gt)
+        for c in range(a, b, 64):
+            later(tt, v("md", c, c + 64), v("md", c, c + 64), v("mda", c, c + 64), OP.add)
+
+    def masks5():
+        later(fill, v("msk5"), 1.0)
+        later(copy, v("c5", 64, 260, 65), v("rtab"))
+        later(ts, e6, bit[5], 2.0, OP.mult)
+        later(fill, v("msk5", 0, 260, 65), 0.0)
+        later(ts, e7, bit[6], 2.0, OP.mult, e6, OP.add)
+        later(ts, v("c6", 128, 516, 129), v("rtab"), e6, OP.add)
+        later(ts, v("c7", 256, 1028, 257), v("rtab"), e7, OP.add)
+        places(64, 128)
+
+    def units(k):
+        o, i = 128 * k, 512 * k
+        later(quant, v("eq", o, o + 128), v("eqs", o, o + 128), v("ee", i, i + 512))
+
+    for j, m in enumerate((15, 2, 4, 8, 32, 64, 16, 14, 12)):
+        ts(v("bi", j, j + 1), v("pi"), m, OP.bitwise_and)
+    fill(v("rst3"), -BIG)
+    copy(v("bff", 0, 9), v("bi", 0, 9))
+    fill(v("rst3", 0, 64, 16), BIG)
+    copy(v("uo"), v("uoi"))
+    ts(dsc, q, 15.0, OP.is_equal, 1.0 - 1.0 / DIG, OP.mult)
+    ts(q1, q, 1.0, OP.add)
+    ts(v("rtab"), v("io4"), q, OP.add)
+    ts(v("t2"), v("n16", 0, 64), q, OP.is_le, -2 * BIG, OP.mult)
+    ts(v("md", 0, 64), v("n16", 0, 64), q, OP.is_gt)
+    for k, m in ((0, 2), (1, 4), (2, 8), (5, 32), (6, 64), (7, 16)):
+        ts(th[k], bit[k], -EPS / m, OP.mult)
+    ts(dsc, dsc, 1.0 / DIG, OP.add)
+    ts(v("mda", 0, 64), v("n16", 0, 64), q1, OP.is_equal, DIG - 1.0, OP.mult)
+    masks(0)
+    fit(99)
+    tt(v("md", 0, 64), v("md", 0, 64), v("mda", 0, 64), OP.add)
+    quant(v("uq"), v("uqs"), v("ut"))
+    upick(0, 1)
+    masks(1)
+
+    def compact(c1, p0=0, p1=128):
+        return v("ds", 15, c1, 16, p0, p1)
+
+    for r in range(R):
+        lst = "list%d" % r
+        dg = T["dg%d" % r]
+        if r == 0:
+            copy(v("tb"), v("tbi"))
+        else:
+            ts(v("tb"), v("tbf"), dsc, OP.mult)
+        quant(v("xq", 0, 256), v("xqs", 0, 256), v("xt", 0, 1024))
+        quant(v("xq", 256, 512), v("xqs", 256, 512), v("xt", 1024, 2048))
+        sgather(v("id0r"), v("iot"), v("tb"))
+
+        def score(k, bank, c0=0, c1=512):
+            mm(v(bank, 0, c1 - c0), v("uc", 128 * k, 128 * k + 128), v("ucs", 128 * k, 128 * k + 128), v("xq", c0, c1), v("xqs", c0, c1))
+
+        def scored(k, bank):
+            act(v("sw%d" % k), v(bank), -1.0)
+
+        def unpack(b):
+            mm(v("b%d" % b), v("eq", 128 * b, 128 * b + 128), v("eqs", 128 * b, 128 * b + 128), v("xq"), v("xqs"))
+
+        def half(b):
+            act(v("fh%d" % b), v("b%d" % b), 0.5)
+
+        score(0, "b4", 0, 256)
+        score(0, "b5", 256, 512)
+        if r == 0:
+            upick(1, 4)
+        ts(v("sw0", 0, 256), v("b4", 0, 256), -1.0, OP.mult)
+        act(v("sw0", 256, 512), v("b5", 0, 256), -1.0)
+        fit(3)
+        vgather(v("g0"), v("sw0"), v("tb"))
+        fit(3)
+        score(1, "b6")
+        scored(1, "b6")
+        sgather(v("o1"), v("sw1"), v("tb"))
+
+        def tail(k, part):
+            dst = "idw" if k == 4 else "id%dr" % (k + 1)
+            if part == 0:
+                scatter(v(dst), v("rk"), v("id%dr" % k))
+            elif part == 1:
+                scan(v("ds", 0, 64), v("md", 0, 64), v(dst), 0.0, OP.mult, OP.add)
+            else:
+                tab = "tab5" if k == 4 else "tbl%d" % k
+                ts(v(tab), compact(64), dsc, OP.mult)
+                sgather(v("o%d" % (k + 2)), v("sw%d" % (k + 2)), v(tab))
+                act(v("lr", 4 * k, 4 * k + 4), compact(64))
+                dma("y", "dga%d%d" % (r, k), 1, ("dg%d" % r, 0, 128, k, k + 1, dg[k]), v("lr", 4 * k, 4 * k + 4))
+
+        for k in range(5):
+            w = WID[k]
+            G = v("g%d" % k)
+            C = "c%d" % k
+            if k < 3:
+                tt(v("gm"), G, v("mq%d" % k), OP.max)
+                scan(v("kk"), v("rst%d" % k), G, BIG, OP.max, OP.min)
+                if k:
+                    tail(k - 1, 0)
+                scan(v("kd"), v("rst3"), v("gm"), BIG, OP.max, OP.min)
+            else:
+                scan(v("kk"), v("rst%d" % k), G, BIG, OP.max, OP.min)
+                tail(k - 1, 0)
+                scan(v("kd"), v("mh"), v("kk"), BIG, OP.min, OP.max)
+            if k:
+                tail(k - 1, 1)
+            fit(3)
+            s = 17 if k < 3 else w + 1
+            for c in range(4):
+                x = v("kd", 16 * c + 15, 16 * c + 16)
+                if k < 3:
+                    ts(v(C, s * c, s * c + 16), v("kk", 16 * c, 16 * c + 16), x, OP.subtract, th[k], OP.is_gt)
+                else:
+                    left = c % 2 == 0 if k == 3 else c < 2
+                    a = 16 * (c ^ 1) if k == 3 else 32 * left
+                    ts(v(C, s * c, s * c + w), v("kk", a, a + w), x, OP.is_gt if left else OP.is_ge)
+            if k:
+                tail(k - 1, 2)
+            scan(v("sm", 0, 4 * s), v(("ms%d" if k < 3 else "msk%d") % k), v(C), 0.0, OP.mult, OP.add)
+            fit(4)
+            if k < 3:
+                ts(v("rk"), v("sm", 16, 68, 17), 1.0 / SEP, OP.mult)
+            else:
+                copy(v("rk"), v("sm", w, 4 * s, s))
+            fit(4)
+            scatter(v("g%d" % (k + 1)), v("rk"), v("o%d" % (k + 1)))
+            fit(99)
+            if r == 0:
+                if k == 0:
+                    score(2, "b7")
+                    score(3, "b4")
+                    scored(2, "b7")
+                    scored(3, "b4")
+                    masks(2)
+                    later(upick, 4, 5)
+                    masks3()
+                elif k == 1:
+                    score(4, "b5")
+                    scored(4, "b5")
+                    later(upick, 5, 6)
+                    masks4()
+                    units(0)
+                    units(1)
+                elif k == 2:
+                    score(5, "b6")
+                    scored(5, "b6")
+                    unpack(0)
+                    later(upick, 6, 8)
+                    units(2)
+                    units(3)
+                elif k == 3:
+                    score(6, "b7")
+                    scored(6, "b7")
+                    score(7, "b4")
+                    for b in range(1, 4):
+                        unpack(b)
+                    masks5()
+                else:
+                    scored(7, "b4")
+                    half(0)
+            elif k == 0:
+                score(2, "b7")
+                scored(2, "b7")
+                score(3, "b4")
+                for b in range(4):
+                    unpack(b)
+                    if b < 3:
+                        score(b + 4, "b%d" % (b + 5))
+                scored(3, "b4")
+                score(7, "b4")
+                half(0)
+            elif k < 3:
+                scored(k + 3, "b%d" % (k + 4))
+                half(k)
+            elif k == 3:
+                scored(6, "b7")
+                scored(7, "b4")
+
+        def runmin(out, a, b=None):
+            scan(out, a, b or a, BIG, OP.min, OP.min)
+
+        def hold(w):
+            if w == 64:
+                scan(v("hh"), v("mh"), v("no", 0, 64), BIG, OP.min, OP.max)
+            else:
+                for a in range(4):
+                    c = 64 * (a % (w // 64))
+                    scan(quad("hh", 0, 64, a), quad("mh", 0, 64, a), quad("no", c, c + 64, a), BIG, OP.min, OP.max)
+
+        def versus(k, w, c):
+            s = w + 1
+            ts(v("c%d" % k, s * c, s * c + w), v("np", 0, w), v("hh", 16 * c + 15, 16 * c + 16), OP.subtract, th[k], OP.is_gt)
+            if k > 5:
+                accum(v("jk", s * c, s * c + s), v("c%d" % k, s * c, s * c + s), v("sum4", c, c + 1))
+
+        def swap1(out, in_, n, src=quad):
+            for a in range(4):
+                o, i = quad(out, 0, n, a), src(in_, 0, n, a ^ 1)
+                if a < 2:
+                    copy(o, i)
+                else:
+                    act(o, i)
+
+        def dsq(_n, c0, n, a):
+            return compact(16 * n, 32 * a, 32 * a + 32)
+
+        def swap2(out, in_, n):
+            copy(v(out, 0, n, 1, 0, 64), v(in_, 0, n, 1, 64, 128))
+            act(v(out, 0, n, 1, 64, 128), v(in_, 0, n, 1, 0, 64))
+
+        def owns(name, src, per):
+            for a in range(4):
+                c = 4 * (a % per)
+                ts(quad(name, 0, 4, a), quad(src, c, c + 4, a), dscp(32 * a, 32 * a + 32), OP.mult)
+
+        runmin(v("no", 0, 64), v("g5"))
+        tail(4, 0)
+        swap1("np", "no", 64)
+        hold(64)
+        tail(4, 1)
+        for c in range(4):
+            versus(5, 64, c)
+        tail(4, 2)
+        fit(99)
+        if r == 0:
+            places(128, 512)
+            later(quant, v("vq"), v("vqs"), v("vt"))
+        scan(v("sm"), v("msk5"), v("c5"), 0.0, OP.mult, OP.add)
+        copy(v("rk"), v("sm", 64, 260, 65))
+        fit(3)
+        scatter(v("w5s%d" % r), v("rk"), v("o6"))
+        swap1("shs", "w5s%d" % r, 128)
+        scatter(v("w5%d" % r), v("rk"), v("idw"))
+        runmin(v("no", 0, 128), v("w5s%d" % r), v("shs"))
+        scan(v("ds", 0, 128), v("md", 0, 128), v("w5%d" % r), 0.0, OP.mult, OP.add)
+        swap2("np", "no", 128)
+        fit(3)
+        hold(128)
+        swap1("sh", "ds", 8, dsq)
+        versus(6, 128, 0)
+        versus(6, 128, 1)
+        tt(v("a5"), compact(128), v("sh", 0, 8), OP.add)
+        versus(6, 128, 2)
+        versus(6, 128, 3)
+        owns("own6", "a5", 2)
+        fit(8)
+        sgather(v("id6"), v("iot"), v("own6"))
+        ts(v("rk"), v("sum4"), 1.0, OP.mult)
+        scatter(v("w6%d" % r), v("rk"), v("id6"))
+        for B in range(4):
+            h = 16 * (4 * (B % 2) + B // 2)
+            dma("y", "dm%d" % r, 4, v(lst, 8 * B, 8 * B + 8, 1, 80, 96), v("a5", 0, 8, 1, h, h + 16))
+        for B in range(8):
+            h = 16 * group_of(B)
+            dma("y", "dl%d" % r, 8, v(lst, 4 * B, 4 * B + 4, 1, 0, 80), ("dg%d" % r, h, h + 16, 0, 5, dg[0:5, h:h + 16, :]))
+        fit(99)
+        scan(v("ds", 0, 256), v("md", 0, 256), v("w6%d" % r), 0.0, OP.mult, OP.add)
+        swap1("sh", "ds", 16, dsq)
+        tt(v("ap6", 0, 16), compact(256), v("sh", 0, 16), OP.add)
+        trans(v("tr"), v("ap6"))
+        swap2("sh", "tr", 32)
+        tt(v("sw", 32, 48), v("tr", 16, 32), v("sh", 16, 32), OP.add)
+        tt(v("sw", 48, 64), v("tr", 0, 16), v("sh", 0, 16), OP.add)
+        tt(v("sw", 0, 32), v("tr"), v("sh"), OP.add)
+        trans(v("tr2"), v("sw"))
+        ts(v("tab7", 16, 32), v("tr2", 32, 48), dsc, OP.mult)
+        ts(v("tab7", 0, 16), v("tr2", 0, 16), dsc, OP.mult)
+        for j in range(2):
+            dma("y", "dn%d" % r, 2, v(lst, 16 * j, 16 * j + 16, 1, 96, 112), v("tr2", 0, 16, 1, 16 * j, 16 * j + 16))
+        sgather(v("gg", 256, 512), v("sw7"), v("tab7", 16, 32))
+        vgather(v("gg", 0, 256), v("sw7"), v("tab7", 0, 16))
+        owns("own7", "tr2", 4)
+        sgather(v("id7"), v("iot"), v("own7"))
+        runmin(v("no"), v("gg", 0, 256))
+        runmin(v("np"), v("gg", 256, 512))
+        hold(256)
+        for c in range(4):
+            versus(7, 256, c)
+        if r == 0:
+            half(1)
+            half(2)
+        half(3)
+        ts(v("rk"), v("sum4"), 1.0, OP.mult)
+        scatter(v("w7%d" % r), v("rk"), v("id7"))
+        ts(v("off", 0, 32, 1, 0, 96), v(lst, 0, 32, 1, 0, 96), dscp(0, 96), OP.mult)
+        trans(quad("tl", 0, 32, 3), quad(lst, 0, 32, 3))
+        scan(v("ds"), v("md"), v("w7%d" % r), 0.0, OP.mult, OP.add)
+        copy(quad("qe", 0, 16, 3), quad("tl", 0, 16, 3))
+        tt(v("qa", 0, 32, 1, 64, 128), compact(512, 64, 128), compact(512, 0, 64), OP.add)
+        tt(quad("qb", 0, 32, 3), quad("qa", 0, 32, 3), quad("qa", 0, 32, 2), OP.add)
+        trans(quad("qt", 0, 32, 3), quad("qb", 0, 32, 3))
+        tt(quad("qe", 16, 32, 3), quad("qt", 0, 16, 3), quad("qt", 16, 32, 3), OP.add)
+        trans(quad("tr7", 0, 32, 3), quad("qe", 0, 32, 3))
+        ts(quad("off", 0, 32, 3), quad("tr7", 0, 32, 3), dscp(96, 128), OP.mult)
+        for b in range(1, 4):
+            sgather(v("pa%d" % b), v("fh%d" % b), v("off", 0, 16))
+        vgather(v("pa0"), v("fh0"), v("off", 0, 16))
+        for b in (1, 0, 2, 3):
+            ttg(v("zt", b, 1024, 4), v("fh%d" % b), v("off", 16, 32), v("pa%d" % b))
+        quant(v("zq"), v("zqs"), v("zt"))
+        rid, pid, _s = topo.addr(nxt)
+        eng = topo.engines(core, nxt)
+        for src, land, sem, loc, es in ((cd("zq"), cd("zl%d" % r), "ac%d" % r, "lc%d" % r, eng[0::2]),
+                                        (v("zqs"), v("zl%ds" % r), "as%d" % r, "ls%d" % r, eng[1::4])):
+            deps("g", [src], [])
+            g.remote_dma(land[5], src[5], T.sem[sem], T.sem[loc], pid, rid, sum(1 << e for e in es))
+            total[sem] = total[loc] = len(es)
+            note("g", (loc, len(es)), [src], [])
+            note("x", (sem, len(es)), [], [land])
+        if r < R - 1:
+            for B in range(8):
+                h = 16 * group_of(B)
+                dma("y", "db%d" % r, 8, v("tbf", 0, 4, 1, h, h + 16), v("tr7", 4 * B, 4 * B + 4, 1, 112, 128))
+        act(v("f0"), v("b0"))
+        act(v("f1"), v("b1"))
+        scatter(v("posw"), v("off"), v("iotm"))
+        scan(v("pds"), v("md"), v("posw"), 0.0, OP.mult, OP.add)
+        ts(v("pos"), v("pds", 15, 512, 16), dsc, OP.mult)
+        if r == R - 1:
+            sgather(v("row"), v("iot"), v("off"))
+            dma("y", "dod", 1, ("od", 0, 8, 0, 512, T.od[:, :]), ("row", 0, 128, 0, 512, T.row[0:128:16, :]))
+        for b in (0, 2, 1, 3):
+            mm(v("b%d" % (4 + b), 0, 256), v("wq", 128 * b, 128 * b + 128), v("wqs", 128 * b, 128 * b + 128), v("zl%d" % r), v("zl%ds" % r))
+        for b in (2, 3):
+            act(v("pp%d" % b), v("b%d" % (4 + b), 0, 256), 0.03125)
+        for b in (0, 1):
+            ts(v("pp%d" % b), v("b%d" % (4 + b), 0, 256), 0.03125, OP.mult)
+        for b in (2, 3):
+            sgather(v("gp%d" % b), v("pp%d" % b), v("pos"))
+        for b in (0, 1):
+            ttg(v("xt", b, 2048, 4), v("pp%d" % b), v("pos"), v("f%d" % b))
+        for b in (2, 3):
+            for c in (0, 256):
+                tt(v("xt", 4 * c + b, 4 * c + 1024, 4), v("gp%d" % b, c, c + 256), v("b%d" % b, c, c + 256), OP.add)
+
+    for c in (0, 256):
+        quant(v("xq", c, c + 256), v("xqs", c, c + 256), v("xt", 4 * c, 4 * c + 1024))
+        mm(v("b4" if c == 0 else "b5", 0, 256), v("vq"), v("vqs"), v("xq", c, c + 256), v("xqs", c, c + 256))
+    dma("y", "doc", 1, ("oc", 0, 128, 0, 2048, T.oc[:, :]), cd("xq"))
+    for k in range(4):
+        dma("y", "dos", 4, ("osc", 4 * k, 4 * k + 4, 0, 512, T.osc[4 * k:4 * k + 4, :]), v("xqs", 0, 512, 1, 32 * k, 32 * k + 4))
+    copy(v("yy", 0, 256), v("b4", 0, 256))
+    act(v("yy", 256, 512), v("b5", 0, 256))
+    dma("y", "dy", 1, ("y", 0, 128, 0, 512, T.y[:, :]), v("yy"))
+    for k in semof:
+        need("g", (semof[k], count[k]))
+    for s in total:
+        need("g", (s, total[s]))

@@ -5,11 +5,11 @@ EPS = 2.0 ** -120
 SEP = 64.0
 DIG = 2.0 ** 14
 R = 3
-WID = {0: 2, 1: 4, 2: 8, 3: 16, 4: 32}
+WID = [2, 4, 8, 16, 32, 64, 128, 256]
 
 SCRATCH = {}
 PLACE = {}
-_used = {"ar": 0, "ar16": 0}
+_used = {"ar": 0, "ar16": 0, "arb": 0}
 SEMAPHORES = ["sv", "ss", "sp", "sg", "dx0", "dx1", "du", "dv", "dp", "dw", "doc", "dos", "dod", "dy"]
 
 
@@ -23,13 +23,15 @@ def _part(name, cols, arena="ar"):
     _used[arena] += -(-cols // 16) * 16
 
 
-for _n, _c in (("n16", 512), ("i17", 68), ("iot", 512), ("iotm", 512), ("io4", 4), ("bff", 16), ("sgk", 32), ("rtab", 4),
-               ("mh", 64), ("md", 512), ("mda", 512), ("t2", 64), ("msk3", 68), ("msk4", 132), ("msk5", 260),
-               ("c0", 68), ("c1", 68), ("c2", 68), ("c3", 68), ("c4", 132), ("c5", 260), ("c6", 516), ("c7", 1028),
-               ("kk", 64), ("gm", 64), ("kd", 64), ("sm", 260), ("no", 256), ("np", 256), ("gg", 512), ("hh", 64), ("g5", 64), ("o5", 64), ("o6", 64),
-               ("jk", 1028), ("sum4", 4), ("sh", 32), ("shs", 128), ("a5", 8), ("ap6", 32), ("tr", 32), ("sw", 64), ("tr2", 64),
-               ("qa", 32), ("qb", 32), ("qt", 32), ("qe", 32), ("tl", 32), ("tr7", 32),
-               ("id6", 64), ("id7", 64), ("posw", 512), ("pds", 512), ("lr", 20), ("tbf", 4), ("idw", 64), ("ds", 512)):
+for _n, _c in (("n16", 64), ("i17", 68), ("iot", 512), ("io4", 4), ("bff", 16), ("sgk", 48), ("rtab", 4), ("big", 128),
+               ("mh", 64), ("md", 256), ("mda", 64), ("c0", 68), ("c1", 68), ("c2", 68),
+               ("kk", 64), ("gm", 64), ("kd", 64), ("sm", 68), ("g5", 64), ("o5", 64), ("o6", 64), ("idw", 64),
+               ("no5", 64), ("np5", 64), ("hh5", 64), ("no6", 128), ("np6", 128), ("hh6", 64), ("id6", 64), ("lr5", 4),
+               ("qa", 16), ("ap6", 16), ("gg", 256), ("no7", 256), ("t7", 288), ("np7", 256), ("hh7", 64), ("idg", 256), ("id7", 64),
+               ("jk", 774), ("sum4", 4), ("ds", 64), ("ds6", 128), ("ds7", 256),
+               ("posw", 512), ("pds", 512), ("lr", 20), ("tbf", 4)):
+    _part(_n, _c)
+for _n, _c in (("de", 512), ("qc", 32), ("qb", 32), ("qt", 32), ("qe", 32), ("tr", 32), ("sh5", 4)):
     _part(_n, _c)
 for _g in range(5):
     for _s in ("g%d", "o%d", "id%dr", "rst%d"):
@@ -38,16 +40,22 @@ for _g in range(5):
 for _g in range(3):
     for _s, _c in (("mq%d", 64), ("ms%d", 68), ("t1%d", 64), ("t3%d", 68)):
         _part(_s % _g, _c)
+for _g in range(3, 8):
+    _part("c%d" % _g, 4 * (WID[_g] + 2), "arb")
+    if _g < 7:
+        _part("msk%d" % _g, 4 * (WID[_g] + 2), "arb")
+_part("smb", 520, "arb")
 for _r in range(R):
     _part("list%d" % _r, 32)
     for _s, _c in (("w5s%d", 128), ("w5%d", 128), ("w6%d", 256), ("w7%d", 512)):
         _part(_s % _r, _c)
     SCRATCH["dg%d" % _r] = ("dram", [5, 128, 4], "float32")
-for _n, _c in (("uo", 64), ("rk", 4), ("tb", 4), ("tab5", 4), ("tab7", 32), ("own6", 4), ("own7", 4), ("off", 32), ("pos", 32),
+for _n, _c in (("uo", 64), ("rk", 4), ("tb", 4), ("tbl4", 4), ("tab7", 16), ("own6", 4), ("off", 32), ("pos", 32),
                ("tbl0", 4), ("tbl1", 4), ("tbl2", 4), ("tbl3", 4)):
     _part(_n, _c, "ar16")
 _buf("ar", _used["ar"])
 _buf("ar16", _used["ar16"], "uint16")
+_buf("arb", _used["arb"], "bfloat16")
 _buf("row", 512)
 _buf("yy", 512)
 for _g in range(8):
@@ -55,13 +63,13 @@ for _g in range(8):
 for _b in range(4):
     _buf("fh%d" % _b, 512)
     _buf("pa%d" % _b, 256)
-    _buf("pp%d" % _b, 256)
+    _buf("pp%d" % _b, 512)
 for _b in range(2):
     _buf("f%d" % _b, 512)
-    _buf("gp%d" % (_b + 2), 512)
+    _buf("fs%d" % (_b + 2), 512)
 for _n, _c in (("pi", 1), ("bi", 16), ("uoi", 64), ("tbi", 4)):
     _buf(_n, _c, "int32")
-for _n, _c in (("xt", 2048), ("ut", 512), ("vt", 512), ("zt", 1024), ("ee", 2048), ("ones", 512)):
+for _n, _c in (("xt", 2048), ("ut", 512), ("vt", 512), ("zt", 1024), ("ee0", 514), ("ee1", 514), ("ones", 520)):
     _buf(_n, _c, "bfloat16")
 for _n, _c in (("xq", 512), ("uq", 128), ("uc", 1024), ("vq", 128), ("wq", 512), ("zq", 256), ("eq", 512)) + tuple(("zl%d" % r, 256) for r in range(R)):
     _buf(_n, _c, "float8_e4m3fn_x4")
@@ -69,8 +77,9 @@ for _n, _c in (("xq", 512), ("uq", 128), ("uc", 1024), ("vq", 128), ("wq", 512),
 for _b in range(8):
     _buf("b%d" % _b, 512, "float32", "psum")
 for _r in range(R):
-    SEMAPHORES += [s % _r for s in ("ac%d", "as%d", "lc%d", "ls%d", "dl%d", "dm%d", "dn%d", "db%d")]
+    SEMAPHORES += [s % _r for s in ("aa%d", "ab%d", "lc%d", "dl%d", "dm%d", "dn%d", "db%d")]
     SEMAPHORES += ["dga%d%d" % (_r, g) for g in range(5)]
+PIECES = ((0, 256), (256, 384), (384, 512))
 
 
 def rank_program(g, core, T, topo):
@@ -100,6 +109,9 @@ def rank_program(g, core, T, topo):
     def quad(name, c0, c1, a):
         return v(name, c0, c1, 1, 32 * a, 32 * a + 32)
 
+    def hf(name, c0, c1, a, st=1):
+        return v(name, c0, c1, st, 64 * a, 64 * a + 64)
+
     def deps(q, ins, outs):
         toks = {}
         for w, views in ((0, ins), (1, outs)):
@@ -127,6 +139,8 @@ def rank_program(g, core, T, topo):
         count[q] += 1
         i.then_inc(T.sem[semof[q]], 1)
         note(q, (semof[q], count[q]), ins, outs)
+        if q == "v" and len({a[1] // 32 for a in ins}) > 1:
+            need(q, (semof[q], count[q]))
 
     def dma(q, sem, group, out, in_):
         out, in_ = [a if len(a) > 6 else a + (1,) for a in (out, in_)]
@@ -135,8 +149,8 @@ def rank_program(g, core, T, topo):
         total[sem] = 16 * group
         note(q, (sem, 16 * group), [in_], [out])
 
-    def cd(name):
-        n, p0, p1, a, b, ap, st = v(name)
+    def cd(name, c0=0, c1=None):
+        n, p0, p1, a, b, ap, st = v(name, c0, c1)
         return (n, p0, p1, a, b, ap.bitcast(dt.uint8), 1)
 
     def ts(out, in0, s1, op0, s2=None, op1=None):
@@ -147,11 +161,11 @@ def rank_program(g, core, T, topo):
         else:
             op("v", lambda e: e.tensor_scalar(out[5], in0[5], a, b, op0, op1), [out], ins)
 
-    def tt(out, a, b, o):
+    def tt(out, a, b, o=OP.add):
         op("v", lambda e: e.tensor_tensor(out[5], a[5], b[5], o), [out], [a, b])
 
-    def ttg(out, win, off, b):
-        op("v", lambda e: e.tensor_tensor(out[5], win[5].indirect(off[5]), b[5], OP.add), [out], [win, off, b])
+    def ttg(out, win, off, b, o=OP.add):
+        op("v", lambda e: e.tensor_tensor(out[5], win[5].indirect(off[5]), b[5], o), [out], [win, off, b])
 
     def scan(out, d0, d1, init, o0, o1):
         op("v", lambda e: e.tensor_tensor_scan(out[5], d0[5], d1[5], init, o0, o1), [out], [d0, d1])
@@ -174,8 +188,13 @@ def rank_program(g, core, T, topo):
     def act(out, in_, scale=1.0):
         op("s", lambda e: e.activation(out[5], in_[5], AF.Copy, scale=scale), [out], [in_])
 
-    def sgather(out, win, off):
-        op("s", lambda e: e.activation(out[5], win[5].indirect(off[5]), AF.Copy), [out], [win, off])
+    def lin(out, in_, scale, bias, func=AF.Identity):
+        col = isinstance(bias, tuple)
+        op("s", lambda e: e.activation(out[5], in_[5], func, bias=bias[5] if col else bias, scale=scale), [out], [in_] + ([bias] if col else []))
+
+    def sgather(out, win, off, scale=None):
+        more = {} if scale is None else {"scale": scale}
+        op("s", lambda e: e.activation(out[5], win[5].indirect(off[5]), AF.Copy, **more), [out], [win, off])
 
     def accum(out, in_, acc):
         op("s", lambda e: e.activation(out[5], in_[5], AF.Copy, accum_out=acc[5]), [out, acc], [in_])
@@ -192,11 +211,14 @@ def rank_program(g, core, T, topo):
         else:
             op("g", lambda e: e.iota(out[5], pat, base, cm, allow_small_or_imprecise_dtypes=True), [out], [])
 
-    def select(out, in_, pat, fill_, base, cm):
-        op("g", lambda e: e.affine_select(out[5], in_[5], pat, OP.is_equal, fill_, base, cm), [out], [in_])
+    def select(out, in_, pat, fill_, base=0, cm=0, cmp=OP.is_equal):
+        op("g", lambda e: e.affine_select(out[5], in_[5], pat, cmp, fill_, base, cm), [out], [in_])
 
     def group_of(B):
-        return 2 * (B % 4) + B // 4
+        return 4 * (B % 2) + 2 * (B // 2 % 2) + B // 4
+
+    def slot(j):
+        return j + 8 if 8 <= j < 16 else j - 8 if 16 <= j < 24 else j
 
     dma("y", "du", 1, v("ut"), ("u", 0, 128, 0, 512, T.u[:, :]))
     dma("s", "dx0", 1, v("xt", 0, 1024), ("x", 0, 128, 0, 1024, T.x[:, 0:1024]))
@@ -208,28 +230,6 @@ def rank_program(g, core, T, topo):
     dma("y", "dw", 2, cd("wq"), ("wc", 0, 128, 0, 2048, T.wc[:, :]))
     dma("y", "dw", 2, v("wqs"), ("ws", 0, 128, 0, 512, T.ws[:, :]))
 
-    iota(v("pi"), [[0, 1]], 0, 1)
-    iota(v("n16", 0, 64), [[0, 4], [1, 16]])
-    iota(v("io4"), [[16, 4]])
-    iota(v("i17"), [[0, 4], [1, 17]])
-    iota(v("uoi"), [[16, 8], [0, 8]])
-    iota(v("iot"), [[1, 512]])
-    fill(v("ones"), 1.0)
-    for b in range(4):
-        select(v("ee", 512 * b, 512 * b + 512), v("ones"), [[-1, 512]], 0.0, b, 4)
-    iota(v("n16", 64, 512), [[0, 28], [1, 16]])
-    iota(v("ap6"), [[0, 32]])
-    for r in range(R):
-        select(v("w5s%d" % r), v("iot", 0, 128), [[0, 128]], BIG, -1, 0)
-        for n, c in (("w5%d", 128), ("w6%d", 256), ("w7%d", 512), ("list%d", 32)):
-            iota(v(n % r), [[0, c]])
-    iota(v("iotm"), [[0, 2], [1, 256]])
-
-    def upick(a, b):
-        o, w, f = v("uc", 128 * a, 128 * b), v("uq"), v("uo", 8 * a, 8 * b)
-        op("v", lambda e: e.tensor_copy(o[5].bitcast(dt.uint32), w[5].bitcast(dt.uint32).indirect(f[5])), [o], [w, f])
-        sgather(v("ucs", 128 * a, 128 * b), v("uqs"), f)
-
     col = [0]
 
     def newcol():
@@ -239,169 +239,214 @@ def rank_program(g, core, T, topo):
     def dscp(a, b):
         return v("sgk", 0, 1, 1, a, b)
 
+    def starts(k):
+        select(v("rst%d" % k), v("big", 0, 64), [[0, 64 // WID[k]], [1, WID[k]]], -BIG)
+
+    def counts(k):
+        s = WID[k] + 2
+        pat = [[32, 2], [0, 2]] if k == 3 else [[0, 2], [16, 2]] if k == 4 else [[16, 4]]
+        for c in (s - 2, s - 1) if k < 7 else (s - 2,):
+            iota(v("c%d" % k, c, 4 * s, s), pat)
+        if k < 7:
+            select(v("msk%d" % k), v("ones", 0, 4 * s), [[0, 4], [1, s]], 0.0, cmp=OP.not_equal)
+
+    def windows(r):
+        select(v("w5s%d" % r), v("big"), [[0, 128]], BIG)
+        for n, c in (("w5%d", 128), ("list%d", 32), ("w6%d", 256), ("w7%d", 512)):
+            iota(v(n % r), [[0, c]])
+
+    iota(v("pi"), [[0, 1]], 0, 1)
+    fill(v("big"), BIG)
+    fill(v("ones"), 1.0)
+    iota(v("n16"), [[0, 4], [1, 16]])
+    iota(v("io4"), [[16, 4]])
+    iota(v("i17"), [[0, 4], [1, 17]])
+    iota(v("uoi"), [[16, 8], [0, 8]])
+    starts(0)
+    starts(3)
+    iota(v("iot"), [[1, 512]])
+    starts(1)
+    starts(2)
+    for b in range(2):
+        select(v("ee%d" % b), v("ones", 0, 514), [[-1, 514]], 0.0, 2 + b, 4)
+    counts(3)
+    starts(4)
+    counts(4)
+    counts(5)
+    windows(0)
+    counts(6)
+    counts(7)
+    windows(1)
+    windows(2)
+
     q = v("bff", 0, 1)
-    dsc, q1, e6, e7 = newcol(), newcol(), newcol(), newcol()
-    bit, th, rs0, rs, rw = {}, {}, {}, {}, {}
-    for k, c in ((0, 1), (1, 2), (2, 3), (5, 4), (6, 5), (7, 6)):
-        bit[k], th[k] = v("bff", c, c + 1), newcol()
+    dsc, q1, nq2, bq, bm, e6, e7, e7c = [newcol() for _ in range(8)]
+    bit = {k: v("bff", c, c + 1) for k, c in ((0, 1), (1, 2), (2, 3), (6, 4), (5, 5), (7, 6))}
+    th = {k: newcol() for k in bit}
     lo = {0: v("bff", 7, 8), 1: v("bff", 8, 9), 2: bit[2]}
-    for k in range(3):
-        rs0[k], rs[k], rw[k] = newcol(), newcol(), newcol()
-    spare = []
+    for j, m in enumerate((15, 14, 12, 2, 4, 8, 32, 64, 16)):
+        c = (0, 7, 8, 1, 2, 3, 4, 5, 6)[j]
+        ts(v("bi", c, c + 1), v("pi"), m, OP.bitwise_and)
+    copy(v("bff", 0, 9), v("bi", 0, 9))
+    copy(v("uo"), v("uoi"))
+    ts(v("rtab"), v("io4"), q, OP.add)
+    ts(q1, q, 1.0, OP.add)
+    ts(dsc, q, 15.0, OP.is_equal, 1.0 - 1.0 / DIG, OP.mult)
+    ts(v("md", 0, 64), v("n16"), q, OP.is_gt)
+    ts(v("mda"), v("n16"), q1, OP.is_equal, DIG - 1.0, OP.mult)
+    ts(dsc, dsc, 1.0 / DIG, OP.add)
+    cols = {k: [newcol() for _ in range(5)] for k in range(3)}
 
-    def later(f, *a):
-        spare.append((f, a))
+    def ends():
+        for k in range(2):
+            lin(cols[k][2], lo[k + 1], 2.0, 2.0 * WID[k])
+        lin(cols[2][3], lo[2], -1.0, 2.0 * WID[2])
+        for k in range(2):
+            lin(cols[k][3], lo[k], -1.0, cols[k][2])
 
-    def fit(n):
-        for f, a in spare[:n]:
-            f(*a)
-        del spare[:n]
+    def partner(k):
+        rw = cols[k][3]
+        ts(v("ms%d" % k), v("i17"), rw, OP.subtract, -float(WID[k]), OP.not_equal)
+        ts(v("t3%d" % k), v("i17"), rw, OP.is_equal, SEP - 1.0, OP.mult)
 
     def masks(k):
-        m, t, s, u = "mq%d" % k, "t1%d" % k, "ms%d" % k, "t3%d" % k
-        later(ts, rs0[k], bit[k], -2.0, OP.mult, lo[k], OP.add)
-        later(ts, v(t), v("n16", 0, 64), lo[k], OP.is_ge)
-        later(ts, v("c%d" % k, 16, 68, 17), v("rtab"), bit[k], OP.subtract, SEP, OP.mult)
-        later(fill, v("rst%d" % k), -BIG)
-        later(ts, rs[k], rs0[k], float(WID[k]), OP.add)
-        later(ts, rw[k], rs0[k], 2.0 * WID[k], OP.add)
-        later(tt, v(m), v(t), v("t2"), OP.mult)
-        later(fill, v("rst%d" % k, 0, 64, WID[k]), BIG)
-        later(ts, v(s), v("i17"), rs[k], OP.not_equal)
-        later(ts, v(u), v("i17"), rw[k], OP.is_equal, SEP - 1.0, OP.mult)
-        later(ts, v(m), v(m), BIG, OP.add)
-        later(tt, v(s), v(s), v(u), OP.add)
-        later(fill, v(s, 0, 68, 17), 0.0)
+        nm, hb, d2, rw, nb = cols[k]
+        m = MASK[k]
+        lin(nm, lo[k], -0.5, nq2)
+        lin(hb, lo[k], BIG / 2, bq)
+        lin(nb, bit[k], -SEP, 0.0)
+        lin(th[k], bit[k], -EPS / m, 0.0)
+        lin(v("t1%d" % k), v("n16"), 1.0, nm, AF.Abs)
+        lin(v("c%d" % k, 16, 68, 17), v("rtab"), SEP, nb)
+        lin(v("mq%d" % k), v("t1%d" % k), BIG, hb)
 
-    def masks3():
-        later(fill, v("msk3"), 1.0)
-        later(ts, v("mh"), v("n16", 0, 64), q, OP.is_equal, -2 * BIG, OP.mult)
-        later(copy, v("c3", 16, 68, 34), v("rtab", 0, 4, 2))
-        later(ts, v("c3", 33, 68, 34), v("rtab", 1, 4, 2), -16.0, OP.add)
-        later(fill, v("msk3", 0, 68, 17), 0.0)
-        later(ts, v("mh"), v("mh"), BIG, OP.add)
-
-    def masks4():
-        later(fill, v("rst4"), -BIG)
-        later(fill, v("msk4"), 1.0)
-        later(copy, v("c4", 32, 66, 33), v("rtab", 0, 2))
-        later(ts, v("c4", 98, 132, 33), v("rtab", 2, 4), -32.0, OP.add)
-        later(fill, v("rst4", 0, 64, 32), BIG)
-        later(fill, v("msk4", 0, 132, 33), 0.0)
-
-    def places(a, b):
-        for c in range(a, b, 64):
-            later(ts, v("mda", c, c + 64), v("n16", c, c + 64), q1, OP.is_equal, DIG - 1.0, OP.mult)
-            later(ts, v("md", c, c + 64), v("n16", c, c + 64), q, OP.is_gt)
-        for c in range(a, b, 64):
-            later(tt, v("md", c, c + 64), v("md", c, c + 64), v("mda", c, c + 64), OP.add)
-
-    def masks5():
-        later(fill, v("msk5"), 1.0)
-        later(copy, v("c5", 64, 260, 65), v("rtab"))
-        later(ts, e6, bit[5], 2.0, OP.mult)
-        later(fill, v("msk5", 0, 260, 65), 0.0)
-        later(ts, e7, bit[6], 2.0, OP.mult, e6, OP.add)
-        later(ts, v("c6", 128, 516, 129), v("rtab"), e6, OP.add)
-        later(ts, v("c7", 256, 1028, 257), v("rtab"), e7, OP.add)
-        places(64, 128)
-
-    def units(k):
-        o, i = 128 * k, 512 * k
-        later(quant, v("eq", o, o + 128), v("eqs", o, o + 128), v("ee", i, i + 512))
-
-    for j, m in enumerate((15, 2, 4, 8, 32, 64, 16, 14, 12)):
-        ts(v("bi", j, j + 1), v("pi"), m, OP.bitwise_and)
-    fill(v("rst3"), -BIG)
-    copy(v("bff", 0, 9), v("bi", 0, 9))
-    fill(v("rst3", 0, 64, 16), BIG)
-    copy(v("uo"), v("uoi"))
-    ts(dsc, q, 15.0, OP.is_equal, 1.0 - 1.0 / DIG, OP.mult)
-    ts(q1, q, 1.0, OP.add)
-    ts(v("rtab"), v("io4"), q, OP.add)
-    ts(v("t2"), v("n16", 0, 64), q, OP.is_le, -2 * BIG, OP.mult)
-    ts(v("md", 0, 64), v("n16", 0, 64), q, OP.is_gt)
-    for k, m in ((0, 2), (1, 4), (2, 8), (5, 32), (6, 64), (7, 16)):
-        ts(th[k], bit[k], -EPS / m, OP.mult)
-    ts(dsc, dsc, 1.0 / DIG, OP.add)
-    ts(v("mda", 0, 64), v("n16", 0, 64), q1, OP.is_equal, DIG - 1.0, OP.mult)
+    MASK = {0: 2, 1: 4, 2: 8, 5: 64, 6: 32, 7: 16}
+    ends()
+    lin(nq2, q, -0.5, 0.0)
+    lin(bq, q, -BIG / 2, -BIG / 4)
+    ts(e6, bit[5], q, OP.add)
+    tt(v("md", 0, 64), v("md", 0, 64), v("mda"))
+    ts(e7, bit[6], 4.0, OP.mult, e6, OP.add)
+    for k in range(3):
+        partner(k)
+    ts(e7c, e7, 48.0, OP.add)
+    for k in range(3):
+        tt(v("ms%d" % k), v("ms%d" % k), v("t3%d" % k))
     masks(0)
-    fit(99)
-    tt(v("md", 0, 64), v("md", 0, 64), v("mda", 0, 64), OP.add)
-    quant(v("uq"), v("uqs"), v("ut"))
-    upick(0, 1)
     masks(1)
 
-    def compact(c1, p0=0, p1=128):
-        return v("ds", 15, c1, 16, p0, p1)
+    def upick(a, b):
+        o, w, f = v("uc", 128 * a, 128 * b), v("uq"), v("uo", 8 * a, 8 * b)
+        op("v", lambda e: e.tensor_copy(o[5].bitcast(dt.uint32), w[5].bitcast(dt.uint32).indirect(f[5])), [o], [w, f])
+        sgather(v("ucs", 128 * a, 128 * b), v("uqs"), f)
+
+    def units(b):
+        c = 2 - 2 * (b // 2)
+        quant(v("eq", 128 * b, 128 * b + 128), v("eqs", 128 * b, 128 * b + 128), v("ee%d" % (b % 2), c, c + 512))
+
+    quant(v("uq"), v("uqs"), v("ut"))
+    upick(0, 1)
+    upick(1, 4)
+    masks(2)
+    lin(bm, q, -BIG, -BIG / 2)
+    for k in (5, 6, 7):
+        lin(th[k], bit[k], -EPS / MASK[k], 0.0)
+    lin(v("mh"), v("n16"), BIG, bm)
+    upick(4, 6)
+
+    def compact(name, c0, c1, p0=0, p1=128):
+        return v(name, c0 + 15, c1, 16, p0, p1)
+
+    def diag(out, row, c0, c1):
+        scan(out, v("md", 0, c1 - c0), v(row, c0, c1), 0.0, OP.mult, OP.add)
+
+    def runmin(out, a, b=None):
+        scan(out, a, b or a, BIG, OP.min, OP.min)
+
+    def hold(out, m, row):
+        scan(out, m, row, BIG, OP.min, OP.max)
+
+    def quantx(i):
+        a, b = PIECES[i]
+        quant(v("xq", a, b), v("xqs", a, b), v("xt", 4 * a, 4 * b))
 
     for r in range(R):
         lst = "list%d" % r
         dg = T["dg%d" % r]
-        if r == 0:
-            copy(v("tb"), v("tbi"))
-        else:
-            ts(v("tb"), v("tbf"), dsc, OP.mult)
-        quant(v("xq", 0, 256), v("xqs", 0, 256), v("xt", 0, 1024))
-        quant(v("xq", 256, 512), v("xqs", 256, 512), v("xt", 1024, 2048))
-        sgather(v("id0r"), v("iot"), v("tb"))
 
         def score(k, bank, c0=0, c1=512):
             mm(v(bank, 0, c1 - c0), v("uc", 128 * k, 128 * k + 128), v("ucs", 128 * k, 128 * k + 128), v("xq", c0, c1), v("xqs", c0, c1))
 
-        def scored(k, bank):
-            act(v("sw%d" % k), v(bank), -1.0)
+        def sbank(k):
+            return "b%d" % ((k + 6) % 8)
+
+        def scored(k):
+            act(v("sw%d" % k), v(sbank(k)), -1.0)
 
         def unpack(b):
-            mm(v("b%d" % b), v("eq", 128 * b, 128 * b + 128), v("eqs", 128 * b, 128 * b + 128), v("xq"), v("xqs"))
+            mm(v(sbank(b)), v("eq", 128 * b, 128 * b + 128), v("eqs", 128 * b, 128 * b + 128), v("xq"), v("xqs"))
 
         def half(b):
-            act(v("fh%d" % b), v("b%d" % b), 0.5)
+            act(v("fh%d" % b), v(sbank(b)), 0.5)
 
-        score(0, "b4", 0, 256)
-        score(0, "b5", 256, 512)
+        def whole(b):
+            act(v("f%d" % b), v(sbank(b)))
+
+        for i, (a, b) in enumerate(PIECES):
+            quantx(i)
+            score(0, "b%d" % (4 + i), a, b)
         if r == 0:
-            upick(1, 4)
-        ts(v("sw0", 0, 256), v("b4", 0, 256), -1.0, OP.mult)
-        act(v("sw0", 256, 512), v("b5", 0, 256), -1.0)
-        fit(3)
+            copy(v("tb"), v("tbi"))
+            upick(6, 7)
+        act(v("sw0", 0, 256), v("b4", 0, 256), -1.0)
+        ts(v("sw0", 256, 384), v("b5", 0, 128), -1.0, OP.mult)
+        ts(v("sw0", 384, 512), v("b6", 0, 128), -1.0, OP.mult)
+        for k in range(1, 6):
+            score(k, sbank(k))
+        scored(1)
+        if r == 0:
+            sgather(v("id0r"), v("iot"), v("tb"))
+        ttg(v("gm"), v("sw0"), v("tb"), v("mq0"), OP.max)
         vgather(v("g0"), v("sw0"), v("tb"))
-        fit(3)
-        score(1, "b6")
-        scored(1, "b6")
         sgather(v("o1"), v("sw1"), v("tb"))
+        scored(2)
+        if r == 0:
+            act(v("md", 64, 128), v("md", 0, 64))
+            act(v("md", 128, 256), v("md", 0, 128))
 
-        def tail(k, part):
-            dst = "idw" if k == 4 else "id%dr" % (k + 1)
-            if part == 0:
-                scatter(v(dst), v("rk"), v("id%dr" % k))
-            elif part == 1:
-                scan(v("ds", 0, 64), v("md", 0, 64), v(dst), 0.0, OP.mult, OP.add)
-            else:
-                tab = "tab5" if k == 4 else "tbl%d" % k
-                ts(v(tab), compact(64), dsc, OP.mult)
-                sgather(v("o%d" % (k + 2)), v("sw%d" % (k + 2)), v(tab))
-                act(v("lr", 4 * k, 4 * k + 4), compact(64))
-                dma("y", "dga%d%d" % (r, k), 1, ("dg%d" % r, 0, 128, k, k + 1, dg[k]), v("lr", 4 * k, 4 * k + 4))
+        def ids(k):
+            return "idw" if k == 5 else "id%dr" % k
+
+        def table(k):
+            tab = "tbl%d" % k
+            ts(v(tab), compact("ds", 0, 64), dsc, OP.mult)
+            sgather(v("o%d" % (k + 2)), v("sw%d" % (k + 2)), v(tab))
+            act(v("lr", 4 * k, 4 * k + 4), compact("ds", 0, 64))
+            dma("y", "dga%d%d" % (r, k), 1, ("dg%d" % r, 0, 128, k, k + 1, dg[k]), v("lr", 4 * k, 4 * k + 4))
+
+        def place(k, add):
+            s = WID[k] + 2
+            scan(v("smb", 0, 4 * s), v("msk%d" % k), v("c%d" % k), 0.0, OP.mult, OP.add)
+            ts(v("rk"), v("smb", s - 2, 4 * s, s), add, OP.add)
 
         for k in range(5):
             w = WID[k]
             G = v("g%d" % k)
             C = "c%d" % k
-            if k < 3:
+            if 0 < k < 3:
                 tt(v("gm"), G, v("mq%d" % k), OP.max)
-                scan(v("kk"), v("rst%d" % k), G, BIG, OP.max, OP.min)
-                if k:
-                    tail(k - 1, 0)
+            if k == 0:
                 scan(v("kd"), v("rst3"), v("gm"), BIG, OP.max, OP.min)
-            else:
-                scan(v("kk"), v("rst%d" % k), G, BIG, OP.max, OP.min)
-                tail(k - 1, 0)
-                scan(v("kd"), v("mh"), v("kk"), BIG, OP.min, OP.max)
+            scan(v("kk"), v("rst%d" % k), G, BIG, OP.max, OP.min)
             if k:
-                tail(k - 1, 1)
-            fit(3)
-            s = 17 if k < 3 else w + 1
+                diag(v("ds"), ids(k), 0, 64)
+            if 0 < k < 3:
+                scan(v("kd"), v("rst3"), v("gm"), BIG, OP.max, OP.min)
+            elif k:
+                hold(v("kd"), v("mh"), v("kk"))
+            if k:
+                table(k - 1)
+            s = 17 if k < 3 else w + 2
             for c in range(4):
                 x = v("kd", 16 * c + 15, 16 * c + 16)
                 if k < 3:
@@ -410,234 +455,194 @@ def rank_program(g, core, T, topo):
                     left = c % 2 == 0 if k == 3 else c < 2
                     a = 16 * (c ^ 1) if k == 3 else 32 * left
                     ts(v(C, s * c, s * c + w), v("kk", a, a + w), x, OP.is_gt if left else OP.is_ge)
-            if k:
-                tail(k - 1, 2)
-            scan(v("sm", 0, 4 * s), v(("ms%d" if k < 3 else "msk%d") % k), v(C), 0.0, OP.mult, OP.add)
-            fit(4)
+            if r == 0 and k == 1:
+                upick(7, 8)
+            if r == 0 and k in (2, 3):
+                units(2 * k - 4)
             if k < 3:
+                scan(v("sm"), v("ms%d" % k), v(C), 0.0, OP.mult, OP.add)
+                if r == 0 and k == 2:
+                    units(1)
                 ts(v("rk"), v("sm", 16, 68, 17), 1.0 / SEP, OP.mult)
             else:
-                copy(v("rk"), v("sm", w, 4 * s, s))
-            fit(4)
+                place(k, q)
+            if r == 0 and k == 3:
+                units(3)
             scatter(v("g%d" % (k + 1)), v("rk"), v("o%d" % (k + 1)))
-            fit(99)
-            if r == 0:
-                if k == 0:
-                    score(2, "b7")
-                    score(3, "b4")
-                    scored(2, "b7")
-                    scored(3, "b4")
-                    masks(2)
-                    later(upick, 4, 5)
-                    masks3()
-                elif k == 1:
-                    score(4, "b5")
-                    scored(4, "b5")
-                    later(upick, 5, 6)
-                    masks4()
-                    units(0)
-                    units(1)
-                elif k == 2:
-                    score(5, "b6")
-                    scored(5, "b6")
-                    unpack(0)
-                    later(upick, 6, 8)
-                    units(2)
-                    units(3)
-                elif k == 3:
-                    score(6, "b7")
-                    scored(6, "b7")
-                    score(7, "b4")
-                    for b in range(1, 4):
-                        unpack(b)
-                    masks5()
-                else:
-                    scored(7, "b4")
-                    half(0)
-            elif k == 0:
-                score(2, "b7")
-                scored(2, "b7")
-                score(3, "b4")
-                for b in range(4):
-                    unpack(b)
-                    if b < 3:
-                        score(b + 4, "b%d" % (b + 5))
-                scored(3, "b4")
-                score(7, "b4")
-                half(0)
-            elif k < 3:
-                scored(k + 3, "b%d" % (k + 4))
-                half(k)
+            scatter(v(ids(k + 1)), v("rk"), v(ids(k)))
+            if k == 0:
+                score(6, sbank(6))
+                scored(3)
+            elif k == 1:
+                score(7, sbank(7))
+                scored(4)
+                scored(5)
+            elif k == 2:
+                unpack(0)
+                unpack(1)
+                scored(6)
+                scored(7)
             elif k == 3:
-                scored(6, "b7")
-                scored(7, "b4")
+                unpack(2)
+                unpack(3)
+                half(0)
+                whole(0)
 
-        def runmin(out, a, b=None):
-            scan(out, a, b or a, BIG, OP.min, OP.min)
+        def versus(k, c):
+            w = WID[k]
+            s = w + 2
+            ts(v("c%d" % k, s * c, s * c + w), v("np%d" % k), v("hh%d" % k, 16 * c + 15, 16 * c + 16), OP.subtract, th[k], OP.is_gt)
 
-        def hold(w):
-            if w == 64:
-                scan(v("hh"), v("mh"), v("no", 0, 64), BIG, OP.min, OP.max)
-            else:
-                for a in range(4):
-                    c = 64 * (a % (w // 64))
-                    scan(quad("hh", 0, 64, a), quad("mh", 0, 64, a), quad("no", c, c + 64, a), BIG, OP.min, OP.max)
-
-        def versus(k, w, c):
-            s = w + 1
-            ts(v("c%d" % k, s * c, s * c + w), v("np", 0, w), v("hh", 16 * c + 15, 16 * c + 16), OP.subtract, th[k], OP.is_gt)
-            if k > 5:
-                accum(v("jk", s * c, s * c + s), v("c%d" % k, s * c, s * c + s), v("sum4", c, c + 1))
-
-        def swap1(out, in_, n, src=quad):
-            for a in range(4):
-                o, i = quad(out, 0, n, a), src(in_, 0, n, a ^ 1)
-                if a < 2:
-                    copy(o, i)
-                else:
-                    act(o, i)
-
-        def dsq(_n, c0, n, a):
-            return compact(16 * n, 32 * a, 32 * a + 32)
-
-        def swap2(out, in_, n):
-            copy(v(out, 0, n, 1, 0, 64), v(in_, 0, n, 1, 64, 128))
-            act(v(out, 0, n, 1, 64, 128), v(in_, 0, n, 1, 0, 64))
-
-        def owns(name, src, per):
-            for a in range(4):
-                c = 4 * (a % per)
-                ts(quad(name, 0, 4, a), quad(src, c, c + 4, a), dscp(32 * a, 32 * a + 32), OP.mult)
-
-        runmin(v("no", 0, 64), v("g5"))
-        tail(4, 0)
-        swap1("np", "no", 64)
-        hold(64)
-        tail(4, 1)
+        runmin(v("no5"), v("g5"))
+        diag(v("ds"), "idw", 0, 64)
+        act(hf("np5", 0, 64, 1), hf("no5", 0, 64, 0))
+        copy(hf("np5", 0, 64, 0), hf("no5", 0, 64, 1))
+        hold(v("hh5"), v("mh"), v("no5"))
+        table(4)
         for c in range(4):
-            versus(5, 64, c)
-        tail(4, 2)
-        fit(99)
-        if r == 0:
-            places(128, 512)
-            later(quant, v("vq"), v("vqs"), v("vt"))
-        scan(v("sm"), v("msk5"), v("c5"), 0.0, OP.mult, OP.add)
-        copy(v("rk"), v("sm", 64, 260, 65))
-        fit(3)
+            versus(5, c)
+        half(1)
+        place(5, q)
         scatter(v("w5s%d" % r), v("rk"), v("o6"))
-        swap1("shs", "w5s%d" % r, 128)
         scatter(v("w5%d" % r), v("rk"), v("idw"))
-        runmin(v("no", 0, 128), v("w5s%d" % r), v("shs"))
-        scan(v("ds", 0, 128), v("md", 0, 128), v("w5%d" % r), 0.0, OP.mult, OP.add)
-        swap2("np", "no", 128)
-        fit(3)
-        hold(128)
-        swap1("sh", "ds", 8, dsq)
-        versus(6, 128, 0)
-        versus(6, 128, 1)
-        tt(v("a5"), compact(128), v("sh", 0, 8), OP.add)
-        versus(6, 128, 2)
-        versus(6, 128, 3)
-        owns("own6", "a5", 2)
-        fit(8)
+        runmin(hf("no6", 0, 128, 0), hf("w5s%d" % r, 0, 128, 0), hf("w5s%d" % r, 0, 128, 1))
+        for a in (0, 1):
+            act(quad("np6", 0, 128, a), quad("no6", 0, 128, a ^ 1))
+        for a in (0, 1):
+            hold(hf("hh6", 0, 64, a), hf("mh", 0, 64, 0), hf("no6", 64 * a, 64 * a + 64, 0))
+        for a in (2, 3):
+            copy(quad("np6", 0, 128, a), quad("no6", 0, 128, 3 - a))
+        diag(v("ds6"), "w5%d" % r, 0, 128)
+        for a in (0, 1):
+            act(hf("sh5", 0, 4, a), compact("ds6", 64 * a, 64 * a + 64, 64 - 64 * a, 128 - 64 * a))
+        for c in range(3):
+            versus(6, c)
+        for a in (0, 1):
+            tt(hf("lr5", 0, 4, a), compact("ds6", 64 * a, 64 * a + 64, 64 * a, 64 * a + 64), hf("sh5", 0, 4, a))
+        versus(6, 3)
+        ts(v("own6"), v("lr5"), dsc, OP.mult)
         sgather(v("id6"), v("iot"), v("own6"))
-        ts(v("rk"), v("sum4"), 1.0, OP.mult)
-        scatter(v("w6%d" % r), v("rk"), v("id6"))
-        for B in range(4):
-            h = 16 * (4 * (B % 2) + B // 2)
-            dma("y", "dm%d" % r, 4, v(lst, 8 * B, 8 * B + 8, 1, 80, 96), v("a5", 0, 8, 1, h, h + 16))
+        whole(1)
         for B in range(8):
-            h = 16 * group_of(B)
-            dma("y", "dl%d" % r, 8, v(lst, 4 * B, 4 * B + 4, 1, 0, 80), ("dg%d" % r, h, h + 16, 0, 5, dg[0:5, h:h + 16, :]))
-        fit(99)
-        scan(v("ds", 0, 256), v("md", 0, 256), v("w6%d" % r), 0.0, OP.mult, OP.add)
-        swap1("sh", "ds", 16, dsq)
-        tt(v("ap6", 0, 16), compact(256), v("sh", 0, 16), OP.add)
-        trans(v("tr"), v("ap6"))
-        swap2("sh", "tr", 32)
-        tt(v("sw", 32, 48), v("tr", 16, 32), v("sh", 16, 32), OP.add)
-        tt(v("sw", 48, 64), v("tr", 0, 16), v("sh", 0, 16), OP.add)
-        tt(v("sw", 0, 32), v("tr"), v("sh"), OP.add)
-        trans(v("tr2"), v("sw"))
-        ts(v("tab7", 16, 32), v("tr2", 32, 48), dsc, OP.mult)
-        ts(v("tab7", 0, 16), v("tr2", 0, 16), dsc, OP.mult)
-        for j in range(2):
-            dma("y", "dn%d" % r, 2, v(lst, 16 * j, 16 * j + 16, 1, 96, 112), v("tr2", 0, 16, 1, 16 * j, 16 * j + 16))
-        sgather(v("gg", 256, 512), v("sw7"), v("tab7", 16, 32))
-        vgather(v("gg", 0, 256), v("sw7"), v("tab7", 0, 16))
-        owns("own7", "tr2", 4)
-        sgather(v("id7"), v("iot"), v("own7"))
-        runmin(v("no"), v("gg", 0, 256))
-        runmin(v("np"), v("gg", 256, 512))
-        hold(256)
+            h, c = 16 * group_of(B), slot(4 * B)
+            dma("y", "dl%d" % r, 8, v(lst, c, c + 4, 1, 0, 80), ("dg%d" % r, h, h + 16, 0, 5, dg[0:5, h:h + 16, :]))
+        for B in range(8):
+            h, c = 16 * group_of(B), slot(4 * B)
+            dma("y", "dm%d" % r, 8, v(lst, c, c + 4, 1, 80, 96), v("lr5", 0, 4, 1, h, h + 16))
+        place(6, e6)
+        scatter(v("w6%d" % r), v("rk"), v("id6"))
+        diag(v("ds7"), "w6%d" % r, 0, 256)
+        tt(hf("qa", 0, 16, 0), compact("ds7", 0, 256, 0, 64), compact("ds7", 0, 256, 64, 128))
+        tt(quad("ap6", 0, 16, 0), quad("qa", 0, 16, 0), quad("qa", 0, 16, 1))
+        for a in range(4):
+            ts(quad("tab7", 0, 16, a), quad("ap6", 0, 16, 0), dscp(0, 32), OP.mult)
+        sgather(v("gg", 128, 256), v("sw7"), v("tab7", 8, 16))
+        vgather(v("gg", 0, 128), v("sw7"), v("tab7", 0, 8))
+        for j in range(4):
+            c = slot(8 * j)
+            dma("y", "dn%d" % r, 4, v(lst, c, c + 8, 1, 96, 112), v("ap6", 8 * (j % 2), 8 * (j % 2) + 8, 1, 16 * (j // 2), 16 * (j // 2) + 16))
+        sgather(v("idg"), v("iot"), v("tab7"))
+        for a in range(4):
+            c = 64 * (2 * (a % 2) + a // 2)
+            act(quad("id7", 0, 64, a), quad("idg", c, c + 64, a))
+        half(2)
+        runmin(v("no7"), v("gg"))
+        trans(v("t7", 0, 256), v("no7"))
+        trans(v("t7", 256, 288), v("no7", 0, 32))
+        for a in range(4):
+            c = 64 * (2 * (a % 2) + a // 2)
+            hold(quad("hh7", 0, 64, a), quad("mh", 0, 64, a), quad("no7", c, c + 64, a))
+        trans(v("np7"), v("t7", 16, 272))
         for c in range(4):
-            versus(7, 256, c)
-        if r == 0:
-            half(1)
-            half(2)
+            versus(7, c)
+            if c < 3:
+                accum(v("jk", 258 * c, 258 * c + 257), v("c7", 258 * c, 258 * c + 257), v("sum4", c, c + 1))
         half(3)
-        ts(v("rk"), v("sum4"), 1.0, OP.mult)
-        scatter(v("w7%d" % r), v("rk"), v("id7"))
+        scan(v("smb", 0, 256), v("ones", 0, 256), v("c7", 774, 1030), 0.0, OP.mult, OP.add)
         ts(v("off", 0, 32, 1, 0, 96), v(lst, 0, 32, 1, 0, 96), dscp(0, 96), OP.mult)
-        trans(quad("tl", 0, 32, 3), quad(lst, 0, 32, 3))
-        scan(v("ds"), v("md"), v("w7%d" % r), 0.0, OP.mult, OP.add)
-        copy(quad("qe", 0, 16, 3), quad("tl", 0, 16, 3))
-        tt(v("qa", 0, 32, 1, 64, 128), compact(512, 64, 128), compact(512, 0, 64), OP.add)
-        tt(quad("qb", 0, 32, 3), quad("qa", 0, 32, 3), quad("qa", 0, 32, 2), OP.add)
+        ts(v("rk", 3, 4), v("smb", 255, 256), e7c, OP.add)
+        ts(v("rk", 0, 3), v("sum4", 0, 3), e7, OP.add)
+        trans(quad("qe", 0, 32, 3), quad(lst, 0, 32, 3))
+        scatter(v("w7%d" % r), v("rk"), v("id7"))
+        for j in range(4):
+            c = 16 * slot(8 * j)
+            diag(v("de", c, c + 128), "w7%d" % r, 128 * j, 128 * j + 128)
+        tt(hf("qc", 0, 32, 1), compact("de", 0, 512, 64, 128), compact("de", 0, 512, 0, 64))
+        tt(quad("qb", 0, 32, 3), quad("qc", 0, 32, 3), quad("qc", 0, 32, 2))
         trans(quad("qt", 0, 32, 3), quad("qb", 0, 32, 3))
-        tt(quad("qe", 16, 32, 3), quad("qt", 0, 16, 3), quad("qt", 16, 32, 3), OP.add)
-        trans(quad("tr7", 0, 32, 3), quad("qe", 0, 32, 3))
-        ts(quad("off", 0, 32, 3), quad("tr7", 0, 32, 3), dscp(96, 128), OP.mult)
-        for b in range(1, 4):
-            sgather(v("pa%d" % b), v("fh%d" % b), v("off", 0, 16))
-        vgather(v("pa0"), v("fh0"), v("off", 0, 16))
-        for b in (1, 0, 2, 3):
-            ttg(v("zt", b, 1024, 4), v("fh%d" % b), v("off", 16, 32), v("pa%d" % b))
-        quant(v("zq"), v("zqs"), v("zt"))
+        tt(quad("qe", 16, 32, 3), quad("qt", 0, 16, 3), quad("qt", 16, 32, 3))
+        trans(quad("tr", 0, 32, 3), quad("qe", 0, 32, 3))
+        ts(quad("off", 0, 32, 3), quad("tr", 0, 32, 3), dscp(96, 128), OP.mult)
+
         rid, pid, _s = topo.addr(nxt)
         eng = topo.engines(core, nxt)
-        for src, land, sem, loc, es in ((cd("zq"), cd("zl%d" % r), "ac%d" % r, "lc%d" % r, eng[0::2]),
-                                        (v("zqs"), v("zl%ds" % r), "as%d" % r, "ls%d" % r, eng[1::4])):
-            deps("g", [src], [])
-            g.remote_dma(land[5], src[5], T.sem[sem], T.sem[loc], pid, rid, sum(1 << e for e in es))
-            total[sem] = total[loc] = len(es)
-            note("g", (loc, len(es)), [src], [])
-            note("x", (sem, len(es)), [], [land])
+        ways = (eng[0::2], eng[1::4])
+        n_eng = len(ways[0]) + len(ways[1])
+        for j in range(2):
+            c = 128 * j
+            first, second = v("off", 16 * j, 16 * j + 8), v("off", 16 * j + 8, 16 * j + 16)
+            for b in (1, 2, 3) if j == 0 else range(4):
+                sgather(v("pa%d" % b, c, c + 128), v("fh%d" % b), first)
+            if j == 0:
+                vgather(v("pa0", c, c + 128), v("fh0"), first)
+            for b in range(4):
+                ttg(v("zt", 4 * c + b, 4 * c + 512, 4), v("fh%d" % b), second, v("pa%d" % b, c, c + 128))
+            quant(v("zq", c, c + 128), v("zqs", c, c + 128), v("zt", 4 * c, 4 * c + 512))
+            sem, loc = ("aa%d", "ab%d")[j] % r, "lc%d" % r
+            for src, land, es in ((cd("zq", c, c + 128), cd("zl%d" % r, c, c + 128), ways[0]),
+                                  (v("zqs", c, c + 128), v("zl%ds" % r, c, c + 128), ways[1])):
+                deps("g", [src], [])
+                g.remote_dma(land[5], src[5], T.sem[sem], T.sem[loc], pid, rid, sum(1 << e for e in es))
+                note("g", (loc, 2 * n_eng), [src], [])
+                note("x", (sem, n_eng), [], [land])
+            total[sem] = n_eng
+            total[loc] = 2 * n_eng
         if r < R - 1:
             for B in range(8):
-                h = 16 * group_of(B)
-                dma("y", "db%d" % r, 8, v("tbf", 0, 4, 1, h, h + 16), v("tr7", 4 * B, 4 * B + 4, 1, 112, 128))
-        act(v("f0"), v("b0"))
-        act(v("f1"), v("b1"))
-        scatter(v("posw"), v("off"), v("iotm"))
-        scan(v("pds"), v("md"), v("posw"), 0.0, OP.mult, OP.add)
-        ts(v("pos"), v("pds", 15, 512, 16), dsc, OP.mult)
-        if r == R - 1:
+                h, c = 16 * group_of(B), slot(4 * B)
+                dma("y", "db%d" % r, 8, v("tbf", 0, 4, 1, h, h + 16), v("tr", c, c + 4, 1, 112, 128))
+        scatter(v("posw"), v("off"), v("iot"))
+        for j in range(2):
+            for b in (2, 3):
+                sgather(v("fs%d" % b, 256 * j, 256 * j + 256), v("fh%d" % b), v("off", 16 * j, 16 * j + 16), 64.0)
+        for c in (0, 256):
+            diag(v("pds", c, c + 256), "posw", c, c + 256)
+        if r == 0:
+            quant(v("vq"), v("vqs"), v("vt"))
+        if r < R - 1:
+            ts(v("tb"), v("tbf"), dsc, OP.mult)
+            sgather(v("id0r"), v("iot"), v("tb"))
+        else:
             sgather(v("row"), v("iot"), v("off"))
-            dma("y", "dod", 1, ("od", 0, 8, 0, 512, T.od[:, :]), ("row", 0, 128, 0, 512, T.row[0:128:16, :]))
-        for b in (0, 2, 1, 3):
-            mm(v("b%d" % (4 + b), 0, 256), v("wq", 128 * b, 128 * b + 128), v("wqs", 128 * b, 128 * b + 128), v("zl%d" % r), v("zl%ds" % r))
-        for b in (2, 3):
-            act(v("pp%d" % b), v("b%d" % (4 + b), 0, 256), 0.03125)
+            for j in range(4):
+                c = 16 * slot(8 * j)
+                dma("y", "dod", 4, ("od", 0, 8, 128 * j, 128 * j + 128, T.od[:, 128 * j:128 * j + 128]),
+                    ("row", 0, 128, c, c + 128, T.row[0:128:16, c:c + 128]))
+        ts(v("pos"), v("pds", 15, 512, 16), dsc, OP.mult)
+        for j in range(2):
+            c = 128 * j
+            for b in (2, 0, 3, 1):
+                mm(v("b%d" % (4 * j + b), 0, 128), v("wq", 128 * b, 128 * b + 128), v("wqs", 128 * b, 128 * b + 128),
+                   v("zl%d" % r, c, c + 128), v("zl%ds" % r, c, c + 128))
+            for b in range(4):
+                for a in (2 * c, 2 * c + 128):
+                    if b < 2:
+                        act(v("pp%d" % b, a, a + 128), v("b%d" % (4 * j + b), 0, 128), 0.03125)
+                    else:
+                        tt(v("pp%d" % b, a, a + 128), v("b%d" % (4 * j + b), 0, 128), v("fs%d" % b, a, a + 128))
         for b in (0, 1):
-            ts(v("pp%d" % b), v("b%d" % (4 + b), 0, 256), 0.03125, OP.mult)
-        for b in (2, 3):
-            sgather(v("gp%d" % b), v("pp%d" % b), v("pos"))
-        for b in (0, 1):
+            sgather(v("xt", b + 2, 2048, 4), v("pp%d" % (b + 2)), v("pos"), 0.03125)
             ttg(v("xt", b, 2048, 4), v("pp%d" % b), v("pos"), v("f%d" % b))
-        for b in (2, 3):
-            for c in (0, 256):
-                tt(v("xt", 4 * c + b, 4 * c + 1024, 4), v("gp%d" % b, c, c + 256), v("b%d" % b, c, c + 256), OP.add)
 
-    for c in (0, 256):
-        quant(v("xq", c, c + 256), v("xqs", c, c + 256), v("xt", 4 * c, 4 * c + 1024))
-        mm(v("b4" if c == 0 else "b5", 0, 256), v("vq"), v("vqs"), v("xq", c, c + 256), v("xqs", c, c + 256))
-    dma("y", "doc", 1, ("oc", 0, 128, 0, 2048, T.oc[:, :]), cd("xq"))
+    for i, (a, b) in enumerate(PIECES):
+        quantx(i)
+        mm(v("b%d" % (4 + i), 0, b - a), v("vq"), v("vqs"), v("xq", a, b), v("xqs", a, b))
+        dma("y", "doc", 3, ("oc", 0, 128, 4 * a, 4 * b, T.oc[:, 4 * a:4 * b]), cd("xq", a, b))
+    for i, (a, b) in enumerate(PIECES):
+        (copy if i else act)(v("yy", a, b), v("b%d" % (4 + i), 0, b - a))
+        dma("y", "dy", 3, ("y", 0, 128, a, b, T.y[:, a:b]), v("yy", a, b))
     for k in range(4):
-        dma("y", "dos", 4, ("osc", 4 * k, 4 * k + 4, 0, 512, T.osc[4 * k:4 * k + 4, :]), v("xqs", 0, 512, 1, 32 * k, 32 * k + 4))
-    copy(v("yy", 0, 256), v("b4", 0, 256))
-    act(v("yy", 256, 512), v("b5", 0, 256))
-    dma("y", "dy", 1, ("y", 0, 128, 0, 512, T.y[:, :]), v("yy"))
+        dma("s", "dos", 4, ("osc", 4 * k, 4 * k + 4, 0, 512, T.osc[4 * k:4 * k + 4, :]), v("xqs", 0, 512, 1, 32 * k, 32 * k + 4))
     for k in semof:
         need("g", (semof[k], count[k]))
     for s in total:

@@ -23,19 +23,18 @@ def _part(name, cols, arena="ar"):
     _used[arena] += -(-cols // 16) * 16
 
 
-for _n, _c in (("n16", 64), ("i17", 68), ("iot", 512), ("io4", 4), ("bff", 16), ("sgk", 48), ("rtab", 4), ("big", 128),
-               ("mh", 64), ("md", 256), ("mda", 64), ("c0", 68), ("c1", 68), ("c2", 68),
-               ("kk", 64), ("gm", 64), ("kd", 64), ("sm", 68), ("g5", 64), ("o5", 64), ("o6", 64), ("idw", 64),
-               ("no5", 64), ("np5", 64), ("hh5", 64), ("no6", 128), ("np6", 128), ("hh6", 64), ("id6", 64), ("lr5", 4),
-               ("qa", 16), ("ap6", 16), ("gg", 256), ("no7", 256), ("t7", 288), ("np7", 256), ("hh7", 64), ("idg", 256), ("id7", 64),
-               ("jk", 774), ("sum4", 4), ("ds", 64), ("ds6", 128), ("ds7", 256),
+for _n, _c in (("n16", 64), ("i17", 68), ("iot", 512), ("io4", 4), ("bff", 16), ("sgk", 48), ("rtab", 4), ("big", 256),
+               ("mh", 64), ("md", 256), ("mda", 64), ("c0", 68), ("c1", 68), ("c2", 68), ("n32", 64), ("iom", 512),
+               ("mk16", 64), ("mk32", 64), ("mk64", 64), ("ke", 160),
+               ("kk", 64), ("gm", 64), ("kd", 64), ("sm", 68), ("g5", 64), ("o5", 64), ("o6", 64), ("o7", 64), ("idw", 64),
+               ("np5", 64), ("no6", 128), ("np6", 128), ("hh6", 64), ("id6", 64), ("lr5", 4), ("sh5", 4),
+               ("qa", 16), ("ap6", 16), ("sa", 16), ("sb", 16), ("nh7", 256), ("no7", 256), ("t7", 288), ("np7", 256), ("hh7", 64),
+               ("jk", 774), ("sum4", 4), ("ds", 64), ("ds6", 128), ("ds7", 256), ("qh", 32), ("qc", 32), ("qb", 32),
                ("posw", 512), ("pds", 512), ("lr", 20), ("tbf", 4)):
-    _part(_n, _c)
-for _n, _c in (("de", 512), ("qc", 32), ("qb", 32), ("qt", 32), ("qe", 32), ("tr", 32), ("sh5", 4)):
     _part(_n, _c)
 for _g in range(5):
     for _s in ("g%d", "o%d", "id%dr", "rst%d"):
-        if _s != "o%d" or _g:
+        if (_s != "o%d" or _g) and (_s != "rst%d" or _g < 4):
             _part(_s % _g, 64)
 for _g in range(3):
     for _s, _c in (("mq%d", 64), ("ms%d", 68), ("t1%d", 64), ("t3%d", 68)):
@@ -44,13 +43,15 @@ for _g in range(3, 8):
     _part("c%d" % _g, 4 * (WID[_g] + 2), "arb")
     if _g < 7:
         _part("msk%d" % _g, 4 * (WID[_g] + 2), "arb")
-_part("smb", 520, "arb")
+for _n, _c in (("smb", 520), ("id7", 64), ("tz", 1024)):
+    _part(_n, _c, "arb")
 for _r in range(R):
     _part("list%d" % _r, 32)
-    for _s, _c in (("w5s%d", 128), ("w5%d", 128), ("w6%d", 256), ("w7%d", 512)):
+    for _s, _c in (("w5s%d", 128), ("w5%d", 128), ("w6s%d", 256), ("w6%d", 256)):
         _part(_s % _r, _c)
+    _part("w7%d" % _r, 528, "arb")
     SCRATCH["dg%d" % _r] = ("dram", [5, 128, 4], "float32")
-for _n, _c in (("uo", 64), ("rk", 4), ("tb", 4), ("tbl4", 4), ("tab7", 16), ("own6", 4), ("off", 32), ("pos", 32),
+for _n, _c in (("uo", 64), ("rk", 4), ("rr", 4), ("tb", 4), ("tbl4", 4), ("own7", 4), ("own6", 4), ("off", 32), ("pos", 32),
                ("tbl0", 4), ("tbl1", 4), ("tbl2", 4), ("tbl3", 4)):
     _part(_n, _c, "ar16")
 _buf("ar", _used["ar"])
@@ -217,9 +218,6 @@ def rank_program(g, core, T, topo):
     def group_of(B):
         return 4 * (B % 2) + 2 * (B // 2 % 2) + B // 4
 
-    def slot(j):
-        return j + 8 if 8 <= j < 16 else j - 8 if 16 <= j < 24 else j
-
     dma("y", "du", 1, v("ut"), ("u", 0, 128, 0, 512, T.u[:, :]))
     dma("s", "dx0", 1, v("xt", 0, 1024), ("x", 0, 128, 0, 1024, T.x[:, 0:1024]))
     dma("y", "dx1", 1, v("xt", 1024, 2048), ("x", 0, 128, 1024, 2048, T.x[:, 1024:2048]))
@@ -245,14 +243,22 @@ def rank_program(g, core, T, topo):
     def counts(k):
         s = WID[k] + 2
         pat = [[32, 2], [0, 2]] if k == 3 else [[0, 2], [16, 2]] if k == 4 else [[16, 4]]
+        if k < 6:
+            iota(v("msk%d" % k), [[0, 4 * s]], 1)
+            for c in (0, 1):
+                iota(v("c%d" % k, s - 1 - c, 4 * s, s), [[0, 4]], c)
+            iota(v("msk%d" % k, s - 2, 4 * s, s), pat)
+            return
         for c in (s - 2, s - 1) if k < 7 else (s - 2,):
             iota(v("c%d" % k, c, 4 * s, s), pat)
         if k < 7:
             select(v("msk%d" % k), v("ones", 0, 4 * s), [[0, 4], [1, s]], 0.0, cmp=OP.not_equal)
 
     def windows(r):
-        select(v("w5s%d" % r), v("big"), [[0, 128]], BIG)
-        for n, c in (("w5%d", 128), ("list%d", 32), ("w6%d", 256), ("w7%d", 512)):
+        select(v("w5s%d" % r), v("big", 0, 128), [[0, 128]], BIG)
+        iota(v("w5%d" % r), [[0, 128]])
+        select(v("w6s%d" % r), v("big"), [[0, 256]], BIG)
+        for n, c in (("w6%d", 256), ("w7%d", 528)):
             iota(v(n % r), [[0, c]])
 
     iota(v("pi"), [[0, 1]], 0, 1)
@@ -266,21 +272,22 @@ def rank_program(g, core, T, topo):
     starts(3)
     iota(v("iot"), [[1, 512]])
     starts(1)
+    iota(v("n32"), [[0, 2], [1, 32]])
     starts(2)
     for b in range(2):
         select(v("ee%d" % b), v("ones", 0, 514), [[-1, 514]], 0.0, 2 + b, 4)
     counts(3)
-    starts(4)
     counts(4)
     counts(5)
-    windows(0)
     counts(6)
+    windows(0)
     counts(7)
+    iota(v("iom"), [[1, 512]], -256)
     windows(1)
     windows(2)
 
     q = v("bff", 0, 1)
-    dsc, q1, nq2, bq, bm, e6, e7, e7c = [newcol() for _ in range(8)]
+    dsc, q1, nq2, bq, bm, e6, e7, e7c, bk, q63 = [newcol() for _ in range(10)]
     bit = {k: v("bff", c, c + 1) for k, c in ((0, 1), (1, 2), (2, 3), (6, 4), (5, 5), (7, 6))}
     th = {k: newcol() for k in bit}
     lo = {0: v("bff", 7, 8), 1: v("bff", 8, 9), 2: bit[2]}
@@ -354,6 +361,12 @@ def rank_program(g, core, T, topo):
     lin(v("mh"), v("n16"), BIG, bm)
     upick(4, 6)
 
+    def backs():
+        lin(bk, q, -BIG, 15.5 * BIG)
+        lin(q63, q, -1.0, 63.0)
+        for n, src in (("mk16", v("n16")), ("mk32", v("n32")), ("mk64", v("iot", 0, 64))):
+            lin(v(n), src, -BIG, bk)
+
     def compact(name, c0, c1, p0=0, p1=128):
         return v(name, c0 + 15, c1, 16, p0, p1)
 
@@ -398,20 +411,21 @@ def rank_program(g, core, T, topo):
         if r == 0:
             copy(v("tb"), v("tbi"))
             upick(6, 7)
-        act(v("sw0", 0, 256), v("b4", 0, 256), -1.0)
-        ts(v("sw0", 256, 384), v("b5", 0, 128), -1.0, OP.mult)
-        ts(v("sw0", 384, 512), v("b6", 0, 128), -1.0, OP.mult)
+        ts(v("sw0", 0, 256), v("b4", 0, 256), -1.0, OP.mult)
+        act(v("sw0", 256, 384), v("b5", 0, 128), -1.0)
+        act(v("sw0", 384, 512), v("b6", 0, 128), -1.0)
         for k in range(1, 6):
             score(k, sbank(k))
+        ttg(v("gm"), v("sw0"), v("tb"), v("mq0"), OP.max)
+        sgather(v("g0"), v("sw0"), v("tb"))
         scored(1)
         if r == 0:
             sgather(v("id0r"), v("iot"), v("tb"))
-        ttg(v("gm"), v("sw0"), v("tb"), v("mq0"), OP.max)
-        vgather(v("g0"), v("sw0"), v("tb"))
         sgather(v("o1"), v("sw1"), v("tb"))
         scored(2)
         if r == 0:
             act(v("md", 64, 128), v("md", 0, 64))
+            backs()
             act(v("md", 128, 256), v("md", 0, 128))
 
         def ids(k):
@@ -424,37 +438,44 @@ def rank_program(g, core, T, topo):
             act(v("lr", 4 * k, 4 * k + 4), compact("ds", 0, 64))
             dma("y", "dga%d%d" % (r, k), 1, ("dg%d" % r, 0, 128, k, k + 1, dg[k]), v("lr", 4 * k, 4 * k + 4))
 
-        def place(k, add):
+        def run(k):
             s = WID[k] + 2
-            scan(v("smb", 0, 4 * s), v("msk%d" % k), v("c%d" % k), 0.0, OP.mult, OP.add)
-            ts(v("rk"), v("smb", s - 2, 4 * s, s), add, OP.add)
+            scan(v("smb", 0, 4 * s), v("msk%d" % k), v("c%d" % k), 0.0, OP.add, OP.mult)
+            return v("smb", s - 2, 4 * s, s)
+
+        def keys(out, m, row):
+            scan(out, m, row, BIG, OP.max, OP.min)
 
         for k in range(5):
             w = WID[k]
             G = v("g%d" % k)
             C = "c%d" % k
-            if 0 < k < 3:
-                tt(v("gm"), G, v("mq%d" % k), OP.max)
             if k == 0:
-                scan(v("kd"), v("rst3"), v("gm"), BIG, OP.max, OP.min)
-            scan(v("kk"), v("rst%d" % k), G, BIG, OP.max, OP.min)
-            if k:
+                keys(v("kd"), v("rst3"), v("gm"))
+                keys(v("kk"), v("rst0"), G)
+            elif k < 3:
+                tt(v("gm"), G, v("mq%d" % k), OP.max)
+                keys(v("kk"), v("rst%d" % k), G)
                 diag(v("ds"), ids(k), 0, 64)
-            if 0 < k < 3:
-                scan(v("kd"), v("rst3"), v("gm"), BIG, OP.max, OP.min)
-            elif k:
-                hold(v("kd"), v("mh"), v("kk"))
-            if k:
+                keys(v("kd"), v("rst3"), v("gm"))
                 table(k - 1)
+            else:
+                keys(v("kd"), v("mk16"), G)
+                if k == 4:
+                    keys(v("kk"), v("mk32"), G)
+                diag(v("ds"), ids(k), 0, 64)
             s = 17 if k < 3 else w + 2
             for c in range(4):
-                x = v("kd", 16 * c + 15, 16 * c + 16)
                 if k < 3:
+                    x = v("kd", 16 * c + 15, 16 * c + 16)
                     ts(v(C, s * c, s * c + 16), v("kk", 16 * c, 16 * c + 16), x, OP.subtract, th[k], OP.is_gt)
                 else:
                     left = c % 2 == 0 if k == 3 else c < 2
-                    a = 16 * (c ^ 1) if k == 3 else 32 * left
-                    ts(v(C, s * c, s * c + w), v("kk", a, a + w), x, OP.is_gt if left else OP.is_ge)
+                    a = 48 - 16 * (c ^ 1) if k == 3 else 32 - 32 * left
+                    x = v("kd", 63 - 16 * c, 64 - 16 * c) if k == 3 or c % 2 == 0 else v("kk", 79 - 16 * c, 80 - 16 * c)
+                    ts(v(C, s * c, s * c + w), v("g%d" % k, a, a + w), x, OP.is_gt if left else OP.is_ge)
+            if k > 2:
+                table(k - 1)
             if r == 0 and k == 1:
                 upick(7, 8)
             if r == 0 and k in (2, 3):
@@ -463,12 +484,16 @@ def rank_program(g, core, T, topo):
                 scan(v("sm"), v("ms%d" % k), v(C), 0.0, OP.mult, OP.add)
                 if r == 0 and k == 2:
                     units(1)
+                if k == 2:
+                    ts(v("rr"), v("sm", 16, 68, 17), -1.0 / SEP, OP.mult, 63.0, OP.add)
                 ts(v("rk"), v("sm", 16, 68, 17), 1.0 / SEP, OP.mult)
             else:
-                place(k, q)
-            if r == 0 and k == 3:
-                units(3)
-            scatter(v("g%d" % (k + 1)), v("rk"), v("o%d" % (k + 1)))
+                n = run(k)
+                if r == 0 and k == 3:
+                    units(3)
+                ts(v("rr"), n, -1.0, OP.mult, q63, OP.add)
+                ts(v("rk"), n, q, OP.add)
+            scatter(v("g%d" % (k + 1)), v("rk" if k < 2 else "rr"), v("o%d" % (k + 1)))
             scatter(v(ids(k + 1)), v("rk"), v(ids(k)))
             if k == 0:
                 score(6, sbank(6))
@@ -491,18 +516,21 @@ def rank_program(g, core, T, topo):
         def versus(k, c):
             w = WID[k]
             s = w + 2
-            ts(v("c%d" % k, s * c, s * c + w), v("np%d" % k), v("hh%d" % k, 16 * c + 15, 16 * c + 16), OP.subtract, th[k], OP.is_gt)
+            e = ENDS[c] if k == 5 else 16 * c + 16
+            ts(v("c%d" % k, s * c, s * c + w), v("np%d" % k), v("ke" if k == 5 else "hh%d" % k, e - 1, e), OP.subtract, th[k], OP.is_gt)
 
-        runmin(v("no5"), v("g5"))
+        ENDS = (16, 48, 96, 160)
+        for a in (0, 1):
+            act(hf("np5", 0, 64, a), hf("g5", 0, 64, 1 - a))
+        for c in range(4):
+            n = 16 * c + 16
+            keys(v("ke", ENDS[c] - n, ENDS[c]), v("mk64", 0, n), v("g5", 64 - n, 64))
         diag(v("ds"), "idw", 0, 64)
-        act(hf("np5", 0, 64, 1), hf("no5", 0, 64, 0))
-        copy(hf("np5", 0, 64, 0), hf("no5", 0, 64, 1))
-        hold(v("hh5"), v("mh"), v("no5"))
-        table(4)
         for c in range(4):
             versus(5, c)
+        table(4)
         half(1)
-        place(5, q)
+        ts(v("rk"), run(5), q, OP.add)
         scatter(v("w5s%d" % r), v("rk"), v("o6"))
         scatter(v("w5%d" % r), v("rk"), v("idw"))
         runmin(hf("no6", 0, 128, 0), hf("w5s%d" % r, 0, 128, 0), hf("w5s%d" % r, 0, 128, 1))
@@ -515,78 +543,95 @@ def rank_program(g, core, T, topo):
         diag(v("ds6"), "w5%d" % r, 0, 128)
         for a in (0, 1):
             act(hf("sh5", 0, 4, a), compact("ds6", 64 * a, 64 * a + 64, 64 - 64 * a, 128 - 64 * a))
-        for c in range(3):
+        for c in range(2):
             versus(6, c)
         for a in (0, 1):
             tt(hf("lr5", 0, 4, a), compact("ds6", 64 * a, 64 * a + 64, 64 * a, 64 * a + 64), hf("sh5", 0, 4, a))
-        versus(6, 3)
+        for c in range(2, 4):
+            versus(6, c)
         ts(v("own6"), v("lr5"), dsc, OP.mult)
+        sgather(v("o7"), v("sw7"), v("own6"))
         sgather(v("id6"), v("iot"), v("own6"))
         whole(1)
         for B in range(8):
-            h, c = 16 * group_of(B), slot(4 * B)
+            h, c = 16 * group_of(B), 4 * B
             dma("y", "dl%d" % r, 8, v(lst, c, c + 4, 1, 0, 80), ("dg%d" % r, h, h + 16, 0, 5, dg[0:5, h:h + 16, :]))
         for B in range(8):
-            h, c = 16 * group_of(B), slot(4 * B)
+            h, c = 16 * group_of(B), 4 * B
             dma("y", "dm%d" % r, 8, v(lst, c, c + 4, 1, 80, 96), v("lr5", 0, 4, 1, h, h + 16))
-        place(6, e6)
+        for c0, c1 in ((0, 390), (390, 520)):
+            scan(v("smb", c0, c1), v("msk6", c0, c1), v("c6", c0, c1), 0.0, OP.mult, OP.add)
+        ts(v("rk"), v("smb", 128, 520, 130), e6, OP.add)
+        scatter(v("w6s%d" % r), v("rk"), v("o7"))
         scatter(v("w6%d" % r), v("rk"), v("id6"))
-        diag(v("ds7"), "w6%d" % r, 0, 256)
-        tt(hf("qa", 0, 16, 0), compact("ds7", 0, 256, 0, 64), compact("ds7", 0, 256, 64, 128))
-        tt(quad("ap6", 0, 16, 0), quad("qa", 0, 16, 0), quad("qa", 0, 16, 1))
-        for a in range(4):
-            ts(quad("tab7", 0, 16, a), quad("ap6", 0, 16, 0), dscp(0, 32), OP.mult)
-        sgather(v("gg", 128, 256), v("sw7"), v("tab7", 8, 16))
-        vgather(v("gg", 0, 128), v("sw7"), v("tab7", 0, 8))
-        for j in range(4):
-            c = slot(8 * j)
-            dma("y", "dn%d" % r, 4, v(lst, c, c + 8, 1, 96, 112), v("ap6", 8 * (j % 2), 8 * (j % 2) + 8, 1, 16 * (j // 2), 16 * (j // 2) + 16))
-        sgather(v("idg"), v("iot"), v("tab7"))
-        for a in range(4):
-            c = 64 * (2 * (a % 2) + a // 2)
-            act(quad("id7", 0, 64, a), quad("idg", c, c + 64, a))
+        runmin(hf("nh7", 0, 256, 0), hf("w6s%d" % r, 0, 256, 0), hf("w6s%d" % r, 0, 256, 1))
         half(2)
-        runmin(v("no7"), v("gg"))
-        trans(v("t7", 0, 256), v("no7"))
-        trans(v("t7", 256, 288), v("no7", 0, 32))
+        runmin(quad("no7", 0, 256, 0), quad("nh7", 0, 256, 0), quad("nh7", 0, 256, 1))
+        trans(quad("t7", 0, 256, 0), quad("no7", 0, 256, 0))
+        trans(quad("t7", 256, 288, 0), quad("no7", 0, 32, 0))
         for a in range(4):
             c = 64 * (2 * (a % 2) + a // 2)
-            hold(quad("hh7", 0, 64, a), quad("mh", 0, 64, a), quad("no7", c, c + 64, a))
-        trans(v("np7"), v("t7", 16, 272))
-        for c in range(4):
-            versus(7, c)
-            if c < 3:
-                accum(v("jk", 258 * c, 258 * c + 257), v("c7", 258 * c, 258 * c + 257), v("sum4", c, c + 1))
-        half(3)
-        scan(v("smb", 0, 256), v("ones", 0, 256), v("c7", 774, 1030), 0.0, OP.mult, OP.add)
+            hold(quad("hh7", 0, 64, a), quad("mh", 0, 64, 0), quad("no7", c, c + 64, 0))
+        for a in range(3):
+            trans(quad("np7", 0, 256, a), quad("t7", 16, 272, 0))
+            if a == 0:
+                act(quad("np7", 0, 256, 3), quad("np7", 0, 256, 0))
+        diag(v("ds7"), "w6%d" % r, 0, 256)
+        act(hf("sa", 0, 16, 0), compact("ds7", 0, 256, 64, 128))
+
+        def count7(c):
+            accum(v("jk", 258 * c, 258 * c + 257), v("c7", 258 * c, 258 * c + 257), v("sum4", c, c + 1))
+
+        versus(7, 0)
+        count7(0)
+        versus(7, 1)
+        tt(hf("qa", 0, 16, 0), compact("ds7", 0, 256, 0, 64), hf("sa", 0, 16, 0))
+        act(quad("sb", 0, 16, 0), quad("qa", 0, 16, 1))
+        count7(1)
+        versus(7, 2)
+        count7(2)
+        versus(7, 3)
+        tt(quad("ap6", 0, 16, 0), quad("qa", 0, 16, 0), quad("sb", 0, 16, 0))
         ts(v("off", 0, 32, 1, 0, 96), v(lst, 0, 32, 1, 0, 96), dscp(0, 96), OP.mult)
+        scan(v("smb", 0, 256), v("ones", 0, 256), v("c7", 774, 1030), 0.0, OP.mult, OP.add)
+        for a in range(4):
+            c = 4 * (2 * (a % 2) + a // 2)
+            ts(quad("own7", 0, 4, a), quad("ap6", c, c + 4, 0), dscp(0, 32), OP.mult)
+        sgather(v("id7"), v("iom"), v("own7"))
+        for j in range(2):
+            dma("y", "dn%d" % r, 2, v(lst, 16 * j, 16 * j + 16, 1, 96, 112), v("ap6", 0, 16, 1, 16 * j, 16 * j + 16))
+        half(3)
         ts(v("rk", 3, 4), v("smb", 255, 256), e7c, OP.add)
         ts(v("rk", 0, 3), v("sum4", 0, 3), e7, OP.add)
-        trans(quad("qe", 0, 32, 3), quad(lst, 0, 32, 3))
-        scatter(v("w7%d" % r), v("rk"), v("id7"))
-        for j in range(4):
-            c = 16 * slot(8 * j)
-            diag(v("de", c, c + 128), "w7%d" % r, 128 * j, 128 * j + 128)
-        tt(hf("qc", 0, 32, 1), compact("de", 0, 512, 64, 128), compact("de", 0, 512, 0, 64))
+        scatter(v("w7%d" % r, 16, 528), v("rk"), v("id7"))
+        trans(v("tz", 0, 512), v("w7%d" % r, 0, 512))
+        trans(v("tz", 512, 1024), v("w7%d" % r, 16, 528))
+        for j in range(2):
+            tt(v("qh", j, 32, 2), v("tz", 512 * j, 512 * j + 512, 32), v("tz", 512 * j + 16, 512 * j + 512, 32))
+        tt(hf("qc", 0, 32, 1), hf("qh", 0, 32, 1), hf("qh", 0, 32, 0))
         tt(quad("qb", 0, 32, 3), quad("qc", 0, 32, 3), quad("qc", 0, 32, 2))
-        trans(quad("qt", 0, 32, 3), quad("qb", 0, 32, 3))
-        tt(quad("qe", 16, 32, 3), quad("qt", 0, 16, 3), quad("qt", 16, 32, 3))
-        trans(quad("tr", 0, 32, 3), quad("qe", 0, 32, 3))
-        ts(quad("off", 0, 32, 3), quad("tr", 0, 32, 3), dscp(96, 128), OP.mult)
+        ts(quad("off", 0, 32, 3), quad("qb", 0, 32, 3), 256.0, OP.add, 0.0, OP.max)
+        ts(v("off", 0, 32, 1, 96, 112), v(lst, 0, 32, 1, 96, 112), dscp(96, 112), OP.mult)
 
         rid, pid, _s = topo.addr(nxt)
         eng = topo.engines(core, nxt)
         ways = (eng[0::2], eng[1::4])
         n_eng = len(ways[0]) + len(ways[1])
+
+        def pair(j, b):
+            c = 128 * j
+            ttg(v("zt", 4 * c + b, 4 * c + 512, 4), v("fh%d" % b), v("off", 16 + 8 * j, 24 + 8 * j), v("pa%d" % b, c, c + 128))
+
+        for j in range(2):
+            for b in (1, 2, 3) if j == 0 else range(4):
+                sgather(v("pa%d" % b, 128 * j, 128 * j + 128), v("fh%d" % b), v("off", 8 * j, 8 * j + 8))
+        vgather(v("pa0", 0, 128), v("fh0"), v("off", 0, 8))
         for j in range(2):
             c = 128 * j
-            first, second = v("off", 16 * j, 16 * j + 8), v("off", 16 * j + 8, 16 * j + 16)
-            for b in (1, 2, 3) if j == 0 else range(4):
-                sgather(v("pa%d" % b, c, c + 128), v("fh%d" % b), first)
+            for b in (1, 0, 2, 3) if j == 0 else (1, 2, 3):
+                pair(j, b)
             if j == 0:
-                vgather(v("pa0", c, c + 128), v("fh0"), first)
-            for b in range(4):
-                ttg(v("zt", 4 * c + b, 4 * c + 512, 4), v("fh%d" % b), second, v("pa%d" % b, c, c + 128))
+                pair(1, 0)
             quant(v("zq", c, c + 128), v("zqs", c, c + 128), v("zt", 4 * c, 4 * c + 512))
             sem, loc = ("aa%d", "ab%d")[j] % r, "lc%d" % r
             for src, land, es in ((cd("zq", c, c + 128), cd("zl%d" % r, c, c + 128), ways[0]),
@@ -599,25 +644,21 @@ def rank_program(g, core, T, topo):
             total[loc] = 2 * n_eng
         if r < R - 1:
             for B in range(8):
-                h, c = 16 * group_of(B), slot(4 * B)
-                dma("y", "db%d" % r, 8, v("tbf", 0, 4, 1, h, h + 16), v("tr", c, c + 4, 1, 112, 128))
+                h, c = 16 * group_of(B), 4 * B
+                dma("y", "db%d" % r, 8, v("tbf", 0, 4, 1, h, h + 16), v("qb", c, c + 4, 1, 112, 128))
         scatter(v("posw"), v("off"), v("iot"))
-        for j in range(2):
-            for b in (2, 3):
-                sgather(v("fs%d" % b, 256 * j, 256 * j + 256), v("fh%d" % b), v("off", 16 * j, 16 * j + 16), 64.0)
-        for c in (0, 256):
-            diag(v("pds", c, c + 256), "posw", c, c + 256)
+        for b in (2, 3):
+            sgather(v("fs%d" % b), v("fh%d" % b), v("off"), 64.0)
         if r == 0:
             quant(v("vq"), v("vqs"), v("vt"))
+        for c in (0, 256):
+            diag(v("pds", c, c + 256), "posw", c, c + 256)
         if r < R - 1:
-            ts(v("tb"), v("tbf"), dsc, OP.mult)
+            ts(v("tb"), v("tbf"), 256.0, OP.add)
             sgather(v("id0r"), v("iot"), v("tb"))
         else:
             sgather(v("row"), v("iot"), v("off"))
-            for j in range(4):
-                c = 16 * slot(8 * j)
-                dma("y", "dod", 4, ("od", 0, 8, 128 * j, 128 * j + 128, T.od[:, 128 * j:128 * j + 128]),
-                    ("row", 0, 128, c, c + 128, T.row[0:128:16, c:c + 128]))
+            dma("y", "dod", 1, ("od", 0, 8, 0, 512, T.od[:, :]), ("row", 0, 128, 0, 512, T.row[0:128:16, :]))
         ts(v("pos"), v("pds", 15, 512, 16), dsc, OP.mult)
         for j in range(2):
             c = 128 * j
@@ -625,14 +666,15 @@ def rank_program(g, core, T, topo):
                 mm(v("b%d" % (4 * j + b), 0, 128), v("wq", 128 * b, 128 * b + 128), v("wqs", 128 * b, 128 * b + 128),
                    v("zl%d" % r, c, c + 128), v("zl%ds" % r, c, c + 128))
             for b in range(4):
-                for a in (2 * c, 2 * c + 128):
+                for a in (c, c + 256):
                     if b < 2:
                         act(v("pp%d" % b, a, a + 128), v("b%d" % (4 * j + b), 0, 128), 0.03125)
                     else:
                         tt(v("pp%d" % b, a, a + 128), v("b%d" % (4 * j + b), 0, 128), v("fs%d" % b, a, a + 128))
         for b in (0, 1):
             sgather(v("xt", b + 2, 2048, 4), v("pp%d" % (b + 2)), v("pos"), 0.03125)
-            ttg(v("xt", b, 2048, 4), v("pp%d" % b), v("pos"), v("f%d" % b))
+            for c0, c1 in ((0, 512),) if b == 0 else ((0, 256), (256, 512)):
+                ttg(v("xt", 4 * c0 + b, 4 * c1, 4), v("pp%d" % b), v("pos", c0 // 16, c1 // 16), v("f%d" % b, c0, c1))
 
     for i, (a, b) in enumerate(PIECES):
         quantx(i)

@@ -1,3 +1,4 @@
+from concourse.bass import DstId, RemoteDMATransfer
 from concourse.mybir import dt, AluOpType as OP, ActivationFunctionType as AF
 
 BIG = 2.0 ** 75
@@ -6,11 +7,13 @@ SEP = 64.0
 DIG = 2.0 ** 14
 R = 3
 WID = [2, 4, 8, 16, 32, 64, 128, 256]
+ZW = 384
+CUT = 44
 
 SCRATCH = {}
 PLACE = {}
 _used = {"ar": 0, "ar16": 0, "arb": 0}
-SEMAPHORES = ["sv", "ss", "sp", "sg", "dx0", "dx1", "du", "dv", "dp", "dw", "doc", "dos", "dod", "dy"]
+SEMAPHORES = ["sv", "ss", "sp", "sg", "dx0", "dx1", "dx2", "du", "dv", "dp", "dw", "doc", "dos", "dod", "dy"]
 
 
 def _buf(name, cols, dtype="float32", where="sbuf"):
@@ -28,8 +31,8 @@ for _n, _c in (("n16", 64), ("i17", 68), ("iot", 512), ("io4", 4), ("bff", 16), 
                ("mk16", 64), ("mk32", 64), ("mk64", 64), ("ke", 160),
                ("kk", 64), ("gm", 64), ("kd", 64), ("sm", 68), ("g5", 64), ("o5", 64), ("o6", 64), ("o7", 64), ("idw", 64),
                ("np5", 64), ("no6", 128), ("np6", 128), ("hh6", 64), ("id6", 64), ("lr5", 4), ("sh5", 4),
-               ("qa", 16), ("ap6", 16), ("sa", 16), ("sb", 16), ("nh7", 256), ("no7", 256), ("t7", 288), ("np7", 256), ("hh7", 64),
-               ("jk", 774), ("sum4", 4), ("ds", 64), ("ds6", 128), ("ds7", 256), ("qh", 32), ("qc", 32), ("qb", 32),
+               ("ap6", 16), ("sa", 64), ("sb", 64), ("m4", 64), ("nh7", 256), ("no7", 256), ("t7", 288), ("np7", 256), ("hh7", 64),
+               ("jk", 774), ("sum4", 4), ("ds", 64), ("ds6", 128), ("ds7", 256), ("qh", 32), ("qc", 32),
                ("posw", 512), ("pds", 512), ("lr", 20), ("tbf", 4)):
     _part(_n, _c)
 for _g in range(5):
@@ -46,12 +49,12 @@ for _g in range(3, 8):
 for _n, _c in (("smb", 520), ("id7", 64), ("tz", 1024)):
     _part(_n, _c, "arb")
 for _r in range(R):
-    _part("list%d" % _r, 32)
+    _part("list%d" % _r, 64)
     for _s, _c in (("w5s%d", 128), ("w5%d", 128), ("w6s%d", 256), ("w6%d", 256)):
         _part(_s % _r, _c)
     _part("w7%d" % _r, 528, "arb")
     SCRATCH["dg%d" % _r] = ("dram", [5, 128, 4], "float32")
-for _n, _c in (("uo", 64), ("rk", 4), ("rr", 4), ("tb", 4), ("tbl4", 4), ("own7", 4), ("own6", 4), ("off", 32), ("pos", 32),
+for _n, _c in (("uo", 64), ("rk", 4), ("rr", 4), ("tb", 4), ("tbl4", 4), ("own7", 4), ("own6", 4), ("off", 32), ("pos", 32), ("pom", 32), ("sel", 2),
                ("tbl0", 4), ("tbl1", 4), ("tbl2", 4), ("tbl3", 4)):
     _part(_n, _c, "ar16")
 _buf("ar", _used["ar"])
@@ -68,11 +71,11 @@ for _b in range(4):
 for _b in range(2):
     _buf("f%d" % _b, 512)
     _buf("fs%d" % (_b + 2), 512)
-for _n, _c in (("pi", 1), ("bi", 16), ("uoi", 64), ("tbi", 4)):
+for _n, _c in (("pi", 1), ("bi", 16), ("uoi", 64), ("tbi", 4), ("pn", 32), ("pm", 32)):
     _buf(_n, _c, "int32")
-for _n, _c in (("xt", 2048), ("ut", 512), ("vt", 512), ("zt", 1024), ("ee0", 514), ("ee1", 514), ("ones", 520)):
+for _n, _c in (("xt", 2048), ("ut", 512), ("vt", 512), ("zt", 1024), ("ee0", 514), ("ee1", 514), ("ones", 520), ("zz", 512)):
     _buf(_n, _c, "bfloat16")
-for _n, _c in (("xq", 512), ("uq", 128), ("uc", 1024), ("vq", 128), ("wq", 512), ("zq", 256), ("eq", 512)) + tuple(("zl%d" % r, 256) for r in range(R)):
+for _n, _c in (("xq", 512), ("uq", 128), ("uc", 1024), ("vq", 128), ("wq", 512), ("zq", ZW), ("eq", 512)) + tuple(("zl%d" % r, ZW) for r in range(R)):
     _buf(_n, _c, "float8_e4m3fn_x4")
     _buf(_n + "s", _c, "uint8")
 for _b in range(8):
@@ -80,6 +83,8 @@ for _b in range(8):
 for _r in range(R):
     SEMAPHORES += [s % _r for s in ("aa%d", "ab%d", "lc%d", "dl%d", "dm%d", "dn%d", "db%d")]
     SEMAPHORES += ["dga%d%d" % (_r, g) for g in range(5)]
+OPT = {"sw0": "vsv", "np6": 3, "early": 1, "pa0": "s", "n0": 6}
+LAST = (0, 192, 384, 512)
 PIECES = ((0, 256), (256, 384), (384, 512))
 
 
@@ -93,6 +98,7 @@ def rank_program(g, core, T, topo):
     count = {k: 0 for k in semof}
     known = {k: {} for k in queues}
     hist = {}
+    behind = {}
     total = {}
 
     def need(q, tok):
@@ -100,6 +106,8 @@ def rank_program(g, core, T, topo):
         if known[q].get(sem, 0) < val:
             queues[q].wait_ge(T.sem[sem], val)
             known[q][sem] = val
+            for s, n in behind.get(tok, {}).items():
+                known[q][s] = max(known[q].get(s, 0), n)
 
     def v(name, c0=0, c1=None, st=1, p0=0, p1=128):
         name, at, cols = PLACE[name]
@@ -122,9 +130,14 @@ def rank_program(g, core, T, topo):
                     if ps and eng != q or (w or hw) and a < p1 and p0 < b and c < c1 and c0 < d and not (s == st > 1 and (c - c0) % st):
                         toks[tok[0]] = max(toks.get(tok[0], 0), tok[1])
         for s in sorted(toks):
-            need(q, (s, toks[s]))
+            if not any(behind.get((t, toks[t]), {}).get(s, 0) >= toks[s] for t in toks if t != s):
+                need(q, (s, toks[s]))
 
     def note(q, tok, ins, outs):
+        if q in known:
+            seen = behind.setdefault(tok, {})
+            for s, n in known[q].items():
+                seen[s] = max(seen.get(s, 0), n)
         for w, views in ((0, ins), (1, outs)):
             for n, p0, p1, c0, c1, ap, st in views:
                 h = hist.setdefault(n, [])
@@ -219,11 +232,13 @@ def rank_program(g, core, T, topo):
         return 4 * (B % 2) + 2 * (B // 2 % 2) + B // 4
 
     dma("y", "du", 1, v("ut"), ("u", 0, 128, 0, 512, T.u[:, :]))
-    dma("s", "dx0", 1, v("xt", 0, 1024), ("x", 0, 128, 0, 1024, T.x[:, 0:1024]))
-    dma("y", "dx1", 1, v("xt", 1024, 2048), ("x", 0, 128, 1024, 2048, T.x[:, 1024:2048]))
+    for i in range(3):
+        a, b = 4 * PIECES[i][0], 4 * PIECES[i][1]
+        dma("y", "dx%d" % i, 1, v("xt", a, b), ("x", 0, 128, a, b, T.x[:, a:b]))
     for B in range(8):
         h = 16 * group_of(B)
-        dma("y", "dp", 8, v("tbi", 0, 4, 1, h, h + 16), ("p", 0, 16, 4 * B, 4 * B + 4, T.p[:, 4 * B:4 * B + 4]))
+        dma("s", "dp", 8, v("tbi", 0, 4, 1, h, h + 16), ("p", 0, 16, 4 * B, 4 * B + 4, T.p[:, 4 * B:4 * B + 4]))
+    need("y", ("dp", 128))
     dma("y", "dv", 1, v("vt"), ("v", 0, 128, 0, 512, T.v[:, :]))
     dma("y", "dw", 2, cd("wq"), ("wc", 0, 128, 0, 2048, T.wc[:, :]))
     dma("y", "dw", 2, v("wqs"), ("ws", 0, 128, 0, 512, T.ws[:, :]))
@@ -257,12 +272,15 @@ def rank_program(g, core, T, topo):
     def windows(r):
         select(v("w5s%d" % r), v("big", 0, 128), [[0, 128]], BIG)
         iota(v("w5%d" % r), [[0, 128]])
+        iota(v("list%d" % r), [[0, 64]])
         select(v("w6s%d" % r), v("big"), [[0, 256]], BIG)
         for n, c in (("w6%d", 256), ("w7%d", 528)):
             iota(v(n % r), [[0, c]])
 
     iota(v("pi"), [[0, 1]], 0, 1)
     fill(v("big"), BIG)
+    for c, m in enumerate((15, 2, 4, 8, 32, 64, 16, 14, 12)):
+        ts(v("bi", c, c + 1), v("pi"), m, OP.bitwise_and)
     fill(v("ones"), 1.0)
     iota(v("n16"), [[0, 4], [1, 16]])
     iota(v("io4"), [[16, 4]])
@@ -282,18 +300,17 @@ def rank_program(g, core, T, topo):
     counts(6)
     windows(0)
     counts(7)
+    select(v("m4"), v("ones", 0, 64), [[0, 16], [1, 4]], 0.0, cmp=OP.not_equal)
+    iota(v("zz"), [[0, 512]])
     iota(v("iom"), [[1, 512]], -256)
     windows(1)
     windows(2)
 
     q = v("bff", 0, 1)
-    dsc, q1, nq2, bq, bm, e6, e7, e7c, bk, q63 = [newcol() for _ in range(10)]
+    dsc, q1, nq2, bq, bm, e6, e7, e7c, bk, q63, g7, g32, dsl = [newcol() for _ in range(13)]
     bit = {k: v("bff", c, c + 1) for k, c in ((0, 1), (1, 2), (2, 3), (6, 4), (5, 5), (7, 6))}
     th = {k: newcol() for k in bit}
     lo = {0: v("bff", 7, 8), 1: v("bff", 8, 9), 2: bit[2]}
-    for j, m in enumerate((15, 14, 12, 2, 4, 8, 32, 64, 16)):
-        c = (0, 7, 8, 1, 2, 3, 4, 5, 6)[j]
-        ts(v("bi", c, c + 1), v("pi"), m, OP.bitwise_and)
     copy(v("bff", 0, 9), v("bi", 0, 9))
     copy(v("uo"), v("uoi"))
     ts(v("rtab"), v("io4"), q, OP.add)
@@ -334,13 +351,8 @@ def rank_program(g, core, T, topo):
     ts(e6, bit[5], q, OP.add)
     tt(v("md", 0, 64), v("md", 0, 64), v("mda"))
     ts(e7, bit[6], 4.0, OP.mult, e6, OP.add)
-    for k in range(3):
-        partner(k)
-    ts(e7c, e7, 48.0, OP.add)
-    for k in range(3):
-        tt(v("ms%d" % k), v("ms%d" % k), v("t3%d" % k))
+    partner(0)
     masks(0)
-    masks(1)
 
     def upick(a, b):
         o, w, f = v("uc", 128 * a, 128 * b), v("uq"), v("uo", 8 * a, 8 * b)
@@ -352,18 +364,21 @@ def rank_program(g, core, T, topo):
         quant(v("eq", 128 * b, 128 * b + 128), v("eqs", 128 * b, 128 * b + 128), v("ee%d" % (b % 2), c, c + 512))
 
     quant(v("uq"), v("uqs"), v("ut"))
-    upick(0, 1)
-    upick(1, 4)
-    masks(2)
-    lin(bm, q, -BIG, -BIG / 2)
-    for k in (5, 6, 7):
-        lin(th[k], bit[k], -EPS / MASK[k], 0.0)
-    lin(v("mh"), v("n16"), BIG, bm)
-    upick(4, 6)
+    partner(1)
+    partner(2)
+    upick(0, 2)
+    ts(e7c, e7, 48.0, OP.add)
+    for k in range(3):
+        tt(v("ms%d" % k), v("ms%d" % k), v("t3%d" % k))
+    masks(1)
 
     def backs():
         lin(bk, q, -BIG, 15.5 * BIG)
+        lin(bm, q, -BIG, -BIG / 2)
         lin(q63, q, -1.0, 63.0)
+        for k in (5, 6, 7):
+            lin(th[k], bit[k], -EPS / MASK[k], 0.0)
+        lin(v("mh"), v("n16"), BIG, bm)
         for n, src in (("mk16", v("n16")), ("mk32", v("n32")), ("mk64", v("iot", 0, 64))):
             lin(v(n), src, -BIG, bk)
 
@@ -410,23 +425,23 @@ def rank_program(g, core, T, topo):
             score(0, "b%d" % (4 + i), a, b)
         if r == 0:
             copy(v("tb"), v("tbi"))
-            upick(6, 7)
-        ts(v("sw0", 0, 256), v("b4", 0, 256), -1.0, OP.mult)
-        act(v("sw0", 256, 384), v("b5", 0, 128), -1.0)
-        act(v("sw0", 384, 512), v("b6", 0, 128), -1.0)
-        for k in range(1, 6):
-            score(k, sbank(k))
+        for i, (a, b) in enumerate(PIECES):
+            if OPT["sw0"][i] == "v":
+                ts(v("sw0", a, b), v("b%d" % (4 + i), 0, b - a), -1.0, OP.mult)
+            else:
+                act(v("sw0", a, b), v("b%d" % (4 + i), 0, b - a), -1.0)
+        score(1, sbank(1))
+        if r == 0:
+            upick(2, 3)
         ttg(v("gm"), v("sw0"), v("tb"), v("mq0"), OP.max)
         sgather(v("g0"), v("sw0"), v("tb"))
+        for k in range(2, 3 if r == 0 else 6):
+            score(k, sbank(k))
         scored(1)
         if r == 0:
             sgather(v("id0r"), v("iot"), v("tb"))
         sgather(v("o1"), v("sw1"), v("tb"))
         scored(2)
-        if r == 0:
-            act(v("md", 64, 128), v("md", 0, 64))
-            backs()
-            act(v("md", 128, 256), v("md", 0, 128))
 
         def ids(k):
             return "idw" if k == 5 else "id%dr" % k
@@ -476,17 +491,21 @@ def rank_program(g, core, T, topo):
                     ts(v(C, s * c, s * c + w), v("g%d" % k, a, a + w), x, OP.is_gt if left else OP.is_ge)
             if k > 2:
                 table(k - 1)
-            if r == 0 and k == 1:
-                upick(7, 8)
+            if r == 0 and k < 2:
+                upick(3 + 3 * k, 4 + 3 * k)
             if r == 0 and k in (2, 3):
                 units(2 * k - 4)
             if k < 3:
                 scan(v("sm"), v("ms%d" % k), v(C), 0.0, OP.mult, OP.add)
+                if r == 0 and k < 2:
+                    upick(4 + 3 * k, 5 + 3 * k)
                 if r == 0 and k == 2:
                     units(1)
                 if k == 2:
                     ts(v("rr"), v("sm", 16, 68, 17), -1.0 / SEP, OP.mult, 63.0, OP.add)
                 ts(v("rk"), v("sm", 16, 68, 17), 1.0 / SEP, OP.mult)
+                if r == 0 and k == 0:
+                    upick(5, 6)
             else:
                 n = run(k)
                 if r == 0 and k == 3:
@@ -496,9 +515,19 @@ def rank_program(g, core, T, topo):
             scatter(v("g%d" % (k + 1)), v("rk" if k < 2 else "rr"), v("o%d" % (k + 1)))
             scatter(v(ids(k + 1)), v("rk"), v(ids(k)))
             if k == 0:
-                score(6, sbank(6))
+                if r == 0:
+                    masks(2)
+                    for j in (3, 4, 5):
+                        score(j, sbank(j))
+                else:
+                    score(6, sbank(6))
                 scored(3)
             elif k == 1:
+                if r == 0:
+                    score(6, sbank(6))
+                    act(v("md", 64, 128), v("md", 0, 64))
+                    backs()
+                    act(v("md", 128, 256), v("md", 0, 128))
                 score(7, sbank(7))
                 scored(4)
                 scored(5)
@@ -530,16 +559,21 @@ def rank_program(g, core, T, topo):
             versus(5, c)
         table(4)
         half(1)
-        ts(v("rk"), run(5), q, OP.add)
+        if r == 0:
+            ts(g7, v("pi"), 112.0, OP.is_ge, 256.0, OP.mult)
+            ts(g32, v("pi"), 112.0, OP.is_ge, 32.0, OP.mult)
+        n = run(5)
+        if r == 0:
+            ts(dsl, g7, 1.0 / 256, OP.mult, dsc, OP.max)
+            ts(v("sel"), v("rtab", 0, 2), g32, OP.add)
+        ts(v("rk"), n, q, OP.add)
         scatter(v("w5s%d" % r), v("rk"), v("o6"))
         scatter(v("w5%d" % r), v("rk"), v("idw"))
         runmin(hf("no6", 0, 128, 0), hf("w5s%d" % r, 0, 128, 0), hf("w5s%d" % r, 0, 128, 1))
-        for a in (0, 1):
-            act(quad("np6", 0, 128, a), quad("no6", 0, 128, a ^ 1))
+        for a in range(4):
+            (act if a < OPT["np6"] else copy)(quad("np6", 0, 128, a), quad("no6", 0, 128, 1 - a % 2))
         for a in (0, 1):
             hold(hf("hh6", 0, 64, a), hf("mh", 0, 64, 0), hf("no6", 64 * a, 64 * a + 64, 0))
-        for a in (2, 3):
-            copy(quad("np6", 0, 128, a), quad("no6", 0, 128, 3 - a))
         diag(v("ds6"), "w5%d" % r, 0, 128)
         for a in (0, 1):
             act(hf("sh5", 0, 4, a), compact("ds6", 64 * a, 64 * a + 64, 64 - 64 * a, 128 - 64 * a))
@@ -577,7 +611,8 @@ def rank_program(g, core, T, topo):
             if a == 0:
                 act(quad("np7", 0, 256, 3), quad("np7", 0, 256, 0))
         diag(v("ds7"), "w6%d" % r, 0, 256)
-        act(hf("sa", 0, 16, 0), compact("ds7", 0, 256, 64, 128))
+        for a in range(4):
+            act(v("sa", a, 64, 4, 0, 32), compact("ds7", 0, 256, 32 * a, 32 * a + 32))
 
         def count7(c):
             accum(v("jk", 258 * c, 258 * c + 257), v("c7", 258 * c, 258 * c + 257), v("sum4", c, c + 1))
@@ -585,104 +620,148 @@ def rank_program(g, core, T, topo):
         versus(7, 0)
         count7(0)
         versus(7, 1)
-        tt(hf("qa", 0, 16, 0), compact("ds7", 0, 256, 0, 64), hf("sa", 0, 16, 0))
-        act(quad("sb", 0, 16, 0), quad("qa", 0, 16, 1))
         count7(1)
         versus(7, 2)
+        scan(quad("sb", 0, 64, 0), quad("m4", 0, 64, 0), quad("sa", 0, 64, 0), 0.0, OP.mult, OP.add)
+        act(quad("ap6", 0, 16, 0), v("sb", 3, 64, 4, 0, 32))
         count7(2)
         versus(7, 3)
-        tt(quad("ap6", 0, 16, 0), quad("qa", 0, 16, 0), quad("sb", 0, 16, 0))
-        ts(v("off", 0, 32, 1, 0, 96), v(lst, 0, 32, 1, 0, 96), dscp(0, 96), OP.mult)
-        scan(v("smb", 0, 256), v("ones", 0, 256), v("c7", 774, 1030), 0.0, OP.mult, OP.add)
         for a in range(4):
-            c = 4 * (2 * (a % 2) + a // 2)
-            ts(quad("own7", 0, 4, a), quad("ap6", c, c + 4, 0), dscp(0, 32), OP.mult)
+            c = 16 * (2 * (a % 2) + a // 2)
+            ts(quad("own7", 0, 4, a), v("sb", c + 3, c + 16, 4, 0, 32), dscp(0, 32), OP.mult)
+        scan(v("smb", 0, 256), v("ones", 0, 256), v("c7", 774, 1030), 0.0, OP.mult, OP.add)
         sgather(v("id7"), v("iom"), v("own7"))
         for j in range(2):
             dma("y", "dn%d" % r, 2, v(lst, 16 * j, 16 * j + 16, 1, 96, 112), v("ap6", 0, 16, 1, 16 * j, 16 * j + 16))
         half(3)
         ts(v("rk", 3, 4), v("smb", 255, 256), e7c, OP.add)
         ts(v("rk", 0, 3), v("sum4", 0, 3), e7, OP.add)
+        if r == 0:
+            quant(v("zq", 128, 256), v("zqs", 128, 256), v("zz"))
         scatter(v("w7%d" % r, 16, 528), v("rk"), v("id7"))
         trans(v("tz", 0, 512), v("w7%d" % r, 0, 512))
         trans(v("tz", 512, 1024), v("w7%d" % r, 16, 528))
         for j in range(2):
             tt(v("qh", j, 32, 2), v("tz", 512 * j, 512 * j + 512, 32), v("tz", 512 * j + 16, 512 * j + 512, 32))
         tt(hf("qc", 0, 32, 1), hf("qh", 0, 32, 1), hf("qh", 0, 32, 0))
-        tt(quad("qb", 0, 32, 3), quad("qc", 0, 32, 3), quad("qc", 0, 32, 2))
-        ts(quad("off", 0, 32, 3), quad("qb", 0, 32, 3), 256.0, OP.add, 0.0, OP.max)
-        ts(v("off", 0, 32, 1, 96, 112), v(lst, 0, 32, 1, 96, 112), dscp(96, 112), OP.mult)
+        tt(quad(lst, 32, 64, 3), quad("qc", 0, 32, 3), quad("qc", 0, 32, 2))
+        o, w, f = v("off"), v(lst), v("sel")
+        op("v", lambda e: e.tensor_scalar(o[5], w[5].indirect(f[5]), dsl[5], g7[5], OP.mult, OP.add), [o], [w, f, dsl, g7])
+        if r < R - 1:
+            for B in range(8):
+                h, c = 16 * group_of(B), 4 * B
+                dma("y", "db%d" % r, 8, v("tbf", 0, 4, 1, h, h + 16), v(lst, 32 + c, 36 + c, 1, 112, 128))
 
         rid, pid, _s = topo.addr(nxt)
         eng = topo.engines(core, nxt)
-        ways = (eng[0::2], eng[1::4])
-        n_eng = len(ways[0]) + len(ways[1])
+        ways = [eng[i::4] for i in range(4)]
+        n_eng = len(eng)
 
         def pair(j, b):
             c = 128 * j
             ttg(v("zt", 4 * c + b, 4 * c + 512, 4), v("fh%d" % b), v("off", 16 + 8 * j, 24 + 8 * j), v("pa%d" % b, c, c + 128))
 
         for j in range(2):
-            for b in (1, 2, 3) if j == 0 else range(4):
+            for b in (1, 2, 3) if j == 0 and OPT["pa0"] == "v" else range(4):
                 sgather(v("pa%d" % b, 128 * j, 128 * j + 128), v("fh%d" % b), v("off", 8 * j, 8 * j + 8))
-        vgather(v("pa0", 0, 128), v("fh0"), v("off", 0, 8))
+        if OPT["pa0"] == "v":
+            vgather(v("pa0", 0, 128), v("fh0"), v("off", 0, 8))
+            n0 = 0
+        else:
+            n0 = OPT["n0"]
+            scatter(v("posw"), v("off", 0, n0), v("iot", 0, 16 * n0))
         for j in range(2):
             c = 128 * j
-            for b in (1, 0, 2, 3) if j == 0 else (1, 2, 3):
+            for b in ((1, 0, 2, 3) if n0 == 0 else range(4)) if j == 0 else (1, 2, 3):
                 pair(j, b)
             if j == 0:
                 pair(1, 0)
-            quant(v("zq", c, c + 128), v("zqs", c, c + 128), v("zt", 4 * c, 4 * c + 512))
+            else:
+                scatter(v("posw"), v("off", n0, n0 + 4), v("iot", 16 * n0, 16 * n0 + 64))
+            quant(v("zq", 2 * c, 2 * c + 128), v("zqs", 2 * c, 2 * c + 128), v("zt", 4 * c, 4 * c + 512))
             sem, loc = ("aa%d", "ab%d")[j] % r, "lc%d" % r
-            for src, land, es in ((cd("zq", c, c + 128), cd("zl%d" % r, c, c + 128), ways[0]),
-                                  (v("zqs", c, c + 128), v("zl%ds" % r, c, c + 128), ways[1])):
-                deps("g", [src], [])
-                g.remote_dma(land[5], src[5], T.sem[sem], T.sem[loc], pid, rid, sum(1 << e for e in es))
-                note("g", (loc, 2 * n_eng), [src], [])
-                note("x", (sem, n_eng), [], [land])
+            a, b = (0, 0) if j == 0 else (ZW - 3 * CUT, ZW - 4 * CUT)
+            parts = [(cd("zq", a + CUT * i, a + CUT * i + CUT), cd("zl%d" % r, a + CUT * i, a + CUT * i + CUT)) for i in range(3)]
+            parts.append((v("zqs", b, b + 4 * CUT), v("zl%ds" % r, b, b + 4 * CUT)))
+            deps("g", [src for src, land in parts], [])
+            g.remote_dma_fused([RemoteDMATransfer(dst_ids=[DstId(rid=rid, pnc=pid)], dma_engine_mask=sum(1 << e for e in es),
+                                                  remote_sem=T.sem[sem], src=src[5], dst=land[5])
+                                for (src, land), es in zip(parts, ways)], local_sem=T.sem[loc])
+            note("g", (loc, 2 * n_eng), [src for src, land in parts], [])
+            note("x", (sem, n_eng), [], [land for src, land in parts])
             total[sem] = n_eng
             total[loc] = 2 * n_eng
         if r < R - 1:
-            for B in range(8):
-                h, c = 16 * group_of(B), 4 * B
-                dma("y", "db%d" % r, 8, v("tbf", 0, 4, 1, h, h + 16), v("qb", c, c + 4, 1, 112, 128))
-        scatter(v("posw"), v("off"), v("iot"))
+            ts(v("tb"), v("tbf"), 256.0, OP.add)
+        scatter(v("posw"), v("off", n0 + 4, 32), v("iot", 16 * n0 + 64, 512))
         for b in (2, 3):
             sgather(v("fs%d" % b), v("fh%d" % b), v("off"), 64.0)
-        if r == 0:
-            quant(v("vq"), v("vqs"), v("vt"))
-        for c in (0, 256):
-            diag(v("pds", c, c + 256), "posw", c, c + 256)
-        if r < R - 1:
-            ts(v("tb"), v("tbf"), 256.0, OP.add)
-            sgather(v("id0r"), v("iot"), v("tb"))
-        else:
-            sgather(v("row"), v("iot"), v("off"))
-            dma("y", "dod", 1, ("od", 0, 8, 0, 512, T.od[:, :]), ("row", 0, 128, 0, 512, T.row[0:128:16, :]))
-        ts(v("pos"), v("pds", 15, 512, 16), dsc, OP.mult)
-        for j in range(2):
+
+        def layer(j):
             c = 128 * j
             for b in (2, 0, 3, 1):
                 mm(v("b%d" % (4 * j + b), 0, 128), v("wq", 128 * b, 128 * b + 128), v("wqs", 128 * b, 128 * b + 128),
-                   v("zl%d" % r, c, c + 128), v("zl%ds" % r, c, c + 128))
-            for b in range(4):
+                   v("zl%d" % r, 2 * c, 2 * c + 128), v("zl%ds" % r, 2 * c, 2 * c + 128))
+            for b in range(2):
                 for a in (c, c + 256):
-                    if b < 2:
-                        act(v("pp%d" % b, a, a + 128), v("b%d" % (4 * j + b), 0, 128), 0.03125)
-                    else:
-                        tt(v("pp%d" % b, a, a + 128), v("b%d" % (4 * j + b), 0, 128), v("fs%d" % b, a, a + 128))
-        for b in (0, 1):
-            sgather(v("xt", b + 2, 2048, 4), v("pp%d" % (b + 2)), v("pos"), 0.03125)
-            for c0, c1 in ((0, 512),) if b == 0 else ((0, 256), (256, 512)):
-                ttg(v("xt", 4 * c0 + b, 4 * c1, 4), v("pp%d" % b), v("pos", c0 // 16, c1 // 16), v("f%d" % b, c0, c1))
+                    act(v("pp%d" % b, a, a + 128), v("b%d" % (4 * j + b), 0, 128), 0.03125)
 
-    for i, (a, b) in enumerate(PIECES):
-        quantx(i)
-        mm(v("b%d" % (4 + i), 0, b - a), v("vq"), v("vqs"), v("xq", a, b), v("xqs", a, b))
-        dma("y", "doc", 3, ("oc", 0, 128, 4 * a, 4 * b, T.oc[:, 4 * a:4 * b]), cd("xq", a, b))
-    for i, (a, b) in enumerate(PIECES):
-        (copy if i else act)(v("yy", a, b), v("b%d" % (4 + i), 0, b - a))
-        dma("y", "dy", 3, ("y", 0, 128, a, b, T.y[:, a:b]), v("yy", a, b))
+        def plus(j, b):
+            for a in (128 * j, 128 * j + 256):
+                tt(v("pp%d" % b, a, a + 128), v("b%d" % (4 * j + b), 0, 128), v("fs%d" % b, a, a + 128))
+
+        early = r > 0 and OPT["early"]
+        if r < R - 1:
+            sgather(v("id0r"), v("iot"), v("tb"))
+        layer(0)
+        if r == R - 1:
+            sgather(v("row"), v("iot"), v("off"))
+            dma("y", "dod", 1, ("od", 0, 8, 0, 512, T.od[:, :]), ("row", 0, 128, 0, 512, T.row[0:128:16, :]))
+        if r == 0:
+            quant(v("vq"), v("vqs"), v("vt"))
+        if early:
+            plus(0, 2)
+        for c in (0, 256):
+            diag(v("pds", c, c + 256), "posw", c, c + 256)
+        if early:
+            plus(0, 3)
+        ts(v("pos"), v("pds", 15, 512, 16), dsc, OP.mult)
+        if not early:
+            plus(0, 2)
+            plus(0, 3)
+        layer(1)
+        plus(1, 2)
+        plus(1, 3)
+
+        def back(b, c0, c1):
+            sgather(v("xt", 4 * c0 + b + 2, 4 * c1, 4), v("pp%d" % (b + 2)), v("pos", c0 // 16, c1 // 16), 0.03125)
+            ttg(v("xt", 4 * c0 + b, 4 * c1, 4), v("pp%d" % b), v("pos", c0 // 16, c1 // 16), v("f%d" % b, c0, c1))
+
+        if r < R - 1:
+            for b, c0, c1 in ((0, 0, 512), (1, 0, 256), (1, 256, 512)):
+                back(b, c0, c1)
+
+    def leave(i, step):
+        a, b = LAST[i], LAST[i + 1]
+        if step == 0:
+            quant(v("xq", a, b), v("xqs", a, b), v("xt", 4 * a, 4 * b))
+            mm(v("b%d" % i, 0, b - a), v("vq"), v("vqs"), v("xq", a, b), v("xqs", a, b))
+            dma("y", "doc", n, ("oc", 0, 128, 4 * a, 4 * b, T.oc[:, 4 * a:4 * b]), cd("xq", a, b))
+        else:
+            (act if i < n - 1 else copy)(v("yy", a, b), v("b%d" % i, 0, b - a))
+            dma("y", "dy", n, ("y", 0, 128, a, b, T.y[:, a:b]), v("yy", a, b))
+
+    n = len(LAST) - 1
+    for i in range(n):
+        back(0, LAST[i], LAST[i + 1])
+        if i:
+            leave(i - 1, 0)
+        back(1, LAST[i], LAST[i + 1])
+        if i > 1:
+            leave(i - 2, 1)
+    leave(n - 1, 0)
+    leave(n - 2, 1)
+    leave(n - 1, 1)
     for k in range(4):
         dma("s", "dos", 4, ("osc", 4 * k, 4 * k + 4, 0, 512, T.osc[4 * k:4 * k + 4, :]), v("xqs", 0, 512, 1, 32 * k, 32 * k + 4))
     for k in semof:

@@ -1,4 +1,3 @@
-from concourse.bass import DstId, RemoteDMATransfer
 from concourse.mybir import dt, AluOpType as OP, ActivationFunctionType as AF
 
 BIG = 2.0 ** 75
@@ -7,8 +6,6 @@ SEP = 64.0
 DIG = 2.0 ** 14
 R = 3
 WID = [2, 4, 8, 16, 32, 64, 128, 256]
-ZW = 384
-CUT = 44
 
 SCRATCH = {}
 PLACE = {}
@@ -27,21 +24,22 @@ def _part(name, cols, arena="ar"):
 
 
 for _n, _c in (("n16", 64), ("i17", 68), ("iot", 512), ("io4", 4), ("bff", 16), ("sgk", 48), ("rtab", 4), ("big", 256),
-               ("mh", 64), ("md", 256), ("mda", 64), ("c0", 68), ("c1", 68), ("c2", 68), ("n32", 64), ("iom", 512),
-               ("mk16", 64), ("mk32", 64), ("mk64", 64), ("ke", 160),
-               ("kk", 64), ("gm", 64), ("kd", 64), ("sm", 68), ("g5", 64), ("o5", 64), ("o6", 64), ("o7", 64), ("idw", 64),
+               ("mh", 64), ("md", 512), ("mda", 64), ("c0", 68), ("c1", 72), ("c2", 72), ("i18", 72), ("mk2", 72), ("kk2", 72), ("n32", 64), ("iom", 512),
+               ("mk16", 64), ("mk32", 64), ("mk64", 64), ("ke", 160), ("mp0", 64), ("gp", 64), ("gw", 64), ("gy", 68),
+               ("kk", 64), ("gm", 64), ("kd", 64), ("sm", 72), ("g5", 64), ("o5", 64), ("o6", 64), ("o7", 64), ("idw", 64),
                ("np5", 64), ("no6", 128), ("np6", 128), ("hh6", 64), ("id6", 64), ("lr5", 4), ("sh5", 4),
-               ("ap6", 16), ("sa", 64), ("sb", 64), ("m4", 64), ("nh7", 256), ("no7", 256), ("t7", 288), ("np7", 256), ("hh7", 64),
-               ("jk", 774), ("sum4", 4), ("ds", 64), ("ds6", 128), ("ds7", 256), ("qh", 32), ("qc", 32),
+               ("ap6", 16), ("sa", 64), ("sb", 64), ("m4", 64), ("nh7", 256), ("t7", 64), ("np7", 256), ("hh7", 64), ("hk7", 64), ("sc", 64), ("sd", 64),
+               ("jk", 774), ("sum4", 4), ("ds", 64), ("ds0", 64), ("ds6", 128), ("ds7", 256), ("qh", 32), ("qc", 32),
                ("posw", 512), ("pds", 512), ("lr", 20), ("tbf", 4)):
     _part(_n, _c)
 for _g in range(5):
     for _s in ("g%d", "o%d", "id%dr", "rst%d"):
         if (_s != "o%d" or _g) and (_s != "rst%d" or _g < 4):
-            _part(_s % _g, 64)
+            _part(_s % _g, 72 if _g == 2 and _s in ("g%d", "rst%d") else 64)
+_part("mq0", 64)
 for _g in range(3):
-    for _s, _c in (("mq%d", 64), ("ms%d", 68), ("t1%d", 64), ("t3%d", 68)):
-        _part(_s % _g, _c)
+    for _s, _c in (("ms%d", 68), ("t1%d", 64), ("t3%d", 68)):
+        _part(_s % _g, 72 if _g else _c)
 for _g in range(3, 8):
     _part("c%d" % _g, 4 * (WID[_g] + 2), "arb")
     if _g < 7:
@@ -54,7 +52,7 @@ for _r in range(R):
         _part(_s % _r, _c)
     _part("w7%d" % _r, 528, "arb")
     SCRATCH["dg%d" % _r] = ("dram", [5, 128, 4], "float32")
-for _n, _c in (("uo", 64), ("rk", 4), ("rr", 4), ("tb", 4), ("tbl4", 4), ("own7", 4), ("own6", 4), ("off", 32), ("pos", 32), ("pom", 32), ("sel", 2),
+for _n, _c in (("uo", 64), ("rk", 4), ("rk0", 4), ("rk1", 2), ("l17", 4), ("rr", 4), ("tb", 4), ("tbl4", 4), ("own7", 4), ("own6", 4), ("off", 32), ("pos", 32), ("pom", 32), ("sel", 2),
                ("tbl0", 4), ("tbl1", 4), ("tbl2", 4), ("tbl3", 4)):
     _part(_n, _c, "ar16")
 _buf("ar", _used["ar"])
@@ -71,11 +69,11 @@ for _b in range(4):
 for _b in range(2):
     _buf("f%d" % _b, 512)
     _buf("fs%d" % (_b + 2), 512)
-for _n, _c in (("pi", 1), ("bi", 16), ("uoi", 64), ("tbi", 4), ("pn", 32), ("pm", 32)):
+for _n, _c in (("pi", 1), ("bi", 16), ("uoi", 64), ("tbi", 16)):
     _buf(_n, _c, "int32")
-for _n, _c in (("xt", 2048), ("ut", 512), ("vt", 512), ("zt", 1024), ("ee0", 514), ("ee1", 514), ("ones", 520), ("zz", 512)):
+for _n, _c in (("xt", 2048), ("ut", 512), ("vt", 512), ("zt", 1024), ("ee0", 514), ("ee1", 514), ("ones", 520)):
     _buf(_n, _c, "bfloat16")
-for _n, _c in (("xq", 512), ("uq", 128), ("uc", 1024), ("vq", 128), ("wq", 512), ("zq", ZW), ("eq", 512)) + tuple(("zl%d" % r, ZW) for r in range(R)):
+for _n, _c in (("xq", 512), ("uq", 128), ("uc", 1024), ("vq", 128), ("wq", 512), ("zq", 256), ("eq", 512)) + tuple(("zl%d" % r, 256) for r in range(R)):
     _buf(_n, _c, "float8_e4m3fn_x4")
     _buf(_n + "s", _c, "uint8")
 for _b in range(8):
@@ -83,7 +81,8 @@ for _b in range(8):
 for _r in range(R):
     SEMAPHORES += [s % _r for s in ("aa%d", "ab%d", "lc%d", "dl%d", "dm%d", "dn%d", "db%d")]
     SEMAPHORES += ["dga%d%d" % (_r, g) for g in range(5)]
-OPT = {"sw0": "vsv", "np6": 3, "early": 1, "pa0": "s", "n0": 6}
+OPT = {"sw0": "vsv", "np6": 3, "early": 1, "pa0": "s", "n0": 8, "n1": 2, "k1": 1, "wa": 128, "send": "plain", "v6": 3, "id0": 1, "xq": "yyy", "vq": 0, "sa": 3, "np5": 2, "joint": 0}
+PRODUCTS = (((3,), (4,), (5,), (6,), (7,)), ((6,), (7,), (), (), ()))
 LAST = (0, 192, 384, 512)
 PIECES = ((0, 256), (256, 384), (384, 512))
 
@@ -112,6 +111,8 @@ def rank_program(g, core, T, topo):
     def v(name, c0=0, c1=None, st=1, p0=0, p1=128):
         name, at, cols = PLACE[name]
         c0, c1 = c0 + at, (cols if c1 is None else c1) + at
+        if st < 0:
+            return (name, p0, p1, c0, c1, T[name][p0:p1, c1 - 1:c0 - 1:-1], 1)
         ap = T[name][p0:p1, c0:c1] if st == 1 else T[name][p0:p1, c0:c1:st]
         return (name, p0, p1, c0, c1, ap, st)
 
@@ -234,11 +235,10 @@ def rank_program(g, core, T, topo):
     dma("y", "du", 1, v("ut"), ("u", 0, 128, 0, 512, T.u[:, :]))
     for i in range(3):
         a, b = 4 * PIECES[i][0], 4 * PIECES[i][1]
-        dma("y", "dx%d" % i, 1, v("xt", a, b), ("x", 0, 128, a, b, T.x[:, a:b]))
-    for B in range(8):
-        h = 16 * group_of(B)
-        dma("s", "dp", 8, v("tbi", 0, 4, 1, h, h + 16), ("p", 0, 16, 4 * B, 4 * B + 4, T.p[:, 4 * B:4 * B + 4]))
-    need("y", ("dp", 128))
+        dma(OPT["xq"][i], "dx%d" % i, 1, v("xt", a, b), ("x", 0, 128, a, b, T.x[:, a:b]))
+    for h in range(2):
+        dma("y", "dp", 2, v("tbi", 0, 16, 1, 16 * h, 16 * h + 16), ("p", 0, 16, 16 * h, 16 * h + 16, T.p[:, 16 * h:16 * h + 16]))
+    need("y", ("dp", 32))
     dma("y", "dv", 1, v("vt"), ("v", 0, 128, 0, 512, T.v[:, :]))
     dma("y", "dw", 2, cd("wq"), ("wc", 0, 128, 0, 2048, T.wc[:, :]))
     dma("y", "dw", 2, v("wqs"), ("ws", 0, 128, 0, 512, T.ws[:, :]))
@@ -253,7 +253,10 @@ def rank_program(g, core, T, topo):
         return v("sgk", 0, 1, 1, a, b)
 
     def starts(k):
-        select(v("rst%d" % k), v("big", 0, 64), [[0, 64 // WID[k]], [1, WID[k]]], -BIG)
+        if k == 2:
+            select(v("rst2"), v("big", 0, 72), [[0, 8], [1, 9]], -BIG, -1)
+        else:
+            select(v("rst%d" % k), v("big", 0, 64), [[0, 64 // WID[k]], [1, WID[k]]], -BIG)
 
     def counts(k):
         s = WID[k] + 2
@@ -286,10 +289,12 @@ def rank_program(g, core, T, topo):
     iota(v("io4"), [[16, 4]])
     iota(v("i17"), [[0, 4], [1, 17]])
     iota(v("uoi"), [[16, 8], [0, 8]])
+    iota(v("i18"), [[0, 4], [1, 18]])
     starts(0)
     starts(3)
     iota(v("iot"), [[1, 512]])
     starts(1)
+    iota(v("c1", 17, 72, 18), [[int(2 * SEP), 4]])
     iota(v("n32"), [[0, 2], [1, 32]])
     starts(2)
     for b in range(2):
@@ -301,13 +306,12 @@ def rank_program(g, core, T, topo):
     windows(0)
     counts(7)
     select(v("m4"), v("ones", 0, 64), [[0, 16], [1, 4]], 0.0, cmp=OP.not_equal)
-    iota(v("zz"), [[0, 512]])
     iota(v("iom"), [[1, 512]], -256)
     windows(1)
     windows(2)
 
     q = v("bff", 0, 1)
-    dsc, q1, nq2, bq, bm, e6, e7, e7c, bk, q63, g7, g32, dsl = [newcol() for _ in range(13)]
+    dsc, q1, nq2, bq, bm, e6, e7, e7c, bk, q63, g7, g32, dsl, e2, dsr = [newcol() for _ in range(15)]
     bit = {k: v("bff", c, c + 1) for k, c in ((0, 1), (1, 2), (2, 3), (6, 4), (5, 5), (7, 6))}
     th = {k: newcol() for k in bit}
     lo = {0: v("bff", 7, 8), 1: v("bff", 8, 9), 2: bit[2]}
@@ -324,35 +328,44 @@ def rank_program(g, core, T, topo):
     def ends():
         for k in range(2):
             lin(cols[k][2], lo[k + 1], 2.0, 2.0 * WID[k])
-        lin(cols[2][3], lo[2], -1.0, 2.0 * WID[2])
+        lin(cols[2][3], lo[2], -9.0 / 8, 17.0)
         for k in range(2):
             lin(cols[k][3], lo[k], -1.0, cols[k][2])
 
     def partner(k):
-        rw = cols[k][3]
-        ts(v("ms%d" % k), v("i17"), rw, OP.subtract, -float(WID[k]), OP.not_equal)
-        ts(v("t3%d" % k), v("i17"), rw, OP.is_equal, SEP - 1.0, OP.mult)
+        rw, i = cols[k][3], v("i18" if k else "i17")
+        ts(v("ms%d" % k), i, rw, OP.subtract, -float(WID[k]), OP.not_equal)
+        ts(v("t3%d" % k), i, rw, OP.is_equal, SEP - 1.0, OP.mult)
 
-    def masks(k):
-        nm, hb, d2, rw, nb = cols[k]
-        m = MASK[k]
-        lin(nm, lo[k], -0.5, nq2)
-        lin(hb, lo[k], BIG / 2, bq)
-        lin(nb, bit[k], -SEP, 0.0)
-        lin(th[k], bit[k], -EPS / m, 0.0)
-        lin(v("t1%d" % k), v("n16"), 1.0, nm, AF.Abs)
-        lin(v("c%d" % k, 16, 68, 17), v("rtab"), SEP, nb)
-        lin(v("mq%d" % k), v("t1%d" % k), BIG, hb)
+    def side(k):
+        if k < 7:
+            lin(th[k], bit[k], -EPS / MASK[k], 0.0)
+        else:
+            lin(th[k], bit[k], EPS / MASK[k], -EPS)
 
-    MASK = {0: 2, 1: 4, 2: 8, 5: 64, 6: 32, 7: 16}
+    MASK = {0: 2, 1: 4, 5: 64, 6: 32, 7: 16}
+    bl, bp, xl, b1, b2 = [newcol() for _ in range(5)]
+    lin(bm, q, -BIG, -BIG / 2)
+    lin(bl, lo[0], BIG, -BIG / 2)
     ends()
-    lin(nq2, q, -0.5, 0.0)
-    lin(bq, q, -BIG / 2, -BIG / 4)
-    ts(e6, bit[5], q, OP.add)
+    lin(v("mh"), v("n16"), BIG, bm)
+    lin(v("t10"), v("n16"), -BIG, bl)
+    lin(bp, cols[0][3], -1.0, 1.5)
+    side(0)
+    lin(bk, q, -BIG, 15.5 * BIG)
+    lin(v("t11", 0, 64), v("n16"), 1.0, bp, AF.Abs)
+    ts(v("c0", 16, 68, 17), v("rtab"), bit[0], OP.subtract, SEP, OP.mult)
     tt(v("md", 0, 64), v("md", 0, 64), v("mda"))
-    ts(e7, bit[6], 4.0, OP.mult, e6, OP.add)
     partner(0)
-    masks(0)
+    spare = []
+
+    def later(f, *a):
+        spare.append((f, a))
+
+    def fit(n):
+        for f, a in spare[:n]:
+            f(*a)
+        del spare[:n]
 
     def upick(a, b):
         o, w, f = v("uc", 128 * a, 128 * b), v("uq"), v("uo", 8 * a, 8 * b)
@@ -365,22 +378,43 @@ def rank_program(g, core, T, topo):
 
     quant(v("uq"), v("uqs"), v("ut"))
     partner(1)
-    partner(2)
     upick(0, 2)
-    ts(e7c, e7, 48.0, OP.add)
-    for k in range(3):
+    tt(v("mq0"), v("mh"), v("t10"), OP.max)
+    ts(v("l17"), v("i17", 0, 4), 17.0, OP.mult, q, OP.add)
+    for k in range(2):
         tt(v("ms%d" % k), v("ms%d" % k), v("t3%d" % k))
-    masks(1)
-
-    def backs():
-        lin(bk, q, -BIG, 15.5 * BIG)
-        lin(bm, q, -BIG, -BIG / 2)
-        lin(q63, q, -1.0, 63.0)
-        for k in (5, 6, 7):
-            lin(th[k], bit[k], -EPS / MASK[k], 0.0)
-        lin(v("mh"), v("n16"), BIG, bm)
-        for n, src in (("mk16", v("n16")), ("mk32", v("n32")), ("mk64", v("iot", 0, 64))):
-            lin(v(n), src, -BIG, bk)
+    lin(v("mp0"), v("t11", 0, 64), BIG, -0.75 * BIG)
+    side(1)
+    lin(e2, bit[2], 0.125, 1.0)
+    zero = v("i17", 0, 68, 17)
+    xr, xe, n2, q15 = [newcol() for _ in range(4)]
+    lin(xl, bit[2], -BIG / 8, BIG)
+    lin(xr, bit[2], BIG / 8, 0.0)
+    lin(b2, bit[2], BIG / 4, -BIG)
+    lin(n2, bit[2], -SEP, 0.0)
+    lin(b1, xl, 1.0, bk)
+    lin(xe, xl, 1.0, -EPS)
+    lin(v("g2", 9, 72, 18), zero, 1.0, xr)
+    lin(v("c2", 17, 72, 18), v("rtab"), SEP, n2)
+    lin(v("mk2"), v("i18"), -BIG, b1)
+    lin(v("g2", 0, 72, 18), zero, 1.0, xe)
+    later(lin, v("mk2", 17, 72, 18), zero, 1.0, b2)
+    later(lin, q63, q, -1.0, 63.0)
+    later(lin, v("mk16"), v("n16"), -BIG, bk)
+    later(lin, v("mk32"), v("n32"), -BIG, bk)
+    later(lin, v("mk64"), v("iot", 0, 64), -BIG, bk)
+    later(side, 5)
+    later(lin, e6, bit[5], 1.0, q)
+    later(lin, q15, q, -1.0, 15.0)
+    later(lin, dsr, q, -1.0, 1.0, AF.Relu)
+    later(act, v("md", 64, 128), v("md", 0, 64))
+    later(lin, e7c, bit[5], 1.0, q15)
+    later(lin, dsr, dsr, 1.0 - 1.0 / DIG, 1.0 / DIG)
+    later(side, 6)
+    later(act, v("md", 128, 256), v("md", 0, 128))
+    later(lin, e7, bit[6], 4.0, e7c)
+    later(side, 7)
+    later(lin, e7c, e7, 1.0, 48.0)
 
     def compact(name, c0, c1, p0=0, p1=128):
         return v(name, c0 + 15, c1, 16, p0, p1)
@@ -423,25 +457,30 @@ def rank_program(g, core, T, topo):
         for i, (a, b) in enumerate(PIECES):
             quantx(i)
             score(0, "b%d" % (4 + i), a, b)
+            if r == 0 and i == 1:
+                upick(2, 4)
+
+        if r:
+            ts(v("tb"), v("tbf"), 256.0, OP.add)
+        ts(v("sw0", 0, 256), v("b4", 0, 256), -1.0, OP.mult)
+        act(v("sw0", 256, 384), v("b5", 0, 128), -1.0)
         if r == 0:
-            copy(v("tb"), v("tbi"))
-        for i, (a, b) in enumerate(PIECES):
-            if OPT["sw0"][i] == "v":
-                ts(v("sw0", a, b), v("b%d" % (4 + i), 0, b - a), -1.0, OP.mult)
-            else:
-                act(v("sw0", a, b), v("b%d" % (4 + i), 0, b - a), -1.0)
+            for a in range(4):
+                c = 4 * (2 * (a % 2) + a // 2)
+                copy(quad("tb", 0, 4, a), quad("tbi", c, c + 4, 0))
+        ts(v("sw0", 384, 512), v("b6", 0, 128), -1.0, OP.mult)
         score(1, sbank(1))
         if r == 0:
-            upick(2, 3)
+            partner(2)
         ttg(v("gm"), v("sw0"), v("tb"), v("mq0"), OP.max)
         sgather(v("g0"), v("sw0"), v("tb"))
         for k in range(2, 3 if r == 0 else 6):
             score(k, sbank(k))
         scored(1)
-        if r == 0:
-            sgather(v("id0r"), v("iot"), v("tb"))
         sgather(v("o1"), v("sw1"), v("tb"))
         scored(2)
+        sgather(v("id0r"), v("iot"), v("tb"))
+        sgather(v("o2"), v("sw2"), v("tb"))
 
         def ids(k):
             return "idw" if k == 5 else "id%dr" % k
@@ -450,12 +489,16 @@ def rank_program(g, core, T, topo):
             tab = "tbl%d" % k
             ts(v(tab), compact("ds", 0, 64), dsc, OP.mult)
             sgather(v("o%d" % (k + 2)), v("sw%d" % (k + 2)), v(tab))
-            act(v("lr", 4 * k, 4 * k + 4), compact("ds", 0, 64))
+            listed(k)
+
+        def listed(k, ds="ds"):
+            act(v("lr", 4 * k, 4 * k + 4), compact(ds, 0, 64))
             dma("y", "dga%d%d" % (r, k), 1, ("dg%d" % r, 0, 128, k, k + 1, dg[k]), v("lr", 4 * k, 4 * k + 4))
 
         def run(k):
             s = WID[k] + 2
-            scan(v("smb", 0, 4 * s), v("msk%d" % k), v("c%d" % k), 0.0, OP.add, OP.mult)
+            for a, b in ((0, 3 * s), (3 * s, 4 * s)) if k == 5 else ((0, 4 * s),):
+                scan(v("smb", a, b), v("msk%d" % k, a, b), v("c%d" % k, a, b), 0.0, OP.add, OP.mult)
             return v("smb", s - 2, 4 * s, s)
 
         def keys(out, m, row):
@@ -468,20 +511,29 @@ def rank_program(g, core, T, topo):
             if k == 0:
                 keys(v("kd"), v("rst3"), v("gm"))
                 keys(v("kk"), v("rst0"), G)
-            elif k < 3:
-                tt(v("gm"), G, v("mq%d" % k), OP.max)
-                keys(v("kk"), v("rst%d" % k), G)
+                if r == 0:
+                    tt(v("ms2"), v("ms2"), v("t32"))
+            elif k == 1:
+                for c in range(0, 64, 16):
+                    runmin(v("kd", c, c + 16), v("gm", c, c + 16), v("gw", c, c + 16))
+                keys(v("kk"), v("rst1"), G)
+                ts(v("c1", 16, 72, 18), v("rk0"), bit[1], OP.subtract, SEP, OP.mult)
+                ts(v("rk1"), v("rk0", 2, 4), -32.0, OP.add)
+            elif k == 2:
+                keys(v("ke", 0, 72), v("mk2"), v("g2", 0, 72, -1))
+                keys(v("kk2"), v("rst2"), G)
                 diag(v("ds"), ids(k), 0, 64)
-                keys(v("kd"), v("rst3"), v("gm"))
-                table(k - 1)
             else:
                 keys(v("kd"), v("mk16"), G)
                 if k == 4:
                     keys(v("kk"), v("mk32"), G)
                 diag(v("ds"), ids(k), 0, 64)
-            s = 17 if k < 3 else w + 2
+            s = 17 if k == 0 else 18 if k < 3 else w + 2
             for c in range(4):
-                if k < 3:
+                if k == 2:
+                    a = 54 - 18 * c
+                    ts(v(C, s * c, s * c + 17), v("kk2", s * c + 1, s * c + 18), v("ke", a + 8, a + 9), OP.subtract, v("ke", a + 17, a + 18), OP.is_gt)
+                elif k < 3:
                     x = v("kd", 16 * c + 15, 16 * c + 16)
                     ts(v(C, s * c, s * c + 16), v("kk", 16 * c, 16 * c + 16), x, OP.subtract, th[k], OP.is_gt)
                 else:
@@ -489,68 +541,65 @@ def rank_program(g, core, T, topo):
                     a = 48 - 16 * (c ^ 1) if k == 3 else 32 - 32 * left
                     x = v("kd", 63 - 16 * c, 64 - 16 * c) if k == 3 or c % 2 == 0 else v("kk", 79 - 16 * c, 80 - 16 * c)
                     ts(v(C, s * c, s * c + w), v("g%d" % k, a, a + w), x, OP.is_gt if left else OP.is_ge)
-            if k > 2:
+            if k > 1:
                 table(k - 1)
-            if r == 0 and k < 2:
-                upick(3 + 3 * k, 4 + 3 * k)
-            if r == 0 and k in (2, 3):
-                units(2 * k - 4)
-            if k < 3:
+            if r == 0 and k > 1:
+                units(k - 2)
+            if k == 0:
+                ttg(v("gp"), v("sw1"), v("tb"), v("mp0"), OP.max)
+                scan(v("sm", 0, 68), v("ms0"), v(C), 0.0, OP.mult, OP.add)
+                ts(v("gy"), v(C), -2 * BIG, OP.mult, BIG, OP.add)
+                ttg(v("gw"), v("sw1"), v("tb"), v("mq0"), OP.max)
+                ts(v("rk0"), v("sm", 16, 68, 17), 1.0 / SEP, OP.mult)
+                ttg(v("gm"), v("gy"), v("l17"), v("gp"), OP.max)
+                scatter(v("g1"), v("rk0"), v("o1"))
+            elif k < 3:
+                if k == 1:
+                    scatter(v("id1r", 0, 32), v("rk0", 0, 2), v("id0r", 0, 32))
                 scan(v("sm"), v("ms%d" % k), v(C), 0.0, OP.mult, OP.add)
-                if r == 0 and k < 2:
-                    upick(4 + 3 * k, 5 + 3 * k)
+                if k == 1:
+                    scatter(v("id1r", 32, 64), v("rk1"), v("id0r", 32, 64))
                 if r == 0 and k == 2:
-                    units(1)
-                if k == 2:
-                    ts(v("rr"), v("sm", 16, 68, 17), -1.0 / SEP, OP.mult, 63.0, OP.add)
-                ts(v("rk"), v("sm", 16, 68, 17), 1.0 / SEP, OP.mult)
-                if r == 0 and k == 0:
                     upick(5, 6)
+                if k == 2:
+                    ts(v("rr"), v("sm", 17, 72, 18), -1.0 / SEP, OP.mult, 63.0, OP.add)
+                else:
+                    ts(v("rr"), v("sm", 17, 72, 18), 1.0 / SEP, OP.mult, e2, OP.add)
+                ts(v("rk"), v("sm", 15 + k, 72, 18), 1.0 / SEP, OP.mult)
+                if r == 0 and k == 1:
+                    upick(4, 5)
             else:
                 n = run(k)
-                if r == 0 and k == 3:
-                    units(3)
+                if r == 0:
+                    upick(k + 3, k + 4)
                 ts(v("rr"), n, -1.0, OP.mult, q63, OP.add)
                 ts(v("rk"), n, q, OP.add)
-            scatter(v("g%d" % (k + 1)), v("rk" if k < 2 else "rr"), v("o%d" % (k + 1)))
-            scatter(v(ids(k + 1)), v("rk"), v(ids(k)))
-            if k == 0:
-                if r == 0:
-                    masks(2)
-                    for j in (3, 4, 5):
-                        score(j, sbank(j))
-                else:
-                    score(6, sbank(6))
-                scored(3)
-            elif k == 1:
-                if r == 0:
-                    score(6, sbank(6))
-                    act(v("md", 64, 128), v("md", 0, 64))
-                    backs()
-                    act(v("md", 128, 256), v("md", 0, 128))
-                score(7, sbank(7))
-                scored(4)
-                scored(5)
-            elif k == 2:
-                unpack(0)
-                unpack(1)
-                scored(6)
-                scored(7)
-            elif k == 3:
-                unpack(2)
-                unpack(3)
-                half(0)
-                whole(0)
+                if k == 3:
+                    diag(v("ds0"), "id1r", 0, 64)
+                    listed(0, "ds0")
+                if r == 0 and k == 4:
+                    units(3)
+            if k:
+                scatter(v("g%d" % (k + 1)), v("rr"), v("o%d" % (k + 1)))
+                scatter(v(ids(k + 1)), v("rk"), v(ids(k if k > 1 else 0)))
+            fit((3, 6, 4, 4, 0)[k])
+            for j in PRODUCTS[r > 0][k]:
+                score(j, sbank(j))
+            for b in range(4) if k == (2 if r else 4) else ():
+                unpack(b)
+            if k < 4:
+                scored(k + 3)
 
         def versus(k, c):
             w = WID[k]
             s = w + 2
-            e = ENDS[c] if k == 5 else 16 * c + 16
+            e = ENDS[c] if k == 5 else 16 * (c ^ 2 if k == 7 else c) + 16
             ts(v("c%d" % k, s * c, s * c + w), v("np%d" % k), v("ke" if k == 5 else "hh%d" % k, e - 1, e), OP.subtract, th[k], OP.is_gt)
 
         ENDS = (16, 48, 96, 160)
         for a in (0, 1):
-            act(hf("np5", 0, 64, a), hf("g5", 0, 64, 1 - a))
+            (act if a < OPT["np5"] else copy)(hf("np5", 0, 64, a), hf("g5", 0, 64, 1 - a))
+        scored(7)
         for c in range(4):
             n = 16 * c + 16
             keys(v("ke", ENDS[c] - n, ENDS[c]), v("mk64", 0, n), v("g5", 64 - n, 64))
@@ -558,7 +607,7 @@ def rank_program(g, core, T, topo):
         for c in range(4):
             versus(5, c)
         table(4)
-        half(1)
+        half(0)
         if r == 0:
             ts(g7, v("pi"), 112.0, OP.is_ge, 256.0, OP.mult)
             ts(g32, v("pi"), 112.0, OP.is_ge, 32.0, OP.mult)
@@ -577,67 +626,76 @@ def rank_program(g, core, T, topo):
         diag(v("ds6"), "w5%d" % r, 0, 128)
         for a in (0, 1):
             act(hf("sh5", 0, 4, a), compact("ds6", 64 * a, 64 * a + 64, 64 - 64 * a, 128 - 64 * a))
-        for c in range(2):
+        for c in range(3):
             versus(6, c)
         for a in (0, 1):
             tt(hf("lr5", 0, 4, a), compact("ds6", 64 * a, 64 * a + 64, 64 * a, 64 * a + 64), hf("sh5", 0, 4, a))
-        for c in range(2, 4):
-            versus(6, c)
+        versus(6, 3)
+        scan(v("smb", 0, 260), v("msk6", 0, 260), v("c6", 0, 260), 0.0, OP.mult, OP.add)
         ts(v("own6"), v("lr5"), dsc, OP.mult)
         sgather(v("o7"), v("sw7"), v("own6"))
         sgather(v("id6"), v("iot"), v("own6"))
-        whole(1)
+        half(1)
         for B in range(8):
             h, c = 16 * group_of(B), 4 * B
             dma("y", "dl%d" % r, 8, v(lst, c, c + 4, 1, 0, 80), ("dg%d" % r, h, h + 16, 0, 5, dg[0:5, h:h + 16, :]))
         for B in range(8):
             h, c = 16 * group_of(B), 4 * B
             dma("y", "dm%d" % r, 8, v(lst, c, c + 4, 1, 80, 96), v("lr5", 0, 4, 1, h, h + 16))
-        for c0, c1 in ((0, 390), (390, 520)):
-            scan(v("smb", c0, c1), v("msk6", c0, c1), v("c6", c0, c1), 0.0, OP.mult, OP.add)
+        for c in (260, 390):
+            scan(v("smb", c, c + 130), v("msk6", c, c + 130), v("c6", c, c + 130), 0.0, OP.mult, OP.add)
         ts(v("rk"), v("smb", 128, 520, 130), e6, OP.add)
         scatter(v("w6s%d" % r), v("rk"), v("o7"))
         scatter(v("w6%d" % r), v("rk"), v("id6"))
         runmin(hf("nh7", 0, 256, 0), hf("w6s%d" % r, 0, 256, 0), hf("w6s%d" % r, 0, 256, 1))
         half(2)
-        runmin(quad("no7", 0, 256, 0), quad("nh7", 0, 256, 0), quad("nh7", 0, 256, 1))
-        trans(quad("t7", 0, 256, 0), quad("no7", 0, 256, 0))
-        trans(quad("t7", 256, 288, 0), quad("no7", 0, 32, 0))
+        runmin(quad("np7", 0, 256, 0), quad("nh7", 0, 256, 0), quad("nh7", 0, 256, 1))
+        for a in range(1, 4 - OPT["vq"]):
+            act(quad("np7", 0, 256, a), quad("np7", 0, 256, 0))
         for a in range(4):
             c = 64 * (2 * (a % 2) + a // 2)
-            hold(quad("hh7", 0, 64, a), quad("mh", 0, 64, 0), quad("no7", c, c + 64, 0))
-        for a in range(3):
-            trans(quad("np7", 0, 256, a), quad("t7", 16, 272, 0))
-            if a == 0:
-                act(quad("np7", 0, 256, 3), quad("np7", 0, 256, 0))
-        diag(v("ds7"), "w6%d" % r, 0, 256)
+            hold(quad("hk7", 0, 64, a), quad("mh", 0, 64, 0), quad("np7", c, c + 64, 0))
+        diag(v("ds7", 0, 128), "w6%d" % r, 0, 128)
+        trans(v("t7"), v("hk7"))
+        diag(v("ds7", 128, 256), "w6%d" % r, 128, 256)
+        if OPT["vq"] == 1:
+            copy(quad("np7", 0, 256, 3), quad("np7", 0, 256, 0))
+        if OPT["vq"] == 2:
+            copy(hf("np7", 0, 256, 1), hf("np7", 0, 256, 0))
+        trans(v("hh7"), v("t7", 0, 64, -1))
         for a in range(4):
-            act(v("sa", a, 64, 4, 0, 32), compact("ds7", 0, 256, 32 * a, 32 * a + 32))
+            (act if a < OPT["sa"] else copy)(v("sa", a, 64, 4, 0, 32), compact("ds7", 0, 256, 32 * a, 32 * a + 32))
 
         def count7(c):
             accum(v("jk", 258 * c, 258 * c + 257), v("c7", 258 * c, 258 * c + 257), v("sum4", c, c + 1))
 
         versus(7, 0)
+        scan(quad("sb", 0, 64, 0), quad("m4", 0, 64, 0), quad("sa", 0, 64, 0), 0.0, OP.mult, OP.add)
         count7(0)
+        act(quad("ap6", 0, 16, 0), v("sb", 3, 64, 4, 0, 32))
         versus(7, 1)
+        trans(quad("sc", 0, 64, 0), quad("sb", 0, 64, 0))
         count7(1)
         versus(7, 2)
-        scan(quad("sb", 0, 64, 0), quad("m4", 0, 64, 0), quad("sa", 0, 64, 0), 0.0, OP.mult, OP.add)
-        act(quad("ap6", 0, 16, 0), v("sb", 3, 64, 4, 0, 32))
+        trans(quad("sd", 0, 64, 0), v("sc", 0, 64, -1, 0, 32))
         count7(2)
-        versus(7, 3)
+        for c in (0, 128):
+            ts(v("c7", 774 + c, 902 + c), v("np7", c, c + 128), v("hh7", 31, 32), OP.subtract, th[7], OP.is_gt)
+        accum(v("jk", 0, 128), v("c7", 774, 902), v("sum4", 3, 4))
         for a in range(4):
-            c = 16 * (2 * (a % 2) + a // 2)
-            ts(quad("own7", 0, 4, a), v("sb", c + 3, c + 16, 4, 0, 32), dscp(0, 32), OP.mult)
-        scan(v("smb", 0, 256), v("ones", 0, 256), v("c7", 774, 1030), 0.0, OP.mult, OP.add)
+            c = 16 * (2 * (a % 2) + a // 2) ^ 32
+            ts(quad("own7", 0, 4, a), v("sd", c + 3, c + 16, 4, 0, 32), (dsr[0], 0, 32) + dsr[3:5] + (T[dsr[0]][0:32, dsr[3]:dsr[4]], 1), OP.mult)
+        scan(v("smb", 0, 128), v("ones", 0, 128), v("c7", 902, 1030), 0.0, OP.mult, OP.add)
         sgather(v("id7"), v("iom"), v("own7"))
         for j in range(2):
             dma("y", "dn%d" % r, 2, v(lst, 16 * j, 16 * j + 16, 1, 96, 112), v("ap6", 0, 16, 1, 16 * j, 16 * j + 16))
         half(3)
-        ts(v("rk", 3, 4), v("smb", 255, 256), e7c, OP.add)
-        ts(v("rk", 0, 3), v("sum4", 0, 3), e7, OP.add)
+        whole(0)
+        whole(1)
         if r == 0:
-            quant(v("zq", 128, 256), v("zqs", 128, 256), v("zz"))
+            act(v("md", 256, 512), v("md", 0, 256))
+        ts(v("rk", 3, 4), v("smb", 127, 128), v("sum4", 3, 4), OP.add, e7c, OP.add)
+        ts(v("rk", 0, 3), v("sum4", 0, 3), e7, OP.add)
         scatter(v("w7%d" % r, 16, 528), v("rk"), v("id7"))
         trans(v("tz", 0, 512), v("w7%d" % r, 0, 512))
         trans(v("tz", 512, 1024), v("w7%d" % r, 16, 528))
@@ -654,46 +712,45 @@ def rank_program(g, core, T, topo):
 
         rid, pid, _s = topo.addr(nxt)
         eng = topo.engines(core, nxt)
-        ways = [eng[i::4] for i in range(4)]
-        n_eng = len(eng)
+        ways = (eng[0::2], eng[1::2])
+        loc = "lc%d" % r
+        joint = r == 0 and OPT["joint"]
+        total[loc] = len(ways[0]) * (3 if joint else 4)
 
         def pair(j, b):
             c = 128 * j
             ttg(v("zt", 4 * c + b, 4 * c + 512, 4), v("fh%d" % b), v("off", 16 + 8 * j, 24 + 8 * j), v("pa%d" % b, c, c + 128))
 
+        def inverse(n):
+            scatter(v("posw"), v("off", done[0], done[0] + n), v("iot", 16 * done[0], 16 * (done[0] + n)))
+            done[0] += n
+
+        done = [0]
         for j in range(2):
-            for b in (1, 2, 3) if j == 0 and OPT["pa0"] == "v" else range(4):
+            for b in range(4):
                 sgather(v("pa%d" % b, 128 * j, 128 * j + 128), v("fh%d" % b), v("off", 8 * j, 8 * j + 8))
-        if OPT["pa0"] == "v":
-            vgather(v("pa0", 0, 128), v("fh0"), v("off", 0, 8))
-            n0 = 0
-        else:
-            n0 = OPT["n0"]
-            scatter(v("posw"), v("off", 0, n0), v("iot", 0, 16 * n0))
+        inverse(OPT["n0"])
         for j in range(2):
             c = 128 * j
-            for b in ((1, 0, 2, 3) if n0 == 0 else range(4)) if j == 0 else (1, 2, 3):
+            for b in range(j, 4):
                 pair(j, b)
             if j == 0:
                 pair(1, 0)
             else:
-                scatter(v("posw"), v("off", n0, n0 + 4), v("iot", 16 * n0, 16 * n0 + 64))
-            quant(v("zq", 2 * c, 2 * c + 128), v("zqs", 2 * c, 2 * c + 128), v("zt", 4 * c, 4 * c + 512))
-            sem, loc = ("aa%d", "ab%d")[j] % r, "lc%d" % r
-            a, b = (0, 0) if j == 0 else (ZW - 3 * CUT, ZW - 4 * CUT)
-            parts = [(cd("zq", a + CUT * i, a + CUT * i + CUT), cd("zl%d" % r, a + CUT * i, a + CUT * i + CUT)) for i in range(3)]
-            parts.append((v("zqs", b, b + 4 * CUT), v("zl%ds" % r, b, b + 4 * CUT)))
-            deps("g", [src for src, land in parts], [])
-            g.remote_dma_fused([RemoteDMATransfer(dst_ids=[DstId(rid=rid, pnc=pid)], dma_engine_mask=sum(1 << e for e in es),
-                                                  remote_sem=T.sem[sem], src=src[5], dst=land[5])
-                                for (src, land), es in zip(parts, ways)], local_sem=T.sem[loc])
-            note("g", (loc, 2 * n_eng), [src for src, land in parts], [])
-            note("x", (sem, n_eng), [], [land for src, land in parts])
-            total[sem] = n_eng
-            total[loc] = 2 * n_eng
-        if r < R - 1:
-            ts(v("tb"), v("tbf"), 256.0, OP.add)
-        scatter(v("posw"), v("off", n0 + 4, 32), v("iot", 16 * n0 + 64, 512))
+                inverse(OPT["n1"])
+            quant(v("zq", c, c + 128), v("zqs", c, c + 128), v("zt", 4 * c, 4 * c + 512))
+            sem = ("aa%d", "ab%d")[j] % r
+            parts = [(cd("zq", c, c + 128), cd("zl%d" % r, c, c + 128))]
+            if j or not joint:
+                a = 0 if joint else c
+                parts.append((v("zqs", a, c + 128), v("zl%ds" % r, a, c + 128)))
+            total[sem] = len(ways[0]) * len(parts)
+            for (src, land), es in zip(parts, ways):
+                deps("g", [src], [])
+                g.remote_dma(land[5], src[5], T.sem[sem], T.sem[loc], pid, rid, sum(1 << e for e in es))
+                note("g", (loc, total[loc]), [src], [])
+                note("x", (sem, total[sem]), [], [land])
+        inverse(32 - done[0])
         for b in (2, 3):
             sgather(v("fs%d" % b), v("fh%d" % b), v("off"), 64.0)
 
@@ -701,7 +758,7 @@ def rank_program(g, core, T, topo):
             c = 128 * j
             for b in (2, 0, 3, 1):
                 mm(v("b%d" % (4 * j + b), 0, 128), v("wq", 128 * b, 128 * b + 128), v("wqs", 128 * b, 128 * b + 128),
-                   v("zl%d" % r, 2 * c, 2 * c + 128), v("zl%ds" % r, 2 * c, 2 * c + 128))
+                   v("zl%d" % r, c, c + 128), v("zl%ds" % r, c, c + 128))
             for b in range(2):
                 for a in (c, c + 256):
                     act(v("pp%d" % b, a, a + 128), v("b%d" % (4 * j + b), 0, 128), 0.03125)
@@ -711,18 +768,15 @@ def rank_program(g, core, T, topo):
                 tt(v("pp%d" % b, a, a + 128), v("b%d" % (4 * j + b), 0, 128), v("fs%d" % b, a, a + 128))
 
         early = r > 0 and OPT["early"]
-        if r < R - 1:
-            sgather(v("id0r"), v("iot"), v("tb"))
-        layer(0)
         if r == R - 1:
             sgather(v("row"), v("iot"), v("off"))
             dma("y", "dod", 1, ("od", 0, 8, 0, 512, T.od[:, :]), ("row", 0, 128, 0, 512, T.row[0:128:16, :]))
+        layer(0)
         if r == 0:
             quant(v("vq"), v("vqs"), v("vt"))
         if early:
             plus(0, 2)
-        for c in (0, 256):
-            diag(v("pds", c, c + 256), "posw", c, c + 256)
+        diag(v("pds"), "posw", 0, 512)
         if early:
             plus(0, 3)
         ts(v("pos"), v("pds", 15, 512, 16), dsc, OP.mult)

from concourse.mybir import dt, AluOpType as OP, ActivationFunctionType as AF

BIG = 2.0 ** 75
EPS = 2.0 ** -120
SEP = 64.0
DIG = 2.0 ** 14
R = 3
WID = [2, 4, 8, 16, 32, 64, 128, 256]

SCRATCH = {}
PLACE = {}
_used = {"ar": 0, "ar16": 0, "arb": 0}
SEMAPHORES = ["sv", "ss", "sp", "sg", "dx0", "dx1", "dx2", "du", "dv", "dp", "dw", "doc", "dos", "dod", "dy"]


def _buf(name, cols, dtype="float32", where="sbuf"):
    SCRATCH[name] = (where, [128, cols], dtype)
    PLACE[name] = (name, 0, cols)


def _part(name, cols, arena="ar"):
    PLACE[name] = (arena, _used[arena], cols)
    _used[arena] += -(-cols // 16) * 16


for _n, _c in (("n16", 64), ("i17", 68), ("iot", 512), ("io4", 4), ("bff", 16), ("sgk", 48), ("rtab", 4), ("big", 256),
               ("mh", 64), ("md", 512), ("mda", 64), ("c0", 68), ("c1", 72), ("c2", 72), ("i18", 72), ("mk2", 72), ("kk2", 72), ("n32", 64), ("iom", 512),
               ("mk16", 64), ("mk32", 64), ("mk64", 64), ("ke", 160), ("mp0", 64), ("gp", 64), ("gw", 64), ("gy", 68),
               ("kk", 64), ("gm", 64), ("kd", 64), ("sm", 72), ("g5", 64), ("o5", 64), ("o6", 64), ("o7", 64), ("idw", 64),
               ("np5", 64), ("no6", 128), ("np6", 128), ("hh6", 64), ("id6", 64), ("lr5", 4), ("sh5", 4),
               ("ap6", 16), ("sa", 64), ("sb", 64), ("m4", 64), ("nh7", 256), ("t7", 64), ("np7", 256), ("hh7", 64), ("hk7", 64), ("sc", 64), ("sd", 64),
               ("jk", 774), ("sum4", 4), ("ds", 64), ("ds0", 64), ("ds6", 128), ("ds7", 256), ("qh", 32), ("qc", 32),
               ("posw", 512), ("pds", 512), ("lr", 20), ("tbf", 4)):
    _part(_n, _c)
for _g in range(5):
    for _s in ("g%d", "o%d", "id%dr", "rst%d"):
        if (_s != "o%d" or _g) and (_s != "rst%d" or _g < 4):
            _part(_s % _g, 72 if _g == 2 and _s in ("g%d", "rst%d") else 64)
_part("mq0", 64)
for _g in range(3):
    for _s, _c in (("ms%d", 68), ("t1%d", 64), ("t3%d", 68)):
        _part(_s % _g, 72 if _g else _c)
for _g in range(3, 8):
    _part("c%d" % _g, 4 * (WID[_g] + 2), "arb")
    if _g < 7:
        _part("msk%d" % _g, 4 * (WID[_g] + 2), "arb")
for _n, _c in (("smb", 520), ("id7", 64), ("tz", 1024)):
    _part(_n, _c, "arb")
for _r in range(R):
    _part("list%d" % _r, 64)
    for _s, _c in (("w5s%d", 128), ("w5%d", 128), ("w6s%d", 256), ("w6%d", 256)):
        _part(_s % _r, _c)
    _part("w7%d" % _r, 528, "arb")
    SCRATCH["dg%d" % _r] = ("dram", [5, 128, 4], "float32")
for _n, _c in (("uo", 64), ("rk", 4), ("rk0", 4), ("rk1", 2), ("l17", 4), ("rr", 4), ("tb", 4), ("tbl4", 4), ("own7", 4), ("own6", 4), ("off", 32), ("pos", 32), ("pom", 32), ("sel", 2),
               ("tbl0", 4), ("tbl1", 4), ("tbl2", 4), ("tbl3", 4)):
    _part(_n, _c, "ar16")
_buf("ar", _used["ar"])
_buf("ar16", _used["ar16"], "uint16")
_buf("arb", _used["arb"], "bfloat16")
_buf("row", 512)
_buf("yy", 512)
for _g in range(8):
    _buf("sw%d" % _g, 512)
for _b in range(4):
    _buf("fh%d" % _b, 512)
    _buf("pa%d" % _b, 256)
    _buf("pp%d" % _b, 512)
for _b in range(2):
    _buf("f%d" % _b, 512)
    _buf("fs%d" % (_b + 2), 512)
for _n, _c in (("pi", 1), ("bi", 16), ("uoi", 64), ("tbi", 16)):
    _buf(_n, _c, "int32")
for _n, _c in (("xt", 2048), ("ut", 512), ("vt", 512), ("zt", 1024), ("ee0", 514), ("ee1", 514), ("ones", 520)):
    _buf(_n, _c, "bfloat16")
for _n, _c in (("xq", 512), ("uq", 128), ("uc", 1024), ("vq", 128), ("wq", 512), ("zq", 256), ("eq", 512)) + tuple(("zl%d" % r, 256) for r in range(R)):
    _buf(_n, _c, "float8_e4m3fn_x4")
    _buf(_n + "s", _c, "uint8")
for _b in range(8):
    _buf("b%d" % _b, 512, "float32", "psum")
for _r in range(R):
    SEMAPHORES += [s % _r for s in ("aa%d", "ab%d", "lc%d", "dl%d", "dm%d", "dn%d", "db%d")]
    SEMAPHORES += ["dga%d%d" % (_r, g) for g in range(5)]
OPT = {"sw0": "vsv", "np6": 3, "early": 1, "pa0": "s", "n0": 8, "n1": 2, "k1": 1, "wa": 128, "send": "plain", "v6": 3, "id0": 1, "xq": "yyy", "vq": 0, "sa": 3, "np5": 2, "joint": 0}
PRODUCTS = (((3,), (4,), (5,), (6,), (7,)), ((6,), (7,), (), (), ()))
LAST = (0, 192, 384, 512)
PIECES = ((0, 256), (256, 384), (384, 512))


def rank_program(g, core, T, topo):
    rank = T.rank_of(core)
    if rank is None:
        return
    nxt = T.cores[(rank + 1) % len(T.cores)]
    queues = {"v": g.vector, "s": g.scalar, "t": g.tensor, "g": g, "y": g.sync}
    semof = {"v": "sv", "s": "ss", "t": "sp", "g": "sg"}
    count = {k: 0 for k in semof}
    known = {k: {} for k in queues}
    hist = {}
    behind = {}
    total = {}

    def need(q, tok):
        sem, val = tok
        if known[q].get(sem, 0) < val:
            queues[q].wait_ge(T.sem[sem], val)
            known[q][sem] = val
            for s, n in behind.get(tok, {}).items():
                known[q][s] = max(known[q].get(s, 0), n)

    def v(name, c0=0, c1=None, st=1, p0=0, p1=128):
        name, at, cols = PLACE[name]
        c0, c1 = c0 + at, (cols if c1 is None else c1) + at
        if st < 0:
            return (name, p0, p1, c0, c1, T[name][p0:p1, c1 - 1:c0 - 1:-1], 1)
        ap = T[name][p0:p1, c0:c1] if st == 1 else T[name][p0:p1, c0:c1:st]
        return (name, p0, p1, c0, c1, ap, st)

    def quad(name, c0, c1, a):
        return v(name, c0, c1, 1, 32 * a, 32 * a + 32)

    def hf(name, c0, c1, a, st=1):
        return v(name, c0, c1, st, 64 * a, 64 * a + 64)

    def deps(q, ins, outs):
        toks = {}
        for w, views in ((0, ins), (1, outs)):
            for n, p0, p1, c0, c1, ap, st in views:
                ps = n in SCRATCH and SCRATCH[n][0] == "psum"
                for (tok, eng, hw, a, b, c, d, s) in hist.get(n, []):
                    if ps and eng != q or (w or hw) and a < p1 and p0 < b and c < c1 and c0 < d and not (s == st > 1 and (c - c0) % st):
                        toks[tok[0]] = max(toks.get(tok[0], 0), tok[1])
        for s in sorted(toks):
            if not any(behind.get((t, toks[t]), {}).get(s, 0) >= toks[s] for t in toks if t != s):
                need(q, (s, toks[s]))

    def note(q, tok, ins, outs):
        if q in known:
            seen = behind.setdefault(tok, {})
            for s, n in known[q].items():
                seen[s] = max(seen.get(s, 0), n)
        for w, views in ((0, ins), (1, outs)):
            for n, p0, p1, c0, c1, ap, st in views:
                h = hist.setdefault(n, [])
                if w:
                    h[:] = [e for e in h if not (st in (1, e[7]) and p0 <= e[3] and e[4] <= p1 and c0 <= e[5] and e[6] <= c1 and (e[5] - c0) % st == 0)]
                else:
                    h[:] = [e for e in h if not (e[1] == q and not e[2] and e[0][0] == tok[0] and e[3:] == (p0, p1, c0, c1, st))]
                h.append((tok, q, w, p0, p1, c0, c1, st))

    def op(q, fn, outs, ins):
        deps(q, ins, outs)
        i = fn(queues[q])
        count[q] += 1
        i.then_inc(T.sem[semof[q]], 1)
        note(q, (semof[q], count[q]), ins, outs)
        if q == "v" and len({a[1] // 32 for a in ins}) > 1:
            need(q, (semof[q], count[q]))

    def dma(q, sem, group, out, in_):
        out, in_ = [a if len(a) > 6 else a + (1,) for a in (out, in_)]
        deps(q, [in_], [out])
        queues[q].dma_start(out[5], in_[5]).then_inc(T.sem[sem], 16)
        total[sem] = 16 * group
        note(q, (sem, 16 * group), [in_], [out])

    def cd(name, c0=0, c1=None):
        n, p0, p1, a, b, ap, st = v(name, c0, c1)
        return (n, p0, p1, a, b, ap.bitcast(dt.uint8), 1)

    def ts(out, in0, s1, op0, s2=None, op1=None):
        ins = [in0] + [s for s in (s1, s2) if isinstance(s, tuple)]
        a, b = [s[5] if isinstance(s, tuple) else s for s in (s1, s2)]
        if op1 is None:
            op("v", lambda e: e.tensor_scalar(out[5], in0[5], a, None, op0), [out], ins)
        else:
            op("v", lambda e: e.tensor_scalar(out[5], in0[5], a, b, op0, op1), [out], ins)

    def tt(out, a, b, o=OP.add):
        op("v", lambda e: e.tensor_tensor(out[5], a[5], b[5], o), [out], [a, b])

    def ttg(out, win, off, b, o=OP.add):
        op("v", lambda e: e.tensor_tensor(out[5], win[5].indirect(off[5]), b[5], o), [out], [win, off, b])

    def scan(out, d0, d1, init, o0, o1):
        op("v", lambda e: e.tensor_tensor_scan(out[5], d0[5], d1[5], init, o0, o1), [out], [d0, d1])

    def copy(out, in_):
        op("v", lambda e: e.tensor_copy(out[5], in_[5]), [out], [in_])

    def trans(out, in_):
        op("v", lambda e: e.transpose(out[5], in_[5]), [out], [in_])

    def fill(out, c):
        op("v", lambda e: e.memset(out[5], c), [out], [])

    def vgather(out, win, off):
        op("v", lambda e: e.tensor_copy(out[5], win[5].indirect(off[5])), [out], [win, off])

    def scatter(win, off, in_):
        op("v", lambda e: e.tensor_copy(win[5].indirect(off[5]), in_[5]), [win], [off, in_])

    def act(out, in_, scale=1.0):
        op("s", lambda e: e.activation(out[5], in_[5], AF.Copy, scale=scale), [out], [in_])

    def lin(out, in_, scale, bias, func=AF.Identity):
        col = isinstance(bias, tuple)
        op("s", lambda e: e.activation(out[5], in_[5], func, bias=bias[5] if col else bias, scale=scale), [out], [in_] + ([bias] if col else []))

    def sgather(out, win, off, scale=None):
        more = {} if scale is None else {"scale": scale}
        op("s", lambda e: e.activation(out[5], win[5].indirect(off[5]), AF.Copy, **more), [out], [win, off])

    def accum(out, in_, acc):
        op("s", lambda e: e.activation(out[5], in_[5], AF.Copy, accum_out=acc[5]), [out, acc], [in_])

    def quant(c, s, t):
        op("v", lambda e: e.quantize_mx(c[5], s[5], t[5]), [c, s], [t])

    def mm(out, l, ls, r_, rs):
        op("t", lambda e: e.matmul_mx(out[5], l[5], ls[5], r_[5], rs[5], True, True), [out], [l, ls, r_, rs])

    def iota(out, pat, base=0, cm=0):
        if out[0] in ("pi", "uoi"):
            op("g", lambda e: e.iota(out[5], pat, base, cm), [out], [])
        else:
            op("g", lambda e: e.iota(out[5], pat, base, cm, allow_small_or_imprecise_dtypes=True), [out], [])

    def select(out, in_, pat, fill_, base=0, cm=0, cmp=OP.is_equal):
        op("g", lambda e: e.affine_select(out[5], in_[5], pat, cmp, fill_, base, cm), [out], [in_])

    def group_of(B):
        return 4 * (B % 2) + 2 * (B // 2 % 2) + B // 4

    dma("y", "du", 1, v("ut"), ("u", 0, 128, 0, 512, T.u[:, :]))
    for i in range(3):
        a, b = 4 * PIECES[i][0], 4 * PIECES[i][1]
        dma(OPT["xq"][i], "dx%d" % i, 1, v("xt", a, b), ("x", 0, 128, a, b, T.x[:, a:b]))
    for h in range(2):
        dma("y", "dp", 2, v("tbi", 0, 16, 1, 16 * h, 16 * h + 16), ("p", 0, 16, 16 * h, 16 * h + 16, T.p[:, 16 * h:16 * h + 16]))
    need("y", ("dp", 32))
    dma("y", "dv", 1, v("vt"), ("v", 0, 128, 0, 512, T.v[:, :]))
    dma("y", "dw", 2, cd("wq"), ("wc", 0, 128, 0, 2048, T.wc[:, :]))
    dma("y", "dw", 2, v("wqs"), ("ws", 0, 128, 0, 512, T.ws[:, :]))

    col = [0]

    def newcol():
        col[0] += 1
        return v("sgk", col[0] - 1, col[0])

    def dscp(a, b):
        return v("sgk", 0, 1, 1, a, b)

    def starts(k):
        if k == 2:
            select(v("rst2"), v("big", 0, 72), [[0, 8], [1, 9]], -BIG, -1)
        else:
            select(v("rst%d" % k), v("big", 0, 64), [[0, 64 // WID[k]], [1, WID[k]]], -BIG)

    def counts(k):
        s = WID[k] + 2
        pat = [[32, 2], [0, 2]] if k == 3 else [[0, 2], [16, 2]] if k == 4 else [[16, 4]]
        if k < 6:
            iota(v("msk%d" % k), [[0, 4 * s]], 1)
            for c in (0, 1):
                iota(v("c%d" % k, s - 1 - c, 4 * s, s), [[0, 4]], c)
            iota(v("msk%d" % k, s - 2, 4 * s, s), pat)
            return
        for c in (s - 2, s - 1) if k < 7 else (s - 2,):
            iota(v("c%d" % k, c, 4 * s, s), pat)
        if k < 7:
            select(v("msk%d" % k), v("ones", 0, 4 * s), [[0, 4], [1, s]], 0.0, cmp=OP.not_equal)

    def windows(r):
        select(v("w5s%d" % r), v("big", 0, 128), [[0, 128]], BIG)
        iota(v("w5%d" % r), [[0, 128]])
        iota(v("list%d" % r), [[0, 64]])
        select(v("w6s%d" % r), v("big"), [[0, 256]], BIG)
        for n, c in (("w6%d", 256), ("w7%d", 528)):
            iota(v(n % r), [[0, c]])

    iota(v("pi"), [[0, 1]], 0, 1)
    fill(v("big"), BIG)
    for c, m in enumerate((15, 2, 4, 8, 32, 64, 16, 14, 12)):
        ts(v("bi", c, c + 1), v("pi"), m, OP.bitwise_and)
    fill(v("ones"), 1.0)
    iota(v("n16"), [[0, 4], [1, 16]])
    iota(v("io4"), [[16, 4]])
    iota(v("i17"), [[0, 4], [1, 17]])
    iota(v("uoi"), [[16, 8], [0, 8]])
    iota(v("i18"), [[0, 4], [1, 18]])
    starts(0)
    starts(3)
    iota(v("iot"), [[1, 512]])
    starts(1)
    iota(v("c1", 17, 72, 18), [[int(2 * SEP), 4]])
    iota(v("n32"), [[0, 2], [1, 32]])
    starts(2)
    for b in range(2):
        select(v("ee%d" % b), v("ones", 0, 514), [[-1, 514]], 0.0, 2 + b, 4)
    counts(3)
    counts(4)
    counts(5)
    counts(6)
    windows(0)
    counts(7)
    select(v("m4"), v("ones", 0, 64), [[0, 16], [1, 4]], 0.0, cmp=OP.not_equal)
    iota(v("iom"), [[1, 512]], -256)
    windows(1)
    windows(2)

    q = v("bff", 0, 1)
    dsc, q1, nq2, bq, bm, e6, e7, e7c, bk, q63, g7, g32, dsl, e2, dsr = [newcol() for _ in range(15)]
    bit = {k: v("bff", c, c + 1) for k, c in ((0, 1), (1, 2), (2, 3), (6, 4), (5, 5), (7, 6))}
    th = {k: newcol() for k in bit}
    lo = {0: v("bff", 7, 8), 1: v("bff", 8, 9), 2: bit[2]}
    copy(v("bff", 0, 9), v("bi", 0, 9))
    copy(v("uo"), v("uoi"))
    ts(v("rtab"), v("io4"), q, OP.add)
    ts(q1, q, 1.0, OP.add)
    ts(dsc, q, 15.0, OP.is_equal, 1.0 - 1.0 / DIG, OP.mult)
    ts(v("md", 0, 64), v("n16"), q, OP.is_gt)
    ts(v("mda"), v("n16"), q1, OP.is_equal, DIG - 1.0, OP.mult)
    ts(dsc, dsc, 1.0 / DIG, OP.add)
    cols = {k: [newcol() for _ in range(5)] for k in range(3)}

    def ends():
        for k in range(2):
            lin(cols[k][2], lo[k + 1], 2.0, 2.0 * WID[k])
        lin(cols[2][3], lo[2], -9.0 / 8, 17.0)
        for k in range(2):
            lin(cols[k][3], lo[k], -1.0, cols[k][2])

    def partner(k):
        rw, i = cols[k][3], v("i18" if k else "i17")
        ts(v("ms%d" % k), i, rw, OP.subtract, -float(WID[k]), OP.not_equal)
        ts(v("t3%d" % k), i, rw, OP.is_equal, SEP - 1.0, OP.mult)

    def side(k):
        if k < 7:
            lin(th[k], bit[k], -EPS / MASK[k], 0.0)
        else:
            lin(th[k], bit[k], EPS / MASK[k], -EPS)

    MASK = {0: 2, 1: 4, 5: 64, 6: 32, 7: 16}
    bl, bp, xl, b1, b2 = [newcol() for _ in range(5)]
    lin(bm, q, -BIG, -BIG / 2)
    lin(bl, lo[0], BIG, -BIG / 2)
    ends()
    lin(v("mh"), v("n16"), BIG, bm)
    lin(v("t10"), v("n16"), -BIG, bl)
    lin(bp, cols[0][3], -1.0, 1.5)
    side(0)
    lin(bk, q, -BIG, 15.5 * BIG)
    lin(v("t11", 0, 64), v("n16"), 1.0, bp, AF.Abs)
    ts(v("c0", 16, 68, 17), v("rtab"), bit[0], OP.subtract, SEP, OP.mult)
    tt(v("md", 0, 64), v("md", 0, 64), v("mda"))
    partner(0)
    spare = []

    def later(f, *a):
        spare.append((f, a))

    def fit(n):
        for f, a in spare[:n]:
            f(*a)
        del spare[:n]

    def upick(a, b):
        o, w, f = v("uc", 128 * a, 128 * b), v("uq"), v("uo", 8 * a, 8 * b)
        op("v", lambda e: e.tensor_copy(o[5].bitcast(dt.uint32), w[5].bitcast(dt.uint32).indirect(f[5])), [o], [w, f])
        sgather(v("ucs", 128 * a, 128 * b), v("uqs"), f)

    def units(b):
        c = 2 - 2 * (b // 2)
        quant(v("eq", 128 * b, 128 * b + 128), v("eqs", 128 * b, 128 * b + 128), v("ee%d" % (b % 2), c, c + 512))

    quant(v("uq"), v("uqs"), v("ut"))
    partner(1)
    upick(0, 2)
    tt(v("mq0"), v("mh"), v("t10"), OP.max)
    ts(v("l17"), v("i17", 0, 4), 17.0, OP.mult, q, OP.add)
    for k in range(2):
        tt(v("ms%d" % k), v("ms%d" % k), v("t3%d" % k))
    lin(v("mp0"), v("t11", 0, 64), BIG, -0.75 * BIG)
    side(1)
    lin(e2, bit[2], 0.125, 1.0)
    zero = v("i17", 0, 68, 17)
    xr, xe, n2, q15 = [newcol() for _ in range(4)]
    lin(xl, bit[2], -BIG / 8, BIG)
    lin(xr, bit[2], BIG / 8, 0.0)
    lin(b2, bit[2], BIG / 4, -BIG)
    lin(n2, bit[2], -SEP, 0.0)
    lin(b1, xl, 1.0, bk)
    lin(xe, xl, 1.0, -EPS)
    lin(v("g2", 9, 72, 18), zero, 1.0, xr)
    lin(v("c2", 17, 72, 18), v("rtab"), SEP, n2)
    lin(v("mk2"), v("i18"), -BIG, b1)
    lin(v("g2", 0, 72, 18), zero, 1.0, xe)
    later(lin, v("mk2", 17, 72, 18), zero, 1.0, b2)
    later(lin, q63, q, -1.0, 63.0)
    later(lin, v("mk16"), v("n16"), -BIG, bk)
    later(lin, v("mk32"), v("n32"), -BIG, bk)
    later(lin, v("mk64"), v("iot", 0, 64), -BIG, bk)
    later(side, 5)
    later(lin, e6, bit[5], 1.0, q)
    later(lin, q15, q, -1.0, 15.0)
    later(lin, dsr, q, -1.0, 1.0, AF.Relu)
    later(act, v("md", 64, 128), v("md", 0, 64))
    later(lin, e7c, bit[5], 1.0, q15)
    later(lin, dsr, dsr, 1.0 - 1.0 / DIG, 1.0 / DIG)
    later(side, 6)
    later(act, v("md", 128, 256), v("md", 0, 128))
    later(lin, e7, bit[6], 4.0, e7c)
    later(side, 7)
    later(lin, e7c, e7, 1.0, 48.0)

    def compact(name, c0, c1, p0=0, p1=128):
        return v(name, c0 + 15, c1, 16, p0, p1)

    def diag(out, row, c0, c1):
        scan(out, v("md", 0, c1 - c0), v(row, c0, c1), 0.0, OP.mult, OP.add)

    def runmin(out, a, b=None):
        scan(out, a, b or a, BIG, OP.min, OP.min)

    def hold(out, m, row):
        scan(out, m, row, BIG, OP.min, OP.max)

    def quantx(i):
        a, b = PIECES[i]
        quant(v("xq", a, b), v("xqs", a, b), v("xt", 4 * a, 4 * b))

    for r in range(R):
        lst = "list%d" % r
        dg = T["dg%d" % r]

        def score(k, bank, c0=0, c1=512):
            mm(v(bank, 0, c1 - c0), v("uc", 128 * k, 128 * k + 128), v("ucs", 128 * k, 128 * k + 128), v("xq", c0, c1), v("xqs", c0, c1))

        def sbank(k):
            return "b%d" % ((k + 6) % 8)

        def scored(k):
            act(v("sw%d" % k), v(sbank(k)), -1.0)

        def unpack(b):
            mm(v(sbank(b)), v("eq", 128 * b, 128 * b + 128), v("eqs", 128 * b, 128 * b + 128), v("xq"), v("xqs"))

        def half(b):
            act(v("fh%d" % b), v(sbank(b)), 0.5)

        def whole(b):
            act(v("f%d" % b), v(sbank(b)))

        for i, (a, b) in enumerate(PIECES):
            quantx(i)
            score(0, "b%d" % (4 + i), a, b)
            if r == 0 and i == 1:
                upick(2, 4)

        if r:
            ts(v("tb"), v("tbf"), 256.0, OP.add)
        ts(v("sw0", 0, 256), v("b4", 0, 256), -1.0, OP.mult)
        act(v("sw0", 256, 384), v("b5", 0, 128), -1.0)
        if r == 0:
            for a in range(4):
                c = 4 * (2 * (a % 2) + a // 2)
                copy(quad("tb", 0, 4, a), quad("tbi", c, c + 4, 0))
        ts(v("sw0", 384, 512), v("b6", 0, 128), -1.0, OP.mult)
        score(1, sbank(1))
        if r == 0:
            partner(2)
        ttg(v("gm"), v("sw0"), v("tb"), v("mq0"), OP.max)
        sgather(v("g0"), v("sw0"), v("tb"))
        for k in range(2, 3 if r == 0 else 6):
            score(k, sbank(k))
        scored(1)
        sgather(v("o1"), v("sw1"), v("tb"))
        scored(2)
        sgather(v("id0r"), v("iot"), v("tb"))
        sgather(v("o2"), v("sw2"), v("tb"))

        def ids(k):
            return "idw" if k == 5 else "id%dr" % k

        def table(k):
            tab = "tbl%d" % k
            ts(v(tab), compact("ds", 0, 64), dsc, OP.mult)
            sgather(v("o%d" % (k + 2)), v("sw%d" % (k + 2)), v(tab))
            listed(k)

        def listed(k, ds="ds"):
            act(v("lr", 4 * k, 4 * k + 4), compact(ds, 0, 64))
            dma("y", "dga%d%d" % (r, k), 1, ("dg%d" % r, 0, 128, k, k + 1, dg[k]), v("lr", 4 * k, 4 * k + 4))

        def run(k):
            s = WID[k] + 2
            for a, b in ((0, 3 * s), (3 * s, 4 * s)) if k == 5 else ((0, 4 * s),):
                scan(v("smb", a, b), v("msk%d" % k, a, b), v("c%d" % k, a, b), 0.0, OP.add, OP.mult)
            return v("smb", s - 2, 4 * s, s)

        def keys(out, m, row):
            scan(out, m, row, BIG, OP.max, OP.min)

        for k in range(5):
            w = WID[k]
            G = v("g%d" % k)
            C = "c%d" % k
            if k == 0:
                keys(v("kd"), v("rst3"), v("gm"))
                keys(v("kk"), v("rst0"), G)
                if r == 0:
                    tt(v("ms2"), v("ms2"), v("t32"))
            elif k == 1:
                for c in range(0, 64, 16):
                    runmin(v("kd", c, c + 16), v("gm", c, c + 16), v("gw", c, c + 16))
                keys(v("kk"), v("rst1"), G)
                ts(v("c1", 16, 72, 18), v("rk0"), bit[1], OP.subtract, SEP, OP.mult)
                ts(v("rk1"), v("rk0", 2, 4), -32.0, OP.add)
            elif k == 2:
                keys(v("ke", 0, 72), v("mk2"), v("g2", 0, 72, -1))
                keys(v("kk2"), v("rst2"), G)
                diag(v("ds"), ids(k), 0, 64)
            else:
                keys(v("kd"), v("mk16"), G)
                if k == 4:
                    keys(v("kk"), v("mk32"), G)
                diag(v("ds"), ids(k), 0, 64)
            s = 17 if k == 0 else 18 if k < 3 else w + 2
            for c in range(4):
                if k == 2:
                    a = 54 - 18 * c
                    ts(v(C, s * c, s * c + 17), v("kk2", s * c + 1, s * c + 18), v("ke", a + 8, a + 9), OP.subtract, v("ke", a + 17, a + 18), OP.is_gt)
                elif k < 3:
                    x = v("kd", 16 * c + 15, 16 * c + 16)
                    ts(v(C, s * c, s * c + 16), v("kk", 16 * c, 16 * c + 16), x, OP.subtract, th[k], OP.is_gt)
                else:
                    left = c % 2 == 0 if k == 3 else c < 2
                    a = 48 - 16 * (c ^ 1) if k == 3 else 32 - 32 * left
                    x = v("kd", 63 - 16 * c, 64 - 16 * c) if k == 3 or c % 2 == 0 else v("kk", 79 - 16 * c, 80 - 16 * c)
                    ts(v(C, s * c, s * c + w), v("g%d" % k, a, a + w), x, OP.is_gt if left else OP.is_ge)
            if k > 1:
                table(k - 1)
            if r == 0 and k > 1:
                units(k - 2)
            if k == 0:
                ttg(v("gp"), v("sw1"), v("tb"), v("mp0"), OP.max)
                scan(v("sm", 0, 68), v("ms0"), v(C), 0.0, OP.mult, OP.add)
                ts(v("gy"), v(C), -2 * BIG, OP.mult, BIG, OP.add)
                ttg(v("gw"), v("sw1"), v("tb"), v("mq0"), OP.max)
                ts(v("rk0"), v("sm", 16, 68, 17), 1.0 / SEP, OP.mult)
                ttg(v("gm"), v("gy"), v("l17"), v("gp"), OP.max)
                scatter(v("g1"), v("rk0"), v("o1"))
            elif k < 3:
                if k == 1:
                    scatter(v("id1r", 0, 32), v("rk0", 0, 2), v("id0r", 0, 32))
                scan(v("sm"), v("ms%d" % k), v(C), 0.0, OP.mult, OP.add)
                if k == 1:
                    scatter(v("id1r", 32, 64), v("rk1"), v("id0r", 32, 64))
                if r == 0 and k == 2:
                    upick(5, 6)
                if k == 2:
                    ts(v("rr"), v("sm", 17, 72, 18), -1.0 / SEP, OP.mult, 63.0, OP.add)
                else:
                    ts(v("rr"), v("sm", 17, 72, 18), 1.0 / SEP, OP.mult, e2, OP.add)
                ts(v("rk"), v("sm", 15 + k, 72, 18), 1.0 / SEP, OP.mult)
                if r == 0 and k == 1:
                    upick(4, 5)
            else:
                n = run(k)
                if r == 0:
                    upick(k + 3, k + 4)
                ts(v("rr"), n, -1.0, OP.mult, q63, OP.add)
                ts(v("rk"), n, q, OP.add)
                if k == 3:
                    diag(v("ds0"), "id1r", 0, 64)
                    listed(0, "ds0")
                if r == 0 and k == 4:
                    units(3)
            if k:
                scatter(v("g%d" % (k + 1)), v("rr"), v("o%d" % (k + 1)))
                scatter(v(ids(k + 1)), v("rk"), v(ids(k if k > 1 else 0)))
            fit((3, 6, 4, 4, 0)[k])
            for j in PRODUCTS[r > 0][k]:
                score(j, sbank(j))
            for b in range(4) if k == (2 if r else 4) else ():
                unpack(b)
            if k < 4:
                scored(k + 3)

        def versus(k, c):
            w = WID[k]
            s = w + 2
            e = ENDS[c] if k == 5 else 16 * (c ^ 2 if k == 7 else c) + 16
            ts(v("c%d" % k, s * c, s * c + w), v("np%d" % k), v("ke" if k == 5 else "hh%d" % k, e - 1, e), OP.subtract, th[k], OP.is_gt)

        ENDS = (16, 48, 96, 160)
        for a in (0, 1):
            (act if a < OPT["np5"] else copy)(hf("np5", 0, 64, a), hf("g5", 0, 64, 1 - a))
        scored(7)
        for c in range(4):
            n = 16 * c + 16
            keys(v("ke", ENDS[c] - n, ENDS[c]), v("mk64", 0, n), v("g5", 64 - n, 64))
        diag(v("ds"), "idw", 0, 64)
        for c in range(4):
            versus(5, c)
        table(4)
        half(0)
        if r == 0:
            ts(g7, v("pi"), 112.0, OP.is_ge, 256.0, OP.mult)
            ts(g32, v("pi"), 112.0, OP.is_ge, 32.0, OP.mult)
        n = run(5)
        if r == 0:
            ts(dsl, g7, 1.0 / 256, OP.mult, dsc, OP.max)
            ts(v("sel"), v("rtab", 0, 2), g32, OP.add)
        ts(v("rk"), n, q, OP.add)
        scatter(v("w5s%d" % r), v("rk"), v("o6"))
        scatter(v("w5%d" % r), v("rk"), v("idw"))
        runmin(hf("no6", 0, 128, 0), hf("w5s%d" % r, 0, 128, 0), hf("w5s%d" % r, 0, 128, 1))
        for a in range(4):
            (act if a < OPT["np6"] else copy)(quad("np6", 0, 128, a), quad("no6", 0, 128, 1 - a % 2))
        for a in (0, 1):
            hold(hf("hh6", 0, 64, a), hf("mh", 0, 64, 0), hf("no6", 64 * a, 64 * a + 64, 0))
        diag(v("ds6"), "w5%d" % r, 0, 128)
        for a in (0, 1):
            act(hf("sh5", 0, 4, a), compact("ds6", 64 * a, 64 * a + 64, 64 - 64 * a, 128 - 64 * a))
        for c in range(3):
            versus(6, c)
        for a in (0, 1):
            tt(hf("lr5", 0, 4, a), compact("ds6", 64 * a, 64 * a + 64, 64 * a, 64 * a + 64), hf("sh5", 0, 4, a))
        versus(6, 3)
        scan(v("smb", 0, 260), v("msk6", 0, 260), v("c6", 0, 260), 0.0, OP.mult, OP.add)
        ts(v("own6"), v("lr5"), dsc, OP.mult)
        sgather(v("o7"), v("sw7"), v("own6"))
        sgather(v("id6"), v("iot"), v("own6"))
        half(1)
        for B in range(8):
            h, c = 16 * group_of(B), 4 * B
            dma("y", "dl%d" % r, 8, v(lst, c, c + 4, 1, 0, 80), ("dg%d" % r, h, h + 16, 0, 5, dg[0:5, h:h + 16, :]))
        for B in range(8):
            h, c = 16 * group_of(B), 4 * B
            dma("y", "dm%d" % r, 8, v(lst, c, c + 4, 1, 80, 96), v("lr5", 0, 4, 1, h, h + 16))
        for c in (260, 390):
            scan(v("smb", c, c + 130), v("msk6", c, c + 130), v("c6", c, c + 130), 0.0, OP.mult, OP.add)
        ts(v("rk"), v("smb", 128, 520, 130), e6, OP.add)
        scatter(v("w6s%d" % r), v("rk"), v("o7"))
        scatter(v("w6%d" % r), v("rk"), v("id6"))
        runmin(hf("nh7", 0, 256, 0), hf("w6s%d" % r, 0, 256, 0), hf("w6s%d" % r, 0, 256, 1))
        half(2)
        runmin(quad("np7", 0, 256, 0), quad("nh7", 0, 256, 0), quad("nh7", 0, 256, 1))
        for a in range(1, 4 - OPT["vq"]):
            act(quad("np7", 0, 256, a), quad("np7", 0, 256, 0))
        for a in range(4):
            c = 64 * (2 * (a % 2) + a // 2)
            hold(quad("hk7", 0, 64, a), quad("mh", 0, 64, 0), quad("np7", c, c + 64, 0))
        diag(v("ds7", 0, 128), "w6%d" % r, 0, 128)
        trans(v("t7"), v("hk7"))
        diag(v("ds7", 128, 256), "w6%d" % r, 128, 256)
        if OPT["vq"] == 1:
            copy(quad("np7", 0, 256, 3), quad("np7", 0, 256, 0))
        if OPT["vq"] == 2:
            copy(hf("np7", 0, 256, 1), hf("np7", 0, 256, 0))
        trans(v("hh7"), v("t7", 0, 64, -1))
        for a in range(4):
            (act if a < OPT["sa"] else copy)(v("sa", a, 64, 4, 0, 32), compact("ds7", 0, 256, 32 * a, 32 * a + 32))

        def count7(c):
            accum(v("jk", 258 * c, 258 * c + 257), v("c7", 258 * c, 258 * c + 257), v("sum4", c, c + 1))

        versus(7, 0)
        scan(quad("sb", 0, 64, 0), quad("m4", 0, 64, 0), quad("sa", 0, 64, 0), 0.0, OP.mult, OP.add)
        count7(0)
        act(quad("ap6", 0, 16, 0), v("sb", 3, 64, 4, 0, 32))
        versus(7, 1)
        trans(quad("sc", 0, 64, 0), quad("sb", 0, 64, 0))
        count7(1)
        versus(7, 2)
        trans(quad("sd", 0, 64, 0), v("sc", 0, 64, -1, 0, 32))
        count7(2)
        for c in (0, 128):
            ts(v("c7", 774 + c, 902 + c), v("np7", c, c + 128), v("hh7", 31, 32), OP.subtract, th[7], OP.is_gt)
        accum(v("jk", 0, 128), v("c7", 774, 902), v("sum4", 3, 4))
        for a in range(4):
            c = 16 * (2 * (a % 2) + a // 2) ^ 32
            ts(quad("own7", 0, 4, a), v("sd", c + 3, c + 16, 4, 0, 32), (dsr[0], 0, 32) + dsr[3:5] + (T[dsr[0]][0:32, dsr[3]:dsr[4]], 1), OP.mult)
        scan(v("smb", 0, 128), v("ones", 0, 128), v("c7", 902, 1030), 0.0, OP.mult, OP.add)
        sgather(v("id7"), v("iom"), v("own7"))
        for j in range(2):
            dma("y", "dn%d" % r, 2, v(lst, 16 * j, 16 * j + 16, 1, 96, 112), v("ap6", 0, 16, 1, 16 * j, 16 * j + 16))
        half(3)
        whole(0)
        whole(1)
        if r == 0:
            act(v("md", 256, 512), v("md", 0, 256))
        ts(v("rk", 3, 4), v("smb", 127, 128), v("sum4", 3, 4), OP.add, e7c, OP.add)
        ts(v("rk", 0, 3), v("sum4", 0, 3), e7, OP.add)
        scatter(v("w7%d" % r, 16, 528), v("rk"), v("id7"))
        trans(v("tz", 0, 512), v("w7%d" % r, 0, 512))
        trans(v("tz", 512, 1024), v("w7%d" % r, 16, 528))
        for j in range(2):
            tt(v("qh", j, 32, 2), v("tz", 512 * j, 512 * j + 512, 32), v("tz", 512 * j + 16, 512 * j + 512, 32))
        tt(hf("qc", 0, 32, 1), hf("qh", 0, 32, 1), hf("qh", 0, 32, 0))
        tt(quad(lst, 32, 64, 3), quad("qc", 0, 32, 3), quad("qc", 0, 32, 2))
        o, w, f = v("off"), v(lst), v("sel")
        op("v", lambda e: e.tensor_scalar(o[5], w[5].indirect(f[5]), dsl[5], g7[5], OP.mult, OP.add), [o], [w, f, dsl, g7])
        if r < R - 1:
            for B in range(8):
                h, c = 16 * group_of(B), 4 * B
                dma("y", "db%d" % r, 8, v("tbf", 0, 4, 1, h, h + 16), v(lst, 32 + c, 36 + c, 1, 112, 128))

        rid, pid, _s = topo.addr(nxt)
        eng = topo.engines(core, nxt)
        ways = (eng[0::2], eng[1::2])
        loc = "lc%d" % r
        joint = r == 0 and OPT["joint"]
        total[loc] = len(ways[0]) * (3 if joint else 4)

        def pair(j, b):
            c = 128 * j
            ttg(v("zt", 4 * c + b, 4 * c + 512, 4), v("fh%d" % b), v("off", 16 + 8 * j, 24 + 8 * j), v("pa%d" % b, c, c + 128))

        def inverse(n):
            scatter(v("posw"), v("off", done[0], done[0] + n), v("iot", 16 * done[0], 16 * (done[0] + n)))
            done[0] += n

        done = [0]
        for j in range(2):
            for b in range(4):
                sgather(v("pa%d" % b, 128 * j, 128 * j + 128), v("fh%d" % b), v("off", 8 * j, 8 * j + 8))
        inverse(OPT["n0"])
        for j in range(2):
            c = 128 * j
            for b in range(j, 4):
                pair(j, b)
            if j == 0:
                pair(1, 0)
            else:
                inverse(OPT["n1"])
            quant(v("zq", c, c + 128), v("zqs", c, c + 128), v("zt", 4 * c, 4 * c + 512))
            sem = ("aa%d", "ab%d")[j] % r
            parts = [(cd("zq", c, c + 128), cd("zl%d" % r, c, c + 128))]
            if j or not joint:
                a = 0 if joint else c
                parts.append((v("zqs", a, c + 128), v("zl%ds" % r, a, c + 128)))
            total[sem] = len(ways[0]) * len(parts)
            for (src, land), es in zip(parts, ways):
                deps("g", [src], [])
                g.remote_dma(land[5], src[5], T.sem[sem], T.sem[loc], pid, rid, sum(1 << e for e in es))
                note("g", (loc, total[loc]), [src], [])
                note("x", (sem, total[sem]), [], [land])
        inverse(32 - done[0])
        for b in (2, 3):
            sgather(v("fs%d" % b), v("fh%d" % b), v("off"), 64.0)

        def layer(j):
            c = 128 * j
            for b in (2, 0, 3, 1):
                mm(v("b%d" % (4 * j + b), 0, 128), v("wq", 128 * b, 128 * b + 128), v("wqs", 128 * b, 128 * b + 128),
                   v("zl%d" % r, c, c + 128), v("zl%ds" % r, c, c + 128))
            for b in range(2):
                for a in (c, c + 256):
                    act(v("pp%d" % b, a, a + 128), v("b%d" % (4 * j + b), 0, 128), 0.03125)

        def plus(j, b):
            for a in (128 * j, 128 * j + 256):
                tt(v("pp%d" % b, a, a + 128), v("b%d" % (4 * j + b), 0, 128), v("fs%d" % b, a, a + 128))

        early = r > 0 and OPT["early"]
        if r == R - 1:
            sgather(v("row"), v("iot"), v("off"))
            dma("y", "dod", 1, ("od", 0, 8, 0, 512, T.od[:, :]), ("row", 0, 128, 0, 512, T.row[0:128:16, :]))
        layer(0)
        if r == 0:
            quant(v("vq"), v("vqs"), v("vt"))
        if early:
            plus(0, 2)
        diag(v("pds"), "posw", 0, 512)
        if early:
            plus(0, 3)
        ts(v("pos"), v("pds", 15, 512, 16), dsc, OP.mult)
        if not early:
            plus(0, 2)
            plus(0, 3)
        layer(1)
        plus(1, 2)
        plus(1, 3)

        def back(b, c0, c1):
            sgather(v("xt", 4 * c0 + b + 2, 4 * c1, 4), v("pp%d" % (b + 2)), v("pos", c0 // 16, c1 // 16), 0.03125)
            ttg(v("xt", 4 * c0 + b, 4 * c1, 4), v("pp%d" % b), v("pos", c0 // 16, c1 // 16), v("f%d" % b, c0, c1))

        if r < R - 1:
            for b, c0, c1 in ((0, 0, 512), (1, 0, 256), (1, 256, 512)):
                back(b, c0, c1)

    def leave(i, step):
        a, b = LAST[i], LAST[i + 1]
        if step == 0:
            quant(v("xq", a, b), v("xqs", a, b), v("xt", 4 * a, 4 * b))
            mm(v("b%d" % i, 0, b - a), v("vq"), v("vqs"), v("xq", a, b), v("xqs", a, b))
            dma("y", "doc", n, ("oc", 0, 128, 4 * a, 4 * b, T.oc[:, 4 * a:4 * b]), cd("xq", a, b))
        else:
            (act if i < n - 1 else copy)(v("yy", a, b), v("b%d" % i, 0, b - a))
            dma("y", "dy", n, ("y", 0, 128, a, b, T.y[:, a:b]), v("yy", a, b))

    n = len(LAST) - 1
    for i in range(n):
        back(0, LAST[i], LAST[i + 1])
        if i:
            leave(i - 1, 0)
        back(1, LAST[i], LAST[i + 1])
        if i > 1:
            leave(i - 2, 1)
    leave(n - 1, 0)
    leave(n - 2, 1)
    leave(n - 1, 1)
    for k in range(4):
        dma("s", "dos", 4, ("osc", 4 * k, 4 * k + 4, 0, 512, T.osc[4 * k:4 * k + 4, :]), v("xqs", 0, 512, 1, 32 * k, 32 * k + 4))
    for k in semof:
        need("g", (semof[k], count[k]))
    for s in total:
        need("g", (s, total[s]))
